import numpy as np
import ml_dtypes


def mxq(x, axis, fmt="e4m3"):
    dtype, down = {"e4m3": (ml_dtypes.float8_e4m3fn, 7), "e5m2": (ml_dtypes.float8_e5m2, 14)}[fmt]
    v = np.moveaxis(np.asarray(x, np.float32).astype(ml_dtypes.bfloat16).astype(np.float64), axis, -1)
    blocks = v.reshape(v.shape[:-1] + (-1, 32))
    amax = np.abs(blocks).max(-1, keepdims=True)
    byte = np.maximum(np.where(amax > 0, np.frexp(amax)[1] - 1 + 127, 0) - down, 1)
    scale = np.exp2(byte - 127.0)
    codes = (blocks / scale).astype(np.float32).astype(dtype).astype(np.float64)
    return np.moveaxis((codes * scale).reshape(v.shape), -1, axis)


WIDE = False


def mx_kscale(k):
    if not WIDE:
        return np.ones(k)
    levels = np.array([10, -10, 5, -5, 0])
    if k % 512:
        return np.exp2(np.random.permutation(np.resize(levels, k // 32))).repeat(32)
    a = np.empty((k // 512, 16))
    for p in range(k // 512):
        a[p, :8] = np.random.permutation(np.resize(levels, 8))
        for g in range(8):
            far = levels[np.abs(levels - a[p, g]) >= 10]
            a[p, g + 8] = far[np.random.randint(len(far))]
    return np.exp2(a.ravel()).repeat(32)


def f64(x):
    return np.asarray(x).astype(np.float64)


def striped(idx):
    return np.tile(idx.reshape(-1, 16).T, (8, 1)).astype(np.uint16)


def unstriped(offs):
    return offs[:16].T.reshape(-1).astype(np.int64)


E2M1 = np.array([0.0, 0.5, 1.0, 1.5, 2.0, 3.0, 4.0, 6.0, -0.0, -0.5, -1.0, -1.5, -2.0, -3.0, -4.0, -6.0])


def pack_weight(w, fmt):
    k, n = w.shape
    w = f64(np.asarray(w, np.float32).astype(ml_dtypes.bfloat16)).reshape(k // 32, 32, n)
    amax = np.abs(w).max(1)
    if fmt == "e4m3":
        byte = np.frexp(amax)[1] - 1 + 127 - 7
    else:
        mant, ex = np.frexp(amax / 6.0)
        byte = np.where(mant > 0.5, ex, ex - 1) + 127
    byte = np.clip(np.where(amax > 0, byte, 1), 1, 254)
    scaled = (w * np.exp2(127.0 - byte)[:, None, :]).reshape(k, n).astype(np.float32)
    by_word = np.ascontiguousarray(scaled.reshape(k // 512, 128, 4, n).transpose(0, 1, 3, 2))
    if fmt == "e4m3":
        words = by_word.astype(ml_dtypes.float8_e4m3fn).view(np.uint8)
    else:
        c = by_word.astype(ml_dtypes.float4_e2m1fn).view(np.uint8) & 0xF
        words = (c[..., 0::2] | (c[..., 1::2] << 4)).reshape(k // 512, 128, 2 * n)
    return np.ascontiguousarray(words), np.ascontiguousarray(byte.astype(np.uint8).reshape(k // 512, 16, n))


def unpack_weight(words, scales, fmt):
    g, _, n = scales.shape
    words = np.ascontiguousarray(words).reshape(g, 128, n, -1)
    if fmt == "e4m3":
        vals = words.view(ml_dtypes.float8_e4m3fn).astype(np.float64)
    else:
        nib = np.empty((g, 128, n, 4), np.uint8)
        nib[..., 0::2] = words & 0xF
        nib[..., 1::2] = words >> 4
        vals = E2M1[nib]
    vals = vals * np.repeat(np.exp2(scales.astype(np.float64) - 127.0), 8, axis=1)[..., None]
    return vals.transpose(0, 1, 3, 2).reshape(g * 512, n)


def gelu(v):
    return 0.5 * v * (1.0 + np.tanh(np.sqrt(2.0 / np.pi) * (v + 0.044715 * v**3)))


K, H, N, T, S, T2, P = 1024, 1024, 1024, 2048, 1024, 2048, 512

def setup_inputs():
    n = np.random.standard_normal
    s = mx_kscale(K)[:, None]
    u = mx_kscale(H)[:, None]
    tab_words, tab_scales = pack_weight(n((K, T)) * s, "e4m3")
    w4_words, w4_scales = pack_weight(n((K, H)) / np.sqrt(K) / s * u.T, "e2m1")
    rings = np.random.permutation(T2)
    return {
        "tab_words": tab_words, "tab_scales": tab_scales,
        "w4_words": w4_words, "w4_scales": w4_scales,
        "w": (0.7 * n((H, N)) / np.sqrt(H) / u).astype(np.float32),
        "wgs": np.exp(0.3 * n((128, S))).astype(np.float32),
        "ideal": (0.7 * n((H, P)) * u).astype(np.float32),
        "target": (0.5 * n((N, P))).astype(np.float32),
        "offs": striped(np.random.permutation(T)[:S]),
        "offs2": striped(np.random.permutation(T2)[:S]),
        "offs3": striped(rings[:P]),
        "offs4": striped(rings[P:2 * P]),
    }

def reference(tab_words, tab_scales, w4_words, w4_scales, w, wgs, ideal, target, offs, offs2, offs3, offs4):
    v = unpack_weight(tab_words, tab_scales, "e4m3")[:, unstriped(offs)]
    w4 = unpack_weight(w4_words, w4_scales, "e2m1")
    h = w4.T @ v
    page = np.zeros((H, T2))
    page[:, unstriped(offs2)] = np.tile(f64(wgs), (H // 128, 1)) * h
    x1 = page[:, unstriped(offs3)]
    x2 = page[:, unstriped(offs4)]
    z = x1 + x2 - f64(ideal)
    y = mxq(f64(w), 0, "e4m3").T @ mxq(z, 0, "e4m3")
    return np.tanh(y) - f64(target)

@@ -1,0 +1,257 @@
+from contextlib import ExitStack
+
+import concourse.mybir as mybir
+from concourse.masks import make_identity
+
+K, H, N, T, S, T2, M = 1024, 1024, 1024, 2048, 1024, 2048, 512
+FLOPS = 2 * K * H * S + 2 * H * N * M
+
+F32 = mybir.dt.float32
+BF16 = mybir.dt.bfloat16
+I32 = mybir.dt.int32
+U32 = mybir.dt.uint32
+U16 = mybir.dt.uint16
+U8 = mybir.dt.uint8
+FP8X4 = mybir.dt.float8_e4m3fn_x4
+FP4X4 = mybir.dt.float4_e2m1fn_x4
+ALU = mybir.AluOpType
+ACT = mybir.ActivationFunctionType
+
+P = 128
+BANK = 512
+HALF = M // 2
+ROW_TILES = H // P
+ALIGN = 64
+
+
+def tile_list_zeolite_ring_check_kernel(
+    tc, tab_words, tab_scales, w4_words, w4_scales, w, wgs, ideal, target, offs, offs2, offs3, offs4, out
+):
+    nc = tc.nc
+    with ExitStack() as ctx:
+        lists = ctx.enter_context(tc.tile_pool(name="lists", bufs=1))
+        sb = ctx.enter_context(tc.tile_pool(name="sb", bufs=1))
+        psum = ctx.enter_context(tc.psum_pool(name="psum", bufs=1))
+
+        def sbuf(name, shape, dtype, tag=None, bufs=1):
+            return sb.tile(shape, dtype, name=name, tag=tag or name, bufs=bufs, align_bytes=ALIGN)
+
+        def bank(name, number):
+            return psum.tile([P, BANK], F32, name=name, tag="bank%d" % number)
+
+        idx = lists.tile([P, S // 16], U16, name="idx")
+        idx2 = lists.tile([P, S // 16], U16, name="idx2")
+        idx3 = lists.tile([P, M // 16], U16, name="idx3")
+        idx4 = lists.tile([P, M // 16], U16, name="idx4")
+        tab_s = sbuf("tab_s", [P, T], U8, tag="slot_wgs")
+        nc.sync.dma_start(idx[:], offs)
+        nc.sync.dma_start(tab_s[96:128, :].bitcast(I32), tab_scales.rearrange("a q n -> q a n").bitcast(I32))
+        nc.sync.dma_start(idx2[:], offs2)
+        nc.sync.dma_start(idx3[:], offs3)
+        nc.sync.dma_start(idx4[:], offs4)
+        tab_w = [sbuf("tab_w%d" % a, [P, T], I32, tag=("slot_w0", "slot_page1")[a]) for a in range(2)]
+        for a in range(2):
+            nc.sync.dma_start(tab_w[a][:], tab_words[a].rearrange("p n t -> p (n t)").bitcast(I32))
+        w4_w = sbuf("w4_w", [P, 2, 2 * H], U8)
+        nc.sync.dma_start(w4_w[:].bitcast(I32), w4_words.rearrange("a p n -> p a n").bitcast(I32))
+
+        w4_s = sbuf("w4_s", [P, 2, H], U8)
+        v_s = sbuf("v_s", [P, 2, S], U8)
+        nc.vector.memset(w4_s[:].bitcast(I32), 0)
+        nc.vector.memset(tab_s[0:96, :].bitcast(I32), 0)
+        nc.vector.memset(v_s[:].bitcast(I32), 0)
+        for q in range(4):
+            nc.scalar.dma_start(
+                w4_s[32 * q : 32 * q + 4, :, :].bitcast(I32),
+                w4_scales[:, 4 * q : 4 * q + 4, :].rearrange("a r n -> r a n").bitcast(I32),
+            )
+        pages = [sbuf("page0", [P, T2], F32)]
+        nc.vector.memset(pages[0][:], 0.0)
+        ident = sbuf("ident", [P, P], F32)
+        make_identity(nc, ident[:])
+
+        picked_s = sbuf("picked_s", [P, S], U8, tag="slot_w1")
+        nc.vector.tensor_copy(picked_s[:], tab_s[:].indirect(idx[:]))
+        for q in range(4):
+            nc.scalar.dma_start(
+                v_s[32 * q : 32 * q + 4, :, :].bitcast(I32),
+                picked_s[96 + 8 * q : 96 + 8 * q + 8, :].bitcast(I32),
+            )
+        wgs_sb = sbuf("wgs_sb", [P, S], F32, tag="slot_wgs")
+        nc.sync.dma_start(wgs_sb[:], wgs)
+
+        v_w = [sbuf("v_w%d" % a, [P, S], U32, tag=("slot_ideal", "slot_target")[a]) for a in range(2)]
+        nc.vector.tensor_copy(v_w[0][:], tab_w[0][:].bitcast(U32).indirect(idx[:]))
+        for hh in range(2):
+            nc.vector.tensor_copy(
+                v_w[1][:, BANK * hh : BANK * (hh + 1)],
+                tab_w[1][:].bitcast(U32).indirect(idx[:, 32 * hh : 32 * (hh + 1)]),
+            )
+        pages.append(sbuf("page1", [P, T2], F32, tag="slot_page1"))
+        nc.gpsimd.memset(pages[1][:], 0.0)
+
+        h_first = [sbuf("h0_%d" % hh, [P, BANK], F32, tag="slot_page%d" % (2 + hh)) for hh in range(2)]
+        h_sb = [None] + [sbuf("h%d" % c, [P, S], F32) for c in range(1, ROW_TILES)]
+        for c in range(ROW_TILES):
+            for hh in range(2):
+                cols = slice(BANK * hh, BANK * (hh + 1))
+                acc = bank("h_acc", (2 * c + hh) % 4)
+                for a in range(2):
+                    nc.tensor.matmul_mx(
+                        out=acc[:],
+                        lhsT=w4_w[:, a, 2 * P * c : 2 * P * (c + 1)].bitcast(FP4X4),
+                        lhsT_scale=w4_s[:, a, P * c : P * (c + 1)],
+                        rhs=v_w[a][:, cols].bitcast(FP8X4),
+                        rhs_scale=v_s[:, a, cols],
+                        start=(a == 0),
+                        stop=(a == 1),
+                    )
+                nc.scalar.copy(h_first[hh][:] if c == 0 else h_sb[c][:, cols], acc[:])
+
+        for hh in range(2):
+            nc.vector.tensor_tensor(
+                pages[0][:].indirect(idx2[:, 32 * hh : 32 * (hh + 1)]),
+                h_first[hh][:],
+                wgs_sb[:, BANK * hh : BANK * (hh + 1)],
+                ALU.mult,
+            )
+            pages.append(sbuf("page%d" % (2 + hh), [P, T2], F32, tag="slot_page%d" % (2 + hh)))
+            nc.gpsimd.memset(pages[2 + hh][:], 0.0)
+
+        w_codes = sbuf("w_codes", [P, 2, N], U32)
+        w_scales = sbuf("w_scales", [P, 2, N], U8)
+        for b in range(2):
+            for nh in range(2):
+                cols = slice(BANK * nh, BANK * (nh + 1))
+                raw = sbuf("w_raw", [P, 4, BANK], F32, tag="slot_w%d" % nh)
+                nc.sync.dma_start(raw[:], w[512 * b : 512 * (b + 1), cols].rearrange("(p t) n -> p t n", t=4))
+                w_bf = sbuf("w_bf", [P, BANK, 4], BF16, bufs=2)
+                nc.scalar.copy(
+                    w_bf[:].rearrange("p (c i) t -> p c t i", i=4),
+                    raw[:].rearrange("p t (c i) -> p c t i", i=4),
+                )
+                nc.vector.quantize_mx(
+                    out=w_codes[:, b, cols].bitcast(FP8X4),
+                    scales=w_scales[:, b, cols],
+                    in_=w_bf[:].rearrange("p n t -> p (n t)"),
+                )
+
+        ideal_sb = sbuf("ideal_sb", [P, ROW_TILES, M], F32, tag="slot_ideal")
+        nc.sync.dma_start(ideal_sb[:], ideal.rearrange("(c p) m -> p c m", p=P))
+        minus_ideal = sbuf("minus_ideal", [P, ROW_TILES, M], F32)
+        for c in range(ROW_TILES):
+            nc.scalar.activation(minus_ideal[:, c, :], ideal_sb[:, c, :], ACT.Copy, scale=-1.0)
+        target_sb = sbuf("target_sb", [P, ROW_TILES, M], F32, tag="slot_target")
+        nc.sync.dma_start(target_sb[:], target.rearrange("(c p) m -> p c m", p=P))
+
+        def scatter(c):
+            nc.vector.tensor_tensor(pages[c % 4][:].indirect(idx2[:]), h_sb[c][:], wgs_sb[:], ALU.mult)
+
+        def fetch(c, m0, width, x1, x2, z_rows):
+            cols = slice(m0 // 16, (m0 + width) // 16)
+            nc.vector.tensor_copy(x1, pages[c % 4][:].indirect(idx3[:, cols]))
+            nc.vector.tensor_copy(x2, pages[c % 4][:].indirect(idx4[:, cols]))
+            acc = bank("z_acc", 4 + c % 2)
+            blocks = width // P
+            terms = (minus_ideal[:, c, m0 : m0 + width], x1, x2)
+            for k, term in enumerate(terms):
+                for j in range(blocks):
+                    nc.tensor.matmul(
+                        acc[:, P * j : P * (j + 1)],
+                        term[:, P * j : P * (j + 1)],
+                        ident[:],
+                        start=(k == 0 and j == 0),
+                        stop=(k == 2 and j == blocks - 1),
+                        is_transpose=True,
+                    )
+            nc.scalar.copy(
+                z_rows[:, :, :, 32 * (c % 4) : 32 * (c % 4 + 1), :],
+                acc[:, 0:width].rearrange("m (j p u e) -> m j u p e", j=blocks, u=2, e=2),
+            )
+
+        def turn_and_quantise(z_rows, width, grouped, name):
+            blocks = width // P
+            words = z_rows[:].rearrange("m j u p e -> m j u (p e)").bitcast(F32)
+            for j in range(blocks):
+                turned = bank("turned", 6 + j % 2)
+                for u in range(2):
+                    nc.tensor.transpose(turned[:, P * u : P * (u + 1)], words[:, j, u, :], ident[:])
+                nc.scalar.copy(
+                    grouped[:, P * j : P * (j + 1), :].bitcast(F32),
+                    turned[:, 0 : 2 * P].rearrange("p (u m) -> p m u", u=2),
+                )
+            codes = sbuf(name + "_codes", [P, width], U32)
+            scales = sbuf(name + "_scales", [P, width], U8)
+            nc.vector.quantize_mx(
+                out=codes[:].bitcast(FP8X4), scales=scales[:], in_=grouped[:].rearrange("p m t -> p (m t)")
+            )
+            return codes, scales
+
+        z_rows0 = sbuf("z_rows0", [P, M // P, 2, P, 2], BF16)
+        for c in range(4):
+            scatter(c + 1)
+            x1 = sbuf("x1", [P, M], F32, bufs=3)
+            x2 = sbuf("x2", [P, M], F32, bufs=3)
+            fetch(c, 0, M, x1[:], x2[:], z_rows0)
+        grouped0 = sbuf("grouped0", [P, M, 4], BF16)
+        z0_codes, z0_scales = turn_and_quantise(z_rows0, M, grouped0, "z0")
+        for c in range(5, ROW_TILES):
+            scatter(c)
+
+        def product(half, z1_codes, z1_scales):
+            banks = []
+            cols = slice(HALF * half, HALF * (half + 1))
+            for j in range(4):
+                acc = bank("y_acc", j)
+                banks.append(acc)
+                for i in range(2):
+                    n_cols = slice(P * (2 * j + i), P * (2 * j + i + 1))
+                    nc.tensor.matmul_mx(
+                        out=acc[:, HALF * i : HALF * (i + 1)],
+                        lhsT=w_codes[:, 0, n_cols].bitcast(FP8X4),
+                        lhsT_scale=w_scales[:, 0, n_cols],
+                        rhs=z0_codes[:, cols].bitcast(FP8X4),
+                        rhs_scale=z0_scales[:, cols],
+                        start=(i == 0),
+                        stop=False,
+                    )
+                for i in range(2):
+                    n_cols = slice(P * (2 * j + i), P * (2 * j + i + 1))
+                    nc.tensor.matmul_mx(
+                        out=acc[:, HALF * i : HALF * (i + 1)],
+                        lhsT=w_codes[:, 1, n_cols].bitcast(FP8X4),
+                        lhsT_scale=w_scales[:, 1, n_cols],
+                        rhs=z1_codes[:].bitcast(FP8X4),
+                        rhs_scale=z1_scales[:],
+                        start=False,
+                        stop=(i == 1),
+                    )
+            return banks
+
+        def finish(half, banks):
+            cols = slice(HALF * half, HALF * (half + 1))
+            for j in range(4):
+                bounded = sbuf("bounded", [P, 2, HALF], F32, bufs=4)
+                nc.scalar.activation(bounded[:].rearrange("p i m -> p (i m)"), banks[j][:], ACT.Tanh)
+                result = sbuf("result", [P, 2, HALF], F32, bufs=4)
+                nc.vector.tensor_tensor(result[:], bounded[:], target_sb[:, 2 * j : 2 * j + 2, cols], ALU.subtract)
+                nc.sync.dma_start(out.rearrange("(c p) m -> p c m", p=P)[:, 2 * j : 2 * j + 2, cols], result[:])
+
+        z_rows_a = sbuf("z_rows_a", [P, HALF // P, 2, P, 2], BF16)
+        x_a = sbuf("x_a", [P, 8, HALF], F32)
+        for c in range(4, ROW_TILES):
+            fetch(c, 0, HALF, x_a[:, 2 * (c - 4), :], x_a[:, 2 * (c - 4) + 1, :], z_rows_a)
+        grouped_a = sbuf("grouped_a", [P, HALF, 4], BF16, tag="slot_late")
+        za_codes, za_scales = turn_and_quantise(z_rows_a, HALF, grouped_a, "za")
+        banks_a = product(0, za_codes, za_scales)
+
+        z_rows_b = sbuf("z_rows_b", [P, HALF // P, 2, P, 2], BF16)
+        x_b = sbuf("x_b", [P, 4, HALF], F32, tag="h7")
+        x_c = sbuf("x_c", [P, 4, HALF], F32, tag="slot_late")
+        for c in range(4, ROW_TILES):
+            x = x_b if c < 6 else x_c
+            fetch(c, HALF, HALF, x[:, 2 * (c % 2), :], x[:, 2 * (c % 2) + 1, :], z_rows_b)
+        grouped_b = sbuf("grouped_b", [P, HALF, 4], BF16)
+        zb_codes, zb_scales = turn_and_quantise(z_rows_b, HALF, grouped_b, "zb")
+        finish(0, banks_a)
+        finish(1, product(1, zb_codes, zb_scales))

@@ -31,10 +31,14 @@ def tile_list_zeolite_ring_check_kernel(
     with ExitStack() as ctx:
         lists = ctx.enter_context(tc.tile_pool(name="lists", bufs=1))
         sb = ctx.enter_context(tc.tile_pool(name="sb", bufs=1))
+        staged = ctx.enter_context(tc.tile_pool(name="staged", bufs=1))
         psum = ctx.enter_context(tc.psum_pool(name="psum", bufs=1))
 
         def sbuf(name, shape, dtype, tag=None, bufs=1):
             return sb.tile(shape, dtype, name=name, tag=tag or name, bufs=bufs, align_bytes=ALIGN)
+
+        def placed(name, shape, dtype, kib):
+            return staged.tile(shape, dtype, name=name, tag=name, align_bytes=ALIGN, offset=1024 * (kib - 32))
 
         def bank(name, number):
             return psum.tile([P, BANK], F32, name=name, tag="bank%d" % number)
@@ -43,59 +47,57 @@ def tile_list_zeolite_ring_check_kernel(
         idx2 = lists.tile([P, S // 16], U16, name="idx2")
         idx3 = lists.tile([P, M // 16], U16, name="idx3")
         idx4 = lists.tile([P, M // 16], U16, name="idx4")
-        tab_s = sbuf("tab_s", [P, T], U8, tag="slot_wgs")
+        tab_s = placed("tab_s", [P, T], U8, 35)
         nc.sync.dma_start(idx[:], offs)
         nc.sync.dma_start(tab_s[96:128, :].bitcast(I32), tab_scales.rearrange("a q n -> q a n").bitcast(I32))
         nc.sync.dma_start(idx2[:], offs2)
         nc.sync.dma_start(idx3[:], offs3)
         nc.sync.dma_start(idx4[:], offs4)
-        tab_w = [sbuf("tab_w%d" % a, [P, T], I32, tag=("slot_w0", "slot_page1")[a]) for a in range(2)]
+        tab_w = [sbuf("tab_w0", [P, T], I32), placed("tab_w1", [P, T], I32, 76 + 4)]
         for a in range(2):
             nc.sync.dma_start(tab_w[a][:], tab_words[a].rearrange("p n t -> p (n t)").bitcast(I32))
-        w4_w = sbuf("w4_w", [P, 2, 2 * H], U8)
-        nc.sync.dma_start(w4_w[:].bitcast(I32), w4_words.rearrange("a p n -> p a n").bitcast(I32))
 
-        w4_s = sbuf("w4_s", [P, 2, H], U8)
-        v_s = sbuf("v_s", [P, 2, S], U8)
-        nc.vector.memset(w4_s[:].bitcast(I32), 0)
+        w4_s = placed("w4_s", [P, 2, H], U8, 67)
+        v_s = placed("v_s", [P, 2, S], U8, 59)
+        nc.gpsimd.memset(w4_s[:].bitcast(I32), 0)
         nc.vector.memset(tab_s[0:96, :].bitcast(I32), 0)
         nc.vector.memset(v_s[:].bitcast(I32), 0)
         for q in range(4):
-            nc.scalar.dma_start(
+            (nc.gpsimd, nc.scalar)[q % 2].dma_start(
                 w4_s[32 * q : 32 * q + 4, :, :].bitcast(I32),
                 w4_scales[:, 4 * q : 4 * q + 4, :].rearrange("a r n -> r a n").bitcast(I32),
             )
-        pages = [sbuf("page0", [P, T2], F32)]
-        nc.vector.memset(pages[0][:], 0.0)
-        ident = sbuf("ident", [P, P], F32)
-        make_identity(nc, ident[:])
 
-        picked_s = sbuf("picked_s", [P, S], U8, tag="slot_w1")
+        picked_s = sbuf("picked_s", [P, S], U8)
         nc.vector.tensor_copy(picked_s[:], tab_s[:].indirect(idx[:]))
         for q in range(4):
             nc.scalar.dma_start(
                 v_s[32 * q : 32 * q + 4, :, :].bitcast(I32),
                 picked_s[96 + 8 * q : 96 + 8 * q + 8, :].bitcast(I32),
             )
-        wgs_sb = sbuf("wgs_sb", [P, S], F32, tag="slot_wgs")
-        nc.sync.dma_start(wgs_sb[:], wgs)
+        ident = sbuf("ident", [P, P], F32, tag="picked_s")
+        make_identity(nc, ident[:])
+        w4_w = placed("w4_w", [P, 2, 2 * H], U8, 32)
+        nc.sync.dma_start(w4_w[:].bitcast(I32), w4_words.rearrange("a p n -> p a n").bitcast(I32))
 
-        v_w = [sbuf("v_w%d" % a, [P, S], U32, tag=("slot_ideal", "slot_target")[a]) for a in range(2)]
+        v_w = [sbuf("v_w%d" % a, [P, S], U32, tag=("slot_minus", "slot_target")[a]) for a in range(2)]
         nc.vector.tensor_copy(v_w[0][:], tab_w[0][:].bitcast(U32).indirect(idx[:]))
+        wgs_sb = sbuf("wgs_sb", [P, S], F32, tag="tab_w0")
+        nc.sync.dma_start(wgs_sb[:], wgs)
         for hh in range(2):
             nc.vector.tensor_copy(
                 v_w[1][:, BANK * hh : BANK * (hh + 1)],
                 tab_w[1][:].bitcast(U32).indirect(idx[:, 32 * hh : 32 * (hh + 1)]),
             )
-        pages.append(sbuf("page1", [P, T2], F32, tag="slot_page1"))
-        nc.gpsimd.memset(pages[1][:], 0.0)
+        pages = [placed("page0", [P, T2], F32, 76)]
+        nc.vector.memset(pages[0][:], 0.0)
 
-        h_first = [sbuf("h0_%d" % hh, [P, BANK], F32, tag="slot_page%d" % (2 + hh)) for hh in range(2)]
+        h_first = [sbuf("h0_0", [P, BANK], F32, tag="slot_page1"), placed("h0_1", [P, BANK], F32, 47)]
         h_sb = [None] + [sbuf("h%d" % c, [P, S], F32) for c in range(1, ROW_TILES)]
         for c in range(ROW_TILES):
             for hh in range(2):
                 cols = slice(BANK * hh, BANK * (hh + 1))
-                acc = bank("h_acc", (2 * c + hh) % 4)
+                acc = bank("h_acc", hh)
                 for a in range(2):
                     nc.tensor.matmul_mx(
                         out=acc[:],
@@ -115,20 +117,24 @@ def tile_list_zeolite_ring_check_kernel(
                 wgs_sb[:, BANK * hh : BANK * (hh + 1)],
                 ALU.mult,
             )
-            pages.append(sbuf("page%d" % (2 + hh), [P, T2], F32, tag="slot_page%d" % (2 + hh)))
-            nc.gpsimd.memset(pages[2 + hh][:], 0.0)
+        pages.append(sbuf("page1", [P, T2], F32, tag="slot_page1"))
+        nc.gpsimd.memset(pages[1][:], 0.0)
+        for i in range(2):
+            pages.append(placed("page%d" % (2 + i), [P, T2], F32, 40 + 8 * i))
+            nc.gpsimd.memset(pages[2 + i][:], 0.0)
 
         w_codes = sbuf("w_codes", [P, 2, N], U32)
         w_scales = sbuf("w_scales", [P, 2, N], U8)
+        w_raw = placed("w_raw", [P, 2, 4, N], F32, 84)
         for b in range(2):
+            raw = w_raw[:, b]
+            nc.sync.dma_start(raw, w[512 * b : 512 * (b + 1), :].rearrange("(p t) n -> p t n", t=4))
             for nh in range(2):
                 cols = slice(BANK * nh, BANK * (nh + 1))
-                raw = sbuf("w_raw", [P, 4, BANK], F32, tag="slot_w%d" % nh)
-                nc.sync.dma_start(raw[:], w[512 * b : 512 * (b + 1), cols].rearrange("(p t) n -> p t n", t=4))
-                w_bf = sbuf("w_bf", [P, BANK, 4], BF16, bufs=2)
+                w_bf = placed("w_bf%d%d" % (b, nh), [P, BANK, 4], BF16, 56 + 8 * b + 4 * nh)
                 nc.scalar.copy(
                     w_bf[:].rearrange("p (c i) t -> p c t i", i=4),
-                    raw[:].rearrange("p t (c i) -> p c t i", i=4),
+                    raw[:, :, cols].rearrange("p t (c i) -> p c t i", i=4),
                 )
                 nc.vector.quantize_mx(
                     out=w_codes[:, b, cols].bitcast(FP8X4),
@@ -136,18 +142,19 @@ def tile_list_zeolite_ring_check_kernel(
                     in_=w_bf[:].rearrange("p n t -> p (n t)"),
                 )
 
-        ideal_sb = sbuf("ideal_sb", [P, ROW_TILES, M], F32, tag="slot_ideal")
+        ideal_sb = sbuf("ideal_sb", [P, ROW_TILES, M], F32, tag="h1")
         nc.sync.dma_start(ideal_sb[:], ideal.rearrange("(c p) m -> p c m", p=P))
-        minus_ideal = sbuf("minus_ideal", [P, ROW_TILES, M], F32)
+        minus_ideal = sbuf("minus_ideal", [P, ROW_TILES, M], F32, tag="slot_minus")
         for c in range(ROW_TILES):
             nc.scalar.activation(minus_ideal[:, c, :], ideal_sb[:, c, :], ACT.Copy, scale=-1.0)
         target_sb = sbuf("target_sb", [P, ROW_TILES, M], F32, tag="slot_target")
         nc.sync.dma_start(target_sb[:], target.rearrange("(c p) m -> p c m", p=P))
 
         def scatter(c):
-            nc.vector.tensor_tensor(pages[c % 4][:].indirect(idx2[:]), h_sb[c][:], wgs_sb[:], ALU.mult)
+            nc.vector.tensor_tensor(h_sb[c][:], h_sb[c][:], wgs_sb[:], ALU.mult)
+            nc.vector.tensor_copy(pages[c % 4][:].indirect(idx2[:]), h_sb[c][:])
 
-        def fetch(c, m0, width, x1, x2, z_rows):
+        def fetch(c, m0, width, x1, x2, z_rows, copy):
             cols = slice(m0 // 16, (m0 + width) // 16)
             nc.vector.tensor_copy(x1, pages[c % 4][:].indirect(idx3[:, cols]))
             nc.vector.tensor_copy(x2, pages[c % 4][:].indirect(idx4[:, cols]))
@@ -164,19 +171,19 @@ def tile_list_zeolite_ring_check_kernel(
                         stop=(k == 2 and j == blocks - 1),
                         is_transpose=True,
                     )
-            nc.scalar.copy(
+            copy(
                 z_rows[:, :, :, 32 * (c % 4) : 32 * (c % 4 + 1), :],
                 acc[:, 0:width].rearrange("m (j p u e) -> m j u p e", j=blocks, u=2, e=2),
             )
 
-        def turn_and_quantise(z_rows, width, grouped, name):
+        def turn_and_quantise(z_rows, width, grouped, name, copy):
             blocks = width // P
             words = z_rows[:].rearrange("m j u p e -> m j u (p e)").bitcast(F32)
             for j in range(blocks):
                 turned = bank("turned", 6 + j % 2)
                 for u in range(2):
                     nc.tensor.transpose(turned[:, P * u : P * (u + 1)], words[:, j, u, :], ident[:])
-                nc.scalar.copy(
+                copy(
                     grouped[:, P * j : P * (j + 1), :].bitcast(F32),
                     turned[:, 0 : 2 * P].rearrange("p (u m) -> p m u", u=2),
                 )
@@ -190,11 +197,11 @@ def tile_list_zeolite_ring_check_kernel(
         z_rows0 = sbuf("z_rows0", [P, M // P, 2, P, 2], BF16)
         for c in range(4):
             scatter(c + 1)
-            x1 = sbuf("x1", [P, M], F32, bufs=3)
-            x2 = sbuf("x2", [P, M], F32, bufs=3)
-            fetch(c, 0, M, x1[:], x2[:], z_rows0)
-        grouped0 = sbuf("grouped0", [P, M, 4], BF16)
-        z0_codes, z0_scales = turn_and_quantise(z_rows0, M, grouped0, "z0")
+            x1 = sbuf("x1", [P, M], F32, bufs=4)
+            x2 = sbuf("x2", [P, M], F32, bufs=4)
+            fetch(c, 0, M, x1[:], x2[:], z_rows0, nc.scalar.copy)
+        grouped0 = placed("grouped0", [P, M, 4], BF16, 72)
+        z0_codes, z0_scales = turn_and_quantise(z_rows0, M, grouped0, "z0", nc.scalar.copy)
         for c in range(5, ROW_TILES):
             scatter(c)
 
@@ -238,20 +245,19 @@ def tile_list_zeolite_ring_check_kernel(
                 nc.sync.dma_start(out.rearrange("(c p) m -> p c m", p=P)[:, 2 * j : 2 * j + 2, cols], result[:])
 
         z_rows_a = sbuf("z_rows_a", [P, HALF // P, 2, P, 2], BF16)
-        x_a = sbuf("x_a", [P, 8, HALF], F32)
+        x_a = placed("x_a", [P, 12, HALF], F32, 64)
         for c in range(4, ROW_TILES):
-            fetch(c, 0, HALF, x_a[:, 2 * (c - 4), :], x_a[:, 2 * (c - 4) + 1, :], z_rows_a)
+            fetch(c, 0, HALF, x_a[:, 2 * (c - 4), :], x_a[:, 2 * (c - 4) + 1, :], z_rows_a, nc.scalar.copy)
         grouped_a = sbuf("grouped_a", [P, HALF, 4], BF16, tag="slot_late")
-        za_codes, za_scales = turn_and_quantise(z_rows_a, HALF, grouped_a, "za")
+        za_codes, za_scales = turn_and_quantise(z_rows_a, HALF, grouped_a, "za", nc.scalar.copy)
         banks_a = product(0, za_codes, za_scales)
 
         z_rows_b = sbuf("z_rows_b", [P, HALF // P, 2, P, 2], BF16)
-        x_b = sbuf("x_b", [P, 4, HALF], F32, tag="h7")
         x_c = sbuf("x_c", [P, 4, HALF], F32, tag="slot_late")
         for c in range(4, ROW_TILES):
-            x = x_b if c < 6 else x_c
-            fetch(c, HALF, HALF, x[:, 2 * (c % 2), :], x[:, 2 * (c % 2) + 1, :], z_rows_b)
+            x = x_a[:, 8:12, :] if c < 6 else x_c
+            fetch(c, HALF, HALF, x[:, 2 * (c % 2), :], x[:, 2 * (c % 2) + 1, :], z_rows_b, nc.scalar.copy)
         grouped_b = sbuf("grouped_b", [P, HALF, 4], BF16)
-        zb_codes, zb_scales = turn_and_quantise(z_rows_b, HALF, grouped_b, "zb")
+        zb_codes, zb_scales = turn_and_quantise(z_rows_b, HALF, grouped_b, "zb", nc.scalar.copy)
         finish(0, banks_a)
         finish(1, product(1, zb_codes, zb_scales))

@@ -19,9 +19,28 @@ ACT = mybir.ActivationFunctionType
 
 P = 128
 BANK = 512
+PASS = 512
 HALF = M // 2
 ROW_TILES = H // P
+PAGES = 4
+PER_COLUMN = 16
 ALIGN = 64
+
+Z_BANK = 4
+TURN_BANK = 6
+
+AT_W4_WORDS = 0
+AT_TAB_SCALES = 3
+AT_PAGE2 = 8
+AT_H0_SECOND = 15
+AT_W_RIGHT = 24
+AT_V_SCALES = 27
+AT_W_LEFT = 32
+AT_W4_SCALES = 35
+AT_Z0_GROUPED = 40
+AT_EARLY_READS = 32
+AT_PAGE0 = 44
+AT_W_RAW = 52
 
 
 def tile_list_zeolite_ring_check_kernel(
@@ -38,152 +57,158 @@ def tile_list_zeolite_ring_check_kernel(
             return sb.tile(shape, dtype, name=name, tag=tag or name, bufs=bufs, align_bytes=ALIGN)
 
         def placed(name, shape, dtype, kib):
-            return staged.tile(shape, dtype, name=name, tag=name, align_bytes=ALIGN, offset=1024 * (kib - 32))
+            return staged.tile(shape, dtype, name=name, tag=name, align_bytes=ALIGN, offset=1024 * kib)
 
         def bank(name, number):
             return psum.tile([P, BANK], F32, name=name, tag="bank%d" % number)
 
-        idx = lists.tile([P, S // 16], U16, name="idx")
-        idx2 = lists.tile([P, S // 16], U16, name="idx2")
-        idx3 = lists.tile([P, M // 16], U16, name="idx3")
-        idx4 = lists.tile([P, M // 16], U16, name="idx4")
-        tab_s = placed("tab_s", [P, T], U8, 35)
+        def entries(first, count):
+            return slice(first // PER_COLUMN, (first + count) // PER_COLUMN)
+
+        idx = lists.tile([P, S // PER_COLUMN], U16, name="idx")
+        idx2 = lists.tile([P, S // PER_COLUMN], U16, name="idx2")
+        idx3 = lists.tile([P, M // PER_COLUMN], U16, name="idx3")
+        idx4 = lists.tile([P, M // PER_COLUMN], U16, name="idx4")
+        tab_s = placed("tab_s", [P, T], U8, AT_TAB_SCALES)
         nc.sync.dma_start(idx[:], offs)
         nc.sync.dma_start(tab_s[96:128, :].bitcast(I32), tab_scales.rearrange("a q n -> q a n").bitcast(I32))
         nc.sync.dma_start(idx2[:], offs2)
         nc.sync.dma_start(idx3[:], offs3)
         nc.sync.dma_start(idx4[:], offs4)
-        tab_w = [sbuf("tab_w0", [P, T], I32), placed("tab_w1", [P, T], I32, 76 + 4)]
+        tab_w = [sbuf("tab_w0", [P, T], I32), placed("tab_w1", [P, T], I32, AT_W_RAW)]
         for a in range(2):
             nc.sync.dma_start(tab_w[a][:], tab_words[a].rearrange("p n t -> p (n t)").bitcast(I32))
 
-        w4_s = placed("w4_s", [P, 2, H], U8, 67)
-        v_s = placed("v_s", [P, 2, S], U8, 59)
+        w4_s = placed("w4_s", [P, 2, H], U8, AT_W4_SCALES)
+        v_s = placed("v_s", [P, 2, S], U8, AT_V_SCALES)
         nc.gpsimd.memset(w4_s[:].bitcast(I32), 0)
         nc.vector.memset(tab_s[0:96, :].bitcast(I32), 0)
         nc.vector.memset(v_s[:].bitcast(I32), 0)
-        for q in range(4):
-            (nc.gpsimd, nc.scalar)[q % 2].dma_start(
-                w4_s[32 * q : 32 * q + 4, :, :].bitcast(I32),
-                w4_scales[:, 4 * q : 4 * q + 4, :].rearrange("a r n -> r a n").bitcast(I32),
+        for g in range(4):
+            (nc.gpsimd, nc.scalar)[g % 2].dma_start(
+                w4_s[32 * g : 32 * g + 4, :, :].bitcast(I32),
+                w4_scales[:, 4 * g : 4 * g + 4, :].rearrange("a r n -> r a n").bitcast(I32),
             )
+        pages = [placed("page0", [P, T2], F32, AT_PAGE0)]
+        nc.vector.memset(pages[0][:], 0.0)
 
         picked_s = sbuf("picked_s", [P, S], U8)
         nc.vector.tensor_copy(picked_s[:], tab_s[:].indirect(idx[:]))
-        for q in range(4):
+        for g in range(4):
             nc.scalar.dma_start(
-                v_s[32 * q : 32 * q + 4, :, :].bitcast(I32),
-                picked_s[96 + 8 * q : 96 + 8 * q + 8, :].bitcast(I32),
+                v_s[32 * g : 32 * g + 4, :, :].bitcast(I32),
+                picked_s[96 + 8 * g : 96 + 8 * g + 8, :].bitcast(I32),
             )
         ident = sbuf("ident", [P, P], F32, tag="picked_s")
         make_identity(nc, ident[:])
-        w4_w = placed("w4_w", [P, 2, 2 * H], U8, 32)
+        w4_w = placed("w4_w", [P, 2, 2 * H], U8, AT_W4_WORDS)
         nc.sync.dma_start(w4_w[:].bitcast(I32), w4_words.rearrange("a p n -> p a n").bitcast(I32))
 
-        v_w = [sbuf("v_w%d" % a, [P, S], U32, tag=("slot_minus", "slot_target")[a]) for a in range(2)]
+        v_w = [sbuf("v_w%d" % a, [P, S], U32) for a in range(2)]
         nc.vector.tensor_copy(v_w[0][:], tab_w[0][:].bitcast(U32).indirect(idx[:]))
         wgs_sb = sbuf("wgs_sb", [P, S], F32, tag="tab_w0")
         nc.sync.dma_start(wgs_sb[:], wgs)
-        for hh in range(2):
+        for part in range(2):
             nc.vector.tensor_copy(
-                v_w[1][:, BANK * hh : BANK * (hh + 1)],
-                tab_w[1][:].bitcast(U32).indirect(idx[:, 32 * hh : 32 * (hh + 1)]),
+                v_w[1][:, BANK * part : BANK * (part + 1)],
+                tab_w[1][:].bitcast(U32).indirect(idx[:, entries(BANK * part, BANK)]),
             )
-        pages = [placed("page0", [P, T2], F32, 76)]
-        nc.vector.memset(pages[0][:], 0.0)
 
-        h_first = [sbuf("h0_0", [P, BANK], F32, tag="slot_page1"), placed("h0_1", [P, BANK], F32, 47)]
-        h_sb = [None] + [sbuf("h%d" % c, [P, S], F32) for c in range(1, ROW_TILES)]
+        h0_parts = [sbuf("h0_first", [P, BANK], F32), placed("h0_second", [P, BANK], F32, AT_H0_SECOND)]
+        h_tiles = {c: sbuf("h%d" % c, [P, S], F32) for c in range(1, ROW_TILES)}
         for c in range(ROW_TILES):
-            for hh in range(2):
-                cols = slice(BANK * hh, BANK * (hh + 1))
-                acc = bank("h_acc", hh)
+            for part in range(2):
+                j_cols = slice(BANK * part, BANK * (part + 1))
+                h_acc = bank("h_acc", part)
                 for a in range(2):
                     nc.tensor.matmul_mx(
-                        out=acc[:],
+                        out=h_acc[:],
                         lhsT=w4_w[:, a, 2 * P * c : 2 * P * (c + 1)].bitcast(FP4X4),
                         lhsT_scale=w4_s[:, a, P * c : P * (c + 1)],
-                        rhs=v_w[a][:, cols].bitcast(FP8X4),
-                        rhs_scale=v_s[:, a, cols],
+                        rhs=v_w[a][:, j_cols].bitcast(FP8X4),
+                        rhs_scale=v_s[:, a, j_cols],
                         start=(a == 0),
                         stop=(a == 1),
                     )
-                nc.scalar.copy(h_first[hh][:] if c == 0 else h_sb[c][:, cols], acc[:])
+                nc.scalar.copy(h0_parts[part][:] if c == 0 else h_tiles[c][:, j_cols], h_acc[:])
 
-        for hh in range(2):
+        for part in range(2):
             nc.vector.tensor_tensor(
-                pages[0][:].indirect(idx2[:, 32 * hh : 32 * (hh + 1)]),
-                h_first[hh][:],
-                wgs_sb[:, BANK * hh : BANK * (hh + 1)],
+                pages[0][:].indirect(idx2[:, entries(BANK * part, BANK)]),
+                h0_parts[part][:],
+                wgs_sb[:, BANK * part : BANK * (part + 1)],
                 ALU.mult,
             )
-        pages.append(sbuf("page1", [P, T2], F32, tag="slot_page1"))
+        pages.append(sbuf("page1", [P, T2], F32, tag="h0_first"))
         nc.gpsimd.memset(pages[1][:], 0.0)
         for i in range(2):
-            pages.append(placed("page%d" % (2 + i), [P, T2], F32, 40 + 8 * i))
+            pages.append(placed("page%d" % (2 + i), [P, T2], F32, AT_PAGE2 + 8 * i))
             nc.gpsimd.memset(pages[2 + i][:], 0.0)
 
-        w_codes = sbuf("w_codes", [P, 2, N], U32)
-        w_scales = sbuf("w_scales", [P, 2, N], U8)
-        w_raw = placed("w_raw", [P, 2, 4, N], F32, 84)
-        for b in range(2):
-            raw = w_raw[:, b]
-            nc.sync.dma_start(raw, w[512 * b : 512 * (b + 1), :].rearrange("(p t) n -> p t n", t=4))
-            for nh in range(2):
-                cols = slice(BANK * nh, BANK * (nh + 1))
-                w_bf = placed("w_bf%d%d" % (b, nh), [P, BANK, 4], BF16, 56 + 8 * b + 4 * nh)
-                nc.scalar.copy(
-                    w_bf[:].rearrange("p (c i) t -> p c t i", i=4),
-                    raw[:, :, cols].rearrange("p t (c i) -> p c t i", i=4),
-                )
+        w_codes = [sbuf("w_codes0", [P, 2, BANK], U32)]
+        w_scales = [sbuf("w_scales%d" % side, [P, 2, BANK], U8) for side in range(2)]
+        w_rounded = {}
+
+        def quantise_w(side):
+            for b in range(2):
                 nc.vector.quantize_mx(
-                    out=w_codes[:, b, cols].bitcast(FP8X4),
-                    scales=w_scales[:, b, cols],
-                    in_=w_bf[:].rearrange("p n t -> p (n t)"),
+                    out=w_codes[side][:, b, :].bitcast(FP8X4),
+                    scales=w_scales[side][:, b, :],
+                    in_=w_rounded[b, side][:].rearrange("p n t -> p (n t)"),
                 )
+
+        w_raw = placed("w_raw", [P, 2, 4, N], F32, AT_W_RAW)
+        for b in range(2):
+            nc.sync.dma_start(w_raw[:, b], w[PASS * b : PASS * (b + 1), :].rearrange("(p t) n -> p t n", t=4))
+            for side in range(2):
+                w_rounded[b, side] = placed(
+                    "w_rounded%d%d" % (b, side), [P, BANK, 4], BF16, (AT_W_LEFT, AT_W_RIGHT)[side] + 4 * b
+                )
+                nc.scalar.copy(
+                    w_rounded[b, side][:].rearrange("p (c i) t -> p c t i", i=4),
+                    w_raw[:, b][:, :, BANK * side : BANK * (side + 1)].rearrange("p t (c i) -> p c t i", i=4),
+                )
+        quantise_w(0)
 
         ideal_sb = sbuf("ideal_sb", [P, ROW_TILES, M], F32, tag="h1")
         nc.sync.dma_start(ideal_sb[:], ideal.rearrange("(c p) m -> p c m", p=P))
-        minus_ideal = sbuf("minus_ideal", [P, ROW_TILES, M], F32, tag="slot_minus")
+        minus_ideal = sbuf("minus_ideal", [P, ROW_TILES, M], F32, tag="v_w0")
         for c in range(ROW_TILES):
             nc.scalar.activation(minus_ideal[:, c, :], ideal_sb[:, c, :], ACT.Copy, scale=-1.0)
-        target_sb = sbuf("target_sb", [P, ROW_TILES, M], F32, tag="slot_target")
+        target_sb = sbuf("target_sb", [P, ROW_TILES, M], F32, tag="v_w1")
         nc.sync.dma_start(target_sb[:], target.rearrange("(c p) m -> p c m", p=P))
 
         def scatter(c):
-            nc.vector.tensor_tensor(h_sb[c][:], h_sb[c][:], wgs_sb[:], ALU.mult)
-            nc.vector.tensor_copy(pages[c % 4][:].indirect(idx2[:]), h_sb[c][:])
+            nc.vector.tensor_tensor(pages[c % PAGES][:].indirect(idx2[:]), h_tiles[c][:], wgs_sb[:], ALU.mult)
 
-        def fetch(c, m0, width, x1, x2, z_rows, copy):
-            cols = slice(m0 // 16, (m0 + width) // 16)
-            nc.vector.tensor_copy(x1, pages[c % 4][:].indirect(idx3[:, cols]))
-            nc.vector.tensor_copy(x2, pages[c % 4][:].indirect(idx4[:, cols]))
-            acc = bank("z_acc", 4 + c % 2)
+        def fetch(c, m0, width, site, facing, z_rows):
+            nc.vector.tensor_copy(site, pages[c % PAGES][:].indirect(idx3[:, entries(m0, width)]))
+            nc.vector.tensor_copy(facing, pages[c % PAGES][:].indirect(idx4[:, entries(m0, width)]))
+            z_acc = bank("z_acc", Z_BANK + c % 2)
             blocks = width // P
-            terms = (minus_ideal[:, c, m0 : m0 + width], x1, x2)
-            for k, term in enumerate(terms):
+            terms = (minus_ideal[:, c, m0 : m0 + width], site, facing)
+            for number, term in enumerate(terms):
                 for j in range(blocks):
                     nc.tensor.matmul(
-                        acc[:, P * j : P * (j + 1)],
+                        z_acc[:, P * j : P * (j + 1)],
                         term[:, P * j : P * (j + 1)],
                         ident[:],
-                        start=(k == 0 and j == 0),
-                        stop=(k == 2 and j == blocks - 1),
+                        start=(number == 0 and j == 0),
+                        stop=(number == len(terms) - 1 and j == blocks - 1),
                         is_transpose=True,
                     )
-            copy(
+            nc.scalar.copy(
                 z_rows[:, :, :, 32 * (c % 4) : 32 * (c % 4 + 1), :],
-                acc[:, 0:width].rearrange("m (j p u e) -> m j u p e", j=blocks, u=2, e=2),
+                z_acc[:, 0:width].rearrange("m (j p u e) -> m j u p e", j=blocks, u=2, e=2),
             )
 
-        def turn_and_quantise(z_rows, width, grouped, name, copy):
-            blocks = width // P
-            words = z_rows[:].rearrange("m j u p e -> m j u (p e)").bitcast(F32)
-            for j in range(blocks):
-                turned = bank("turned", 6 + j % 2)
+        def turn_and_quantise(z_rows, width, grouped, name):
+            pairs = z_rows[:].rearrange("m j u p e -> m j u (p e)").bitcast(F32)
+            for j in range(width // P):
+                turned = bank("turned", TURN_BANK + j % 2)
                 for u in range(2):
-                    nc.tensor.transpose(turned[:, P * u : P * (u + 1)], words[:, j, u, :], ident[:])
-                copy(
+                    nc.tensor.transpose(turned[:, P * u : P * (u + 1)], pairs[:, j, u, :], ident[:])
+                nc.scalar.copy(
                     grouped[:, P * j : P * (j + 1), :].bitcast(F32),
                     turned[:, 0 : 2 * P].rearrange("p (u m) -> p m u", u=2),
                 )
@@ -194,70 +219,63 @@ def tile_list_zeolite_ring_check_kernel(
             )
             return codes, scales
 
-        z_rows0 = sbuf("z_rows0", [P, M // P, 2, P, 2], BF16)
+        z0_rows = sbuf("z0_rows", [P, M // P, 2, P, 2], BF16)
         for c in range(4):
             scatter(c + 1)
-            x1 = sbuf("x1", [P, M], F32, bufs=4)
-            x2 = sbuf("x2", [P, M], F32, bufs=4)
-            fetch(c, 0, M, x1[:], x2[:], z_rows0, nc.scalar.copy)
-        grouped0 = placed("grouped0", [P, M, 4], BF16, 72)
-        z0_codes, z0_scales = turn_and_quantise(z_rows0, M, grouped0, "z0", nc.scalar.copy)
+            site = sbuf("site", [P, M], F32, bufs=4)
+            facing = sbuf("facing", [P, M], F32, bufs=4)
+            fetch(c, 0, M, site[:], facing[:], z0_rows)
+        z0_grouped = placed("z0_grouped", [P, M, 4], BF16, AT_Z0_GROUPED)
+        z0_codes, z0_scales = turn_and_quantise(z0_rows, M, z0_grouped, "z0")
         for c in range(5, ROW_TILES):
             scatter(c)
 
         def product(half, z1_codes, z1_scales):
             banks = []
-            cols = slice(HALF * half, HALF * (half + 1))
+            m_cols = slice(HALF * half, HALF * (half + 1))
+            moving = ((z0_codes[:, m_cols], z0_scales[:, m_cols]), (z1_codes[:], z1_scales[:]))
             for j in range(4):
-                acc = bank("y_acc", j)
-                banks.append(acc)
-                for i in range(2):
-                    n_cols = slice(P * (2 * j + i), P * (2 * j + i + 1))
-                    nc.tensor.matmul_mx(
-                        out=acc[:, HALF * i : HALF * (i + 1)],
-                        lhsT=w_codes[:, 0, n_cols].bitcast(FP8X4),
-                        lhsT_scale=w_scales[:, 0, n_cols],
-                        rhs=z0_codes[:, cols].bitcast(FP8X4),
-                        rhs_scale=z0_scales[:, cols],
-                        start=(i == 0),
-                        stop=False,
-                    )
-                for i in range(2):
-                    n_cols = slice(P * (2 * j + i), P * (2 * j + i + 1))
-                    nc.tensor.matmul_mx(
-                        out=acc[:, HALF * i : HALF * (i + 1)],
-                        lhsT=w_codes[:, 1, n_cols].bitcast(FP8X4),
-                        lhsT_scale=w_scales[:, 1, n_cols],
-                        rhs=z1_codes[:].bitcast(FP8X4),
-                        rhs_scale=z1_scales[:],
-                        start=False,
-                        stop=(i == 1),
-                    )
+                y_acc = bank("y_acc", j)
+                banks.append(y_acc)
+                for b in range(2):
+                    for i in range(2):
+                        n_cols = slice(P * (2 * (j % 2) + i), P * (2 * (j % 2) + i + 1))
+                        nc.tensor.matmul_mx(
+                            out=y_acc[:, HALF * i : HALF * (i + 1)],
+                            lhsT=w_codes[j // 2][:, b, n_cols].bitcast(FP8X4),
+                            lhsT_scale=w_scales[j // 2][:, b, n_cols],
+                            rhs=moving[b][0].bitcast(FP8X4),
+                            rhs_scale=moving[b][1],
+                            start=(b == 0 and i == 0),
+                            stop=(b == 1 and i == 1),
+                        )
             return banks
 
         def finish(half, banks):
-            cols = slice(HALF * half, HALF * (half + 1))
+            m_cols = slice(HALF * half, HALF * (half + 1))
             for j in range(4):
                 bounded = sbuf("bounded", [P, 2, HALF], F32, bufs=4)
                 nc.scalar.activation(bounded[:].rearrange("p i m -> p (i m)"), banks[j][:], ACT.Tanh)
                 result = sbuf("result", [P, 2, HALF], F32, bufs=4)
-                nc.vector.tensor_tensor(result[:], bounded[:], target_sb[:, 2 * j : 2 * j + 2, cols], ALU.subtract)
-                nc.sync.dma_start(out.rearrange("(c p) m -> p c m", p=P)[:, 2 * j : 2 * j + 2, cols], result[:])
+                nc.vector.tensor_tensor(result[:], bounded[:], target_sb[:, 2 * j : 2 * j + 2, m_cols], ALU.subtract)
+                nc.sync.dma_start(out.rearrange("(c p) m -> p c m", p=P)[:, 2 * j : 2 * j + 2, m_cols], result[:])
 
-        z_rows_a = sbuf("z_rows_a", [P, HALF // P, 2, P, 2], BF16)
-        x_a = placed("x_a", [P, 12, HALF], F32, 64)
+        low_rows = sbuf("low_rows", [P, HALF // P, 2, P, 2], BF16)
+        early_reads = placed("early_reads", [P, 10, HALF], F32, AT_EARLY_READS)
         for c in range(4, ROW_TILES):
-            fetch(c, 0, HALF, x_a[:, 2 * (c - 4), :], x_a[:, 2 * (c - 4) + 1, :], z_rows_a, nc.scalar.copy)
-        grouped_a = sbuf("grouped_a", [P, HALF, 4], BF16, tag="slot_late")
-        za_codes, za_scales = turn_and_quantise(z_rows_a, HALF, grouped_a, "za", nc.scalar.copy)
-        banks_a = product(0, za_codes, za_scales)
+            fetch(c, 0, HALF, early_reads[:, 2 * (c - 4), :], early_reads[:, 2 * (c - 4) + 1, :], low_rows)
+        high_rows = sbuf("high_rows", [P, HALF // P, 2, P, 2], BF16)
+        fetch(4, HALF, HALF, early_reads[:, 8, :], early_reads[:, 9, :], high_rows)
+        w_codes.append(placed("w_codes1", [P, 2, BANK], U32, AT_PAGE0))
+        quantise_w(1)
+        low_grouped = sbuf("low_grouped", [P, HALF, 4], BF16)
+        low_codes, low_scales = turn_and_quantise(low_rows, HALF, low_grouped, "low")
+        low_banks = product(0, low_codes, low_scales)
 
-        z_rows_b = sbuf("z_rows_b", [P, HALF // P, 2, P, 2], BF16)
-        x_c = sbuf("x_c", [P, 4, HALF], F32, tag="slot_late")
-        for c in range(4, ROW_TILES):
-            x = x_a[:, 8:12, :] if c < 6 else x_c
-            fetch(c, HALF, HALF, x[:, 2 * (c % 2), :], x[:, 2 * (c % 2) + 1, :], z_rows_b, nc.scalar.copy)
-        grouped_b = sbuf("grouped_b", [P, HALF, 4], BF16)
-        zb_codes, zb_scales = turn_and_quantise(z_rows_b, HALF, grouped_b, "zb", nc.scalar.copy)
-        finish(0, banks_a)
-        finish(1, product(1, zb_codes, zb_scales))
+        late_reads = sbuf("late_reads", [P, 6, HALF], F32, tag="low_grouped")
+        for c in range(5, ROW_TILES):
+            fetch(c, HALF, HALF, late_reads[:, 2 * (c - 5), :], late_reads[:, 2 * (c - 5) + 1, :], high_rows)
+        high_grouped = sbuf("high_grouped", [P, HALF, 4], BF16)
+        high_codes, high_scales = turn_and_quantise(high_rows, HALF, high_grouped, "high")
+        finish(0, low_banks)
+        finish(1, product(1, high_codes, high_scales))

@@ -22,25 +22,31 @@ BANK = 512
 PASS = 512
 HALF = M // 2
 ROW_TILES = H // P
-PAGES = 4
+PAGES = 3
 PER_COLUMN = 16
 ALIGN = 64
+FIRST = 256
 
 Z_BANK = 4
 TURN_BANK = 6
 
-AT_W4_WORDS = 0
-AT_TAB_SCALES = 3
-AT_PAGE2 = 8
-AT_H0_SECOND = 15
-AT_W_RIGHT = 24
-AT_V_SCALES = 27
-AT_W_LEFT = 32
-AT_W4_SCALES = 35
-AT_Z0_GROUPED = 40
-AT_EARLY_READS = 32
-AT_PAGE0 = 44
-AT_W_RAW = 52
+AT_WGS = 0
+AT_PICKED = 3.5
+AT_W4_LOW = 4
+AT_IDEAL_LOW = 9
+AT_TAB_W1 = 16
+AT_DEALT_S = 17
+AT_DEALT_W = 18
+AT_W_RAW0 = 20
+AT_TAB_S = 24
+AT_TAB_W0 = 30
+AT_W4_UP = 36
+AT_WGS_DEALT = 38
+AT_W_RAW1 = 54
+AT_IDEAL_UP = 70
+AT_TARGET = 78
+AT_W_ROUNDED = 94
+AT_Z0_GROUPED = 110
 
 
 def tile_list_zeolite_ring_check_kernel(
@@ -56,8 +62,8 @@ def tile_list_zeolite_ring_check_kernel(
         def sbuf(name, shape, dtype, tag=None, bufs=1):
             return sb.tile(shape, dtype, name=name, tag=tag or name, bufs=bufs, align_bytes=ALIGN)
 
-        def placed(name, shape, dtype, kib):
-            return staged.tile(shape, dtype, name=name, tag=name, align_bytes=ALIGN, offset=1024 * kib)
+        def placed(name, shape, dtype, kib, bufs=1):
+            return staged.tile(shape, dtype, name=name, tag=name, bufs=bufs, align_bytes=ALIGN, offset=int(1024 * kib))
 
         def bank(name, number):
             return psum.tile([P, BANK], F32, name=name, tag="bank%d" % number)
@@ -69,213 +75,280 @@ def tile_list_zeolite_ring_check_kernel(
         idx2 = lists.tile([P, S // PER_COLUMN], U16, name="idx2")
         idx3 = lists.tile([P, M // PER_COLUMN], U16, name="idx3")
         idx4 = lists.tile([P, M // PER_COLUMN], U16, name="idx4")
-        tab_s = placed("tab_s", [P, T], U8, AT_TAB_SCALES)
+        tab_s = placed("tab_s", [P, T], U8, AT_TAB_S)
+        tab_w = [placed("tab_w0", [P, T], I32, AT_TAB_W0), placed("tab_w1", [P, T], I32, AT_TAB_W1)]
+        w4_words_p = w4_words.rearrange("a p n -> p a n")
+        w4_first = sbuf("w4_first", [P, 2, 2 * P], U8)
+        wgs_first = sbuf("wgs_first", [P, FIRST], F32)
         nc.sync.dma_start(idx[:], offs)
         nc.sync.dma_start(tab_s[96:128, :].bitcast(I32), tab_scales.rearrange("a q n -> q a n").bitcast(I32))
+        nc.sync.dma_start(tab_w[0][:], tab_words[0].rearrange("p n t -> p (n t)").bitcast(I32))
         nc.sync.dma_start(idx2[:], offs2)
         nc.sync.dma_start(idx3[:], offs3)
+        nc.sync.dma_start(tab_w[1][:], tab_words[1].rearrange("p n t -> p (n t)").bitcast(I32))
+        nc.sync.dma_start(w4_first[:].bitcast(I32), w4_words_p[:, :, 0 : 2 * P].bitcast(I32))
+        nc.sync.dma_start(wgs_first[:], wgs[:, 0:FIRST])
         nc.sync.dma_start(idx4[:], offs4)
-        tab_w = [sbuf("tab_w0", [P, T], I32), placed("tab_w1", [P, T], I32, AT_W_RAW)]
-        for a in range(2):
-            nc.sync.dma_start(tab_w[a][:], tab_words[a].rearrange("p n t -> p (n t)").bitcast(I32))
 
-        w4_s = placed("w4_s", [P, 2, H], U8, AT_W4_SCALES)
-        v_s = placed("v_s", [P, 2, S], U8, AT_V_SCALES)
+        w4_s = sbuf("w4_s", [P, 2, H], U8)
+        v_s = sbuf("v_s", [P, 2, S], U8)
+        nc.gpsimd.memset(tab_s[0:96, :].bitcast(I32), 0)
         nc.gpsimd.memset(w4_s[:].bitcast(I32), 0)
-        nc.vector.memset(tab_s[0:96, :].bitcast(I32), 0)
         nc.vector.memset(v_s[:].bitcast(I32), 0)
         for g in range(4):
-            (nc.gpsimd, nc.scalar)[g % 2].dma_start(
+            nc.gpsimd.dma_start(
                 w4_s[32 * g : 32 * g + 4, :, :].bitcast(I32),
                 w4_scales[:, 4 * g : 4 * g + 4, :].rearrange("a r n -> r a n").bitcast(I32),
             )
-        pages = [placed("page0", [P, T2], F32, AT_PAGE0)]
+        pages = [sbuf("page%d" % i, [P, T2], F32) for i in range(PAGES)]
         nc.vector.memset(pages[0][:], 0.0)
+        ident = sbuf("ident", [P, P], F32)
+        make_identity(nc, ident[:])
+        for i in range(1, PAGES):
+            nc.gpsimd.memset(pages[i][:], 0.0)
 
-        picked_s = sbuf("picked_s", [P, S], U8)
+        picked_s = placed("picked_s", [P, S], U8, AT_PICKED)
         nc.vector.tensor_copy(picked_s[:], tab_s[:].indirect(idx[:]))
         for g in range(4):
             nc.scalar.dma_start(
                 v_s[32 * g : 32 * g + 4, :, :].bitcast(I32),
                 picked_s[96 + 8 * g : 96 + 8 * g + 8, :].bitcast(I32),
             )
-        ident = sbuf("ident", [P, P], F32, tag="picked_s")
-        make_identity(nc, ident[:])
-        w4_w = placed("w4_w", [P, 2, 2 * H], U8, AT_W4_WORDS)
-        nc.sync.dma_start(w4_w[:].bitcast(I32), w4_words.rearrange("a p n -> p a n").bitcast(I32))
-
         v_w = [sbuf("v_w%d" % a, [P, S], U32) for a in range(2)]
         nc.vector.tensor_copy(v_w[0][:], tab_w[0][:].bitcast(U32).indirect(idx[:]))
-        wgs_sb = sbuf("wgs_sb", [P, S], F32, tag="tab_w0")
-        nc.sync.dma_start(wgs_sb[:], wgs)
-        for part in range(2):
+        for first, count in ((0, FIRST), (FIRST, S - FIRST)):
             nc.vector.tensor_copy(
-                v_w[1][:, BANK * part : BANK * (part + 1)],
-                tab_w[1][:].bitcast(U32).indirect(idx[:, entries(BANK * part, BANK)]),
+                v_w[1][:, first : first + count], tab_w[1][:].bitcast(U32).indirect(idx[:, entries(first, count)])
             )
 
-        h0_parts = [sbuf("h0_first", [P, BANK], F32), placed("h0_second", [P, BANK], F32, AT_H0_SECOND)]
-        h_tiles = {c: sbuf("h%d" % c, [P, S], F32) for c in range(1, ROW_TILES)}
-        for c in range(ROW_TILES):
-            for part in range(2):
-                j_cols = slice(BANK * part, BANK * (part + 1))
-                h_acc = bank("h_acc", part)
-                for a in range(2):
+        wgs_sb = placed("wgs_sb", [P, S], F32, AT_WGS)
+        nc.sync.dma_start(wgs_sb[:], wgs)
+        w4_low = placed("w4_low", [P, 2, 2 * (PASS - P)], U8, AT_W4_LOW)
+        nc.sync.dma_start(w4_low[:].bitcast(I32), w4_words_p[:, :, 2 * P : 2 * PASS].bitcast(I32))
+        w4_up = placed("w4_up", [P, 2, 2 * PASS], U8, AT_W4_UP)
+        nc.sync.dma_start(w4_up[:].bitcast(I32), w4_words_p[:, :, 2 * PASS : 2 * H].bitcast(I32))
+        ideal_low = placed("ideal_low", [P, 4, M], F32, AT_IDEAL_LOW)
+        nc.sync.dma_start(ideal_low[:], ideal[0:PASS, :].rearrange("(c p) m -> p c m", p=P))
+
+        dealt_w = placed("dealt_w", [P, 4, 2, 2 * P], U8, AT_DEALT_W)
+        dealt_s = placed("dealt_s", [P, 4, 2, P], U8, AT_DEALT_S)
+        nc.vector.tensor_copy(
+            dealt_w[:].rearrange("p t a n -> p (t a n)").bitcast(I32).rearrange("p (t ag w) -> p t ag w", t=4, w=4),
+            w4_up[:].rearrange("p a n -> p (a n)").bitcast(I32).rearrange("p (ag t w) -> p t ag w", t=4, w=4),
+        )
+        nc.vector.tensor_copy(
+            dealt_s[:].rearrange("p t a n -> p (t a n)").bitcast(I32).rearrange("p (t a g w) -> p t a g w", t=4, a=2, w=2),
+            w4_s[:, :, PASS:H].bitcast(I32).rearrange("p a (g t w) -> p t a g w", t=4, w=2),
+        )
+
+        def stationary(c, a):
+            if c == 0:
+                return w4_first[:, a, :], w4_s[:, a, 0:P]
+            if c < 4:
+                return w4_low[:, a, 2 * P * (c - 1) : 2 * P * c], w4_s[:, a, P * c : P * (c + 1)]
+            return dealt_w[:, c - 4, a, :], dealt_s[:, c - 4, a, :]
+
+        def first_product(c, j0, width, step, number, dst):
+            h_acc = bank("h_acc", number)
+            pieces = width // step
+            for a in range(2):
+                words, scales = stationary(c, a)
+                for i in range(pieces):
+                    j_cols = slice(j0 + step * i, j0 + step * (i + 1))
                     nc.tensor.matmul_mx(
-                        out=h_acc[:],
-                        lhsT=w4_w[:, a, 2 * P * c : 2 * P * (c + 1)].bitcast(FP4X4),
-                        lhsT_scale=w4_s[:, a, P * c : P * (c + 1)],
+                        out=h_acc[:, step * i : step * (i + 1)],
+                        lhsT=words.bitcast(FP4X4),
+                        lhsT_scale=scales,
                         rhs=v_w[a][:, j_cols].bitcast(FP8X4),
                         rhs_scale=v_s[:, a, j_cols],
-                        start=(a == 0),
-                        stop=(a == 1),
+                        start=(a == 0 and i == 0),
+                        stop=(a == 1 and i == pieces - 1),
                     )
-                nc.scalar.copy(h0_parts[part][:] if c == 0 else h_tiles[c][:, j_cols], h_acc[:])
+            nc.scalar.copy(dst, h_acc[:, 0:width])
 
-        for part in range(2):
-            nc.vector.tensor_tensor(
-                pages[0][:].indirect(idx2[:, entries(BANK * part, BANK)]),
-                h0_parts[part][:],
-                wgs_sb[:, BANK * part : BANK * (part + 1)],
-                ALU.mult,
-            )
-        pages.append(sbuf("page1", [P, T2], F32, tag="h0_first"))
-        nc.gpsimd.memset(pages[1][:], 0.0)
-        for i in range(2):
-            pages.append(placed("page%d" % (2 + i), [P, T2], F32, AT_PAGE2 + 8 * i))
-            nc.gpsimd.memset(pages[2 + i][:], 0.0)
+        h0_first = placed("h0_first", [P, FIRST], F32, AT_WGS_DEALT)
+        h0_rest = placed("h0_rest", [P, S - FIRST], F32, AT_W_RAW1)
+        first_product(0, 0, FIRST, P, 0, h0_first[:])
+        first_product(0, FIRST, BANK - FIRST, P, 1, h0_rest[:, 0 : BANK - FIRST])
+        first_product(0, BANK, BANK, BANK, 2, h0_rest[:, BANK - FIRST :])
+        h_tiles = {1: placed("h1", [P, S], F32, AT_IDEAL_UP), 2: placed("h2", [P, S], F32, AT_TARGET)}
+        for c in range(3, ROW_TILES):
+            h_tiles[c] = sbuf("h%d" % c, [P, S], F32)
+        for c in range(1, ROW_TILES):
+            for part in range(2):
+                first_product(c, BANK * part, BANK, BANK, (2 * c + part + 1) % 4, h_tiles[c][:, BANK * part : BANK * (part + 1)])
 
-        w_codes = [sbuf("w_codes0", [P, 2, BANK], U32)]
-        w_scales = [sbuf("w_scales%d" % side, [P, 2, BANK], U8) for side in range(2)]
-        w_rounded = {}
+        nc.vector.tensor_tensor(pages[0][:].indirect(idx2[:, entries(0, FIRST)]), h0_first[:], wgs_first[:], ALU.mult)
+        nc.vector.tensor_tensor(
+            pages[0][:].indirect(idx2[:, entries(FIRST, S - FIRST)]), h0_rest[:], wgs_sb[:, FIRST:S], ALU.mult
+        )
 
-        def quantise_w(side):
-            for b in range(2):
-                nc.vector.quantize_mx(
-                    out=w_codes[side][:, b, :].bitcast(FP8X4),
-                    scales=w_scales[side][:, b, :],
-                    in_=w_rounded[b, side][:].rearrange("p n t -> p (n t)"),
+        minus_ideal = sbuf("minus_ideal", [P, 4, M], F32)
+        for c in range(4):
+            nc.scalar.activation(minus_ideal[:, c, :], ideal_low[:, c, :], ACT.Copy, scale=-1.0)
+
+        def dealt_rows(matrix, t):
+            return matrix[PASS:H, :].rearrange("(g t i) n -> t g i n", t=4, i=8)[t]
+
+        w_raw = [placed("w_raw0", [P, 4, N], F32, AT_W_RAW0), placed("w_raw1", [P, 4, N], F32, AT_W_RAW1)]
+        nc.sync.dma_start(w_raw[0][:], w[0:PASS, :].rearrange("(p t) n -> p t n", t=4))
+        wgs_dealt = placed("wgs_dealt", [P, 4, S], F32, AT_WGS_DEALT)
+        for t in range(4):
+            for q in range(4):
+                nc.sync.dma_start(
+                    wgs_dealt[32 * q : 32 * (q + 1), t, :], wgs.rearrange("(g t i) j -> t g i j", t=4, i=8)[t]
                 )
-
-        w_raw = placed("w_raw", [P, 2, 4, N], F32, AT_W_RAW)
-        for b in range(2):
-            nc.sync.dma_start(w_raw[:, b], w[PASS * b : PASS * (b + 1), :].rearrange("(p t) n -> p t n", t=4))
-            for side in range(2):
-                w_rounded[b, side] = placed(
-                    "w_rounded%d%d" % (b, side), [P, BANK, 4], BF16, (AT_W_LEFT, AT_W_RIGHT)[side] + 4 * b
-                )
-                nc.scalar.copy(
-                    w_rounded[b, side][:].rearrange("p (c i) t -> p c t i", i=4),
-                    w_raw[:, b][:, :, BANK * side : BANK * (side + 1)].rearrange("p t (c i) -> p c t i", i=4),
-                )
-        quantise_w(0)
-
-        ideal_sb = sbuf("ideal_sb", [P, ROW_TILES, M], F32, tag="h1")
-        nc.sync.dma_start(ideal_sb[:], ideal.rearrange("(c p) m -> p c m", p=P))
-        minus_ideal = sbuf("minus_ideal", [P, ROW_TILES, M], F32, tag="v_w0")
-        for c in range(ROW_TILES):
-            nc.scalar.activation(minus_ideal[:, c, :], ideal_sb[:, c, :], ACT.Copy, scale=-1.0)
-        target_sb = sbuf("target_sb", [P, ROW_TILES, M], F32, tag="v_w1")
+        for t in range(4):
+            nc.sync.dma_start(w_raw[1][:, t, :], dealt_rows(w, t))
+        ideal_up = placed("ideal_up", [P, 4, M], F32, AT_IDEAL_UP)
+        for t in range(4):
+            nc.sync.dma_start(ideal_up[:, t, :], dealt_rows(ideal, t))
+        target_sb = placed("target_sb", [P, ROW_TILES, M], F32, AT_TARGET)
         nc.sync.dma_start(target_sb[:], target.rearrange("(c p) m -> p c m", p=P))
 
-        def scatter(c):
-            nc.vector.tensor_tensor(pages[c % PAGES][:].indirect(idx2[:]), h_tiles[c][:], wgs_sb[:], ALU.mult)
-
-        def fetch(c, m0, width, site, facing, z_rows):
-            nc.vector.tensor_copy(site, pages[c % PAGES][:].indirect(idx3[:, entries(m0, width)]))
-            nc.vector.tensor_copy(facing, pages[c % PAGES][:].indirect(idx4[:, entries(m0, width)]))
-            z_acc = bank("z_acc", Z_BANK + c % 2)
-            blocks = width // P
-            terms = (minus_ideal[:, c, m0 : m0 + width], site, facing)
-            for number, term in enumerate(terms):
-                for j in range(blocks):
-                    nc.tensor.matmul(
-                        z_acc[:, P * j : P * (j + 1)],
-                        term[:, P * j : P * (j + 1)],
-                        ident[:],
-                        start=(number == 0 and j == 0),
-                        stop=(number == len(terms) - 1 and j == blocks - 1),
-                        is_transpose=True,
-                    )
-            nc.scalar.copy(
-                z_rows[:, :, :, 32 * (c % 4) : 32 * (c % 4 + 1), :],
-                z_acc[:, 0:width].rearrange("m (j p u e) -> m j u p e", j=blocks, u=2, e=2),
-            )
-
-        def turn_and_quantise(z_rows, width, grouped, name):
-            pairs = z_rows[:].rearrange("m j u p e -> m j u (p e)").bitcast(F32)
-            for j in range(width // P):
-                turned = bank("turned", TURN_BANK + j % 2)
-                for u in range(2):
-                    nc.tensor.transpose(turned[:, P * u : P * (u + 1)], pairs[:, j, u, :], ident[:])
+        w0_rounded = placed("w0_rounded", [P, N, 4], BF16, AT_W_ROUNDED)
+        w1_rounded = [placed("w1_rounded%d" % side, [P, BANK, 4], BF16, AT_W_ROUNDED + 8 + 4 * side) for side in range(2)]
+        for b in range(2):
+            for side in range(2):
+                n_cols = slice(BANK * side, BANK * (side + 1))
+                rounded = w0_rounded[:, n_cols, :] if b == 0 else w1_rounded[side][:]
                 nc.scalar.copy(
-                    grouped[:, P * j : P * (j + 1), :].bitcast(F32),
-                    turned[:, 0 : 2 * P].rearrange("p (u m) -> p m u", u=2),
+                    rounded.rearrange("p (c i) t -> p c t i", i=4),
+                    w_raw[b][:, :, n_cols].rearrange("p t (c i) -> p c t i", i=4),
                 )
-            codes = sbuf(name + "_codes", [P, width], U32)
+
+        def quantise(name, grouped, width, tag=None):
+            codes = sbuf(name + "_codes", [P, width], U32, tag=tag)
             scales = sbuf(name + "_scales", [P, width], U8)
-            nc.vector.quantize_mx(
-                out=codes[:].bitcast(FP8X4), scales=scales[:], in_=grouped[:].rearrange("p m t -> p (m t)")
-            )
+            nc.vector.quantize_mx(out=codes[:].bitcast(FP8X4), scales=scales[:], in_=grouped)
             return codes, scales
+
+        def scatter(c):
+            weights = wgs_sb[:] if c < 4 else wgs_dealt[:, c - 4, :]
+            nc.vector.tensor_tensor(pages[c % PAGES][:].indirect(idx2[:]), h_tiles[c][:], weights, ALU.mult)
 
         z0_rows = sbuf("z0_rows", [P, M // P, 2, P, 2], BF16)
         for c in range(4):
             scatter(c + 1)
             site = sbuf("site", [P, M], F32, bufs=4)
             facing = sbuf("facing", [P, M], F32, bufs=4)
-            fetch(c, 0, M, site[:], facing[:], z0_rows)
+            nc.vector.tensor_copy(site[:], pages[c % PAGES][:].indirect(idx3[:]))
+            nc.vector.tensor_copy(facing[:], pages[c % PAGES][:].indirect(idx4[:]))
+            z_acc = bank("z_acc", Z_BANK + c % 2)
+            terms = (minus_ideal[:, c, :], site[:], facing[:])
+            for number, term in enumerate(terms):
+                for j in range(4):
+                    nc.tensor.matmul(
+                        z_acc[:, P * j : P * (j + 1)],
+                        term[:, P * j : P * (j + 1)],
+                        ident[:],
+                        start=(number == 0 and j == 0),
+                        stop=(number == 2 and j == 3),
+                        is_transpose=True,
+                    )
+            nc.scalar.copy(
+                z0_rows[:, :, :, 32 * c : 32 * (c + 1), :],
+                z_acc[:].rearrange("m (j p u e) -> m j u p e", j=4, u=2, e=2),
+            )
         z0_grouped = placed("z0_grouped", [P, M, 4], BF16, AT_Z0_GROUPED)
-        z0_codes, z0_scales = turn_and_quantise(z0_rows, M, z0_grouped, "z0")
-        for c in range(5, ROW_TILES):
-            scatter(c)
+        pairs = z0_rows[:].rearrange("m j u p e -> m j u (p e)").bitcast(F32)
+        for j in range(M // P):
+            turned = bank("turned", TURN_BANK + j % 2)
+            for u in range(2):
+                nc.tensor.transpose(turned[:, P * u : P * (u + 1)], pairs[:, j, u, :], ident[:])
+            nc.scalar.copy(
+                z0_grouped[:, P * j : P * (j + 1), :].bitcast(F32),
+                turned[:, 0 : 2 * P].rearrange("p (u m) -> p m u", u=2),
+            )
 
-        def product(half, z1_codes, z1_scales):
-            banks = []
-            m_cols = slice(HALF * half, HALF * (half + 1))
-            moving = ((z0_codes[:, m_cols], z0_scales[:, m_cols]), (z1_codes[:], z1_scales[:]))
+        def read_site(c, m0, width, dst):
+            nc.vector.tensor_tensor(
+                dst, pages[c % PAGES][:].indirect(idx3[:, entries(m0, width)]), ideal_up[:, c - 4, m0 : m0 + width], ALU.subtract
+            )
+
+        def read_facing(c, m0, width, site_part, dst):
+            nc.vector.tensor_tensor(dst, pages[c % PAGES][:].indirect(idx4[:, entries(m0, width)]), site_part, ALU.add)
+
+        scatter(5)
+        z0_codes, z0_scales = quantise("z0", z0_grouped[:].rearrange("p m t -> p (m t)"), M)
+        w0_codes, w0_scales = quantise("w0", w0_rounded[:].rearrange("p n t -> p (n t)"), N)
+        w_quantised = {(0, side): (w0_codes[:, BANK * side : BANK * (side + 1)], w0_scales[:, BANK * side : BANK * (side + 1)]) for side in range(2)}
+
+        y_banks = [bank("y_acc", j) for j in range(8)]
+
+        def second_product(b, half, codes, scales):
             for j in range(4):
-                y_acc = bank("y_acc", j)
-                banks.append(y_acc)
-                for b in range(2):
-                    for i in range(2):
-                        n_cols = slice(P * (2 * (j % 2) + i), P * (2 * (j % 2) + i + 1))
-                        nc.tensor.matmul_mx(
-                            out=y_acc[:, HALF * i : HALF * (i + 1)],
-                            lhsT=w_codes[j // 2][:, b, n_cols].bitcast(FP8X4),
-                            lhsT_scale=w_scales[j // 2][:, b, n_cols],
-                            rhs=moving[b][0].bitcast(FP8X4),
-                            rhs_scale=moving[b][1],
-                            start=(b == 0 and i == 0),
-                            stop=(b == 1 and i == 1),
-                        )
-            return banks
+                w_codes, w_scales = w_quantised[b, j // 2]
+                for i in range(2):
+                    n_cols = slice(P * (2 * (j % 2) + i), P * (2 * (j % 2) + i + 1))
+                    nc.tensor.matmul_mx(
+                        out=y_banks[4 * half + j][:, HALF * i : HALF * (i + 1)],
+                        lhsT=w_codes[:, n_cols].bitcast(FP8X4),
+                        lhsT_scale=w_scales[:, n_cols],
+                        rhs=codes.bitcast(FP8X4),
+                        rhs_scale=scales,
+                        start=(b == 0 and i == 0),
+                        stop=(b == 1 and i == 1),
+                    )
 
-        def finish(half, banks):
+        for half in range(2):
+            m_cols = slice(HALF * half, HALF * (half + 1))
+            second_product(0, half, z0_codes[:, m_cols], z0_scales[:, m_cols])
+
+        site4 = placed("site4", [P, M], F32, AT_Z0_GROUPED)
+        read_site(4, 0, M, site4[:])
+        scatter(6)
+        z45 = placed("z45", [P, 2, M], F32, AT_W_ROUNDED + 6)
+        w_quantised[1, 0] = quantise("w10", w1_rounded[0][:].rearrange("p n t -> p (n t)"), BANK)
+        site5 = sbuf("site5", [P, M], F32)
+        read_site(5, 0, M, site5[:])
+        read_facing(4, 0, M, site4[:], z45[:, 0, :])
+        read_facing(5, 0, M, site5[:], z45[:, 1, :])
+        scatter(7)
+        site6 = placed("site6", [P, M], F32, AT_Z0_GROUPED)
+        read_site(6, 0, M, site6[:])
+
+        shared = sbuf("shared", [P, 2 * HALF], F32)
+        low_tile = sbuf("low_grouped", [P, 4 * HALF], BF16)
+        low_grouped = low_tile[:]
+        high_tile = sbuf("high_grouped", [P, 4 * HALF], BF16)
+        grouped = (low_grouped, high_tile[:])
+
+        def weave(engine_copy, half, u, z_pair):
+            engine_copy(
+                grouped[half].rearrange("p (m t) -> p m t", t=4)[:, :, 2 * u : 2 * u + 2], z_pair.rearrange("p e m -> p m e")
+            )
+
+        for half in range(2):
+            weave(nc.scalar.copy, half, 0, z45[:, :, HALF * half : HALF * (half + 1)])
+        z67_low = sbuf("z67_low", [P, 2, HALF], F32)
+        read_site(7, 0, HALF, shared[:, 0:HALF])
+        read_facing(6, 0, HALF, site6[:, 0:HALF], z67_low[:, 0, :])
+        read_facing(7, 0, HALF, shared[:, 0:HALF], z67_low[:, 1, :])
+        weave(nc.scalar.copy, 0, 1, z67_low[:])
+        read_site(7, HALF, HALF, site6[:, 0:HALF])
+        read_facing(6, HALF, HALF, site6[:, HALF:M], shared[:, 0:HALF])
+        read_facing(7, HALF, HALF, site6[:, 0:HALF], shared[:, HALF : 2 * HALF])
+        low_codes, low_scales = quantise("low", low_grouped, HALF)
+        w_quantised[1, 1] = quantise("w11", w1_rounded[1][:].rearrange("p n t -> p (n t)"), BANK, tag="low_grouped")
+        second_product(1, 0, low_codes[:], low_scales[:])
+        weave(nc.scalar.copy, 1, 1, shared[:, 0 : 2 * HALF].rearrange("p (e m) -> p e m", e=2))
+        high_codes, high_scales = quantise("high", high_tile[:], HALF)
+        second_product(1, 1, high_codes[:], high_scales[:])
+
+        out_rows = out.rearrange("(c p) m -> p c m", p=P)
+        for half in range(2):
             m_cols = slice(HALF * half, HALF * (half + 1))
             for j in range(4):
-                bounded = sbuf("bounded", [P, 2, HALF], F32, bufs=4)
-                nc.scalar.activation(bounded[:].rearrange("p i m -> p (i m)"), banks[j][:], ACT.Tanh)
-                result = sbuf("result", [P, 2, HALF], F32, bufs=4)
-                nc.vector.tensor_tensor(result[:], bounded[:], target_sb[:, 2 * j : 2 * j + 2, m_cols], ALU.subtract)
-                nc.sync.dma_start(out.rearrange("(c p) m -> p c m", p=P)[:, 2 * j : 2 * j + 2, m_cols], result[:])
-
-        low_rows = sbuf("low_rows", [P, HALF // P, 2, P, 2], BF16)
-        early_reads = placed("early_reads", [P, 10, HALF], F32, AT_EARLY_READS)
-        for c in range(4, ROW_TILES):
-            fetch(c, 0, HALF, early_reads[:, 2 * (c - 4), :], early_reads[:, 2 * (c - 4) + 1, :], low_rows)
-        high_rows = sbuf("high_rows", [P, HALF // P, 2, P, 2], BF16)
-        fetch(4, HALF, HALF, early_reads[:, 8, :], early_reads[:, 9, :], high_rows)
-        w_codes.append(placed("w_codes1", [P, 2, BANK], U32, AT_PAGE0))
-        quantise_w(1)
-        low_grouped = sbuf("low_grouped", [P, HALF, 4], BF16)
-        low_codes, low_scales = turn_and_quantise(low_rows, HALF, low_grouped, "low")
-        low_banks = product(0, low_codes, low_scales)
-
-        late_reads = sbuf("late_reads", [P, 6, HALF], F32, tag="low_grouped")
-        for c in range(5, ROW_TILES):
-            fetch(c, HALF, HALF, late_reads[:, 2 * (c - 5), :], late_reads[:, 2 * (c - 5) + 1, :], high_rows)
-        high_grouped = sbuf("high_grouped", [P, HALF, 4], BF16)
-        high_codes, high_scales = turn_and_quantise(high_rows, HALF, high_grouped, "high")
-        finish(0, low_banks)
-        finish(1, product(1, high_codes, high_scales))
+                bounded = placed("bounded", [P, 2, HALF], F32, AT_W_RAW1, bufs=4)
+                result = placed("result", [P, 2, HALF], F32, AT_W_RAW1 + 8, bufs=8)
+                for i0, count in ((0, 1), (1, 1)) if (half, j) == (1, 3) else ((0, 2),):
+                    tiles = slice(i0, i0 + count)
+                    rows = slice(2 * j + i0, 2 * j + i0 + count)
+                    nc.scalar.activation(
+                        bounded[:, tiles, :].rearrange("p i m -> p (i m)"),
+                        y_banks[4 * half + j][:, HALF * i0 : HALF * (i0 + count)],
+                        ACT.Tanh,
+                    )
+                    nc.vector.tensor_tensor(result[:, tiles, :], bounded[:, tiles, :], target_sb[:, rows, m_cols], ALU.subtract)
+                    nc.sync.dma_start(out_rows[:, rows, m_cols], result[:, tiles, :])

@@ -47,6 +47,7 @@ AT_IDEAL_UP = 70
 AT_TARGET = 78
 AT_W_ROUNDED = 94
 AT_Z0_GROUPED = 110
+AT_LOW_GROUPED = 117
 
 
 def tile_list_zeolite_ring_check_kernel(
@@ -217,8 +218,11 @@ def tile_list_zeolite_ring_check_kernel(
                     w_raw[b][:, :, n_cols].rearrange("p t (c i) -> p c t i", i=4),
                 )
 
-        def quantise(name, grouped, width, tag=None):
-            codes = sbuf(name + "_codes", [P, width], U32, tag=tag)
+        def quantise(name, grouped, width, kib=None):
+            if kib is None:
+                codes = sbuf(name + "_codes", [P, width], U32)
+            else:
+                codes = placed(name + "_codes", [P, width], U32, kib)
             scales = sbuf(name + "_scales", [P, width], U8)
             nc.vector.quantize_mx(out=codes[:].bitcast(FP8X4), scales=scales[:], in_=grouped)
             return codes, scales
@@ -250,14 +254,14 @@ def tile_list_zeolite_ring_check_kernel(
                 z0_rows[:, :, :, 32 * c : 32 * (c + 1), :],
                 z_acc[:].rearrange("m (j p u e) -> m j u p e", j=4, u=2, e=2),
             )
-        z0_grouped = placed("z0_grouped", [P, M, 4], BF16, AT_Z0_GROUPED)
+        z0_grouped = [placed("z0_grouped%d" % half, [P, HALF, 4], BF16, AT_Z0_GROUPED + 2 * half) for half in range(2)]
         pairs = z0_rows[:].rearrange("m j u p e -> m j u (p e)").bitcast(F32)
         for j in range(M // P):
             turned = bank("turned", TURN_BANK + j % 2)
             for u in range(2):
                 nc.tensor.transpose(turned[:, P * u : P * (u + 1)], pairs[:, j, u, :], ident[:])
             nc.scalar.copy(
-                z0_grouped[:, P * j : P * (j + 1), :].bitcast(F32),
+                z0_grouped[j // 2][:, P * (j % 2) : P * (j % 2 + 1), :].bitcast(F32),
                 turned[:, 0 : 2 * P].rearrange("p (u m) -> p m u", u=2),
             )
 
@@ -270,14 +274,14 @@ def tile_list_zeolite_ring_check_kernel(
             nc.vector.tensor_tensor(dst, pages[c % PAGES][:].indirect(idx4[:, entries(m0, width)]), site_part, ALU.add)
 
         scatter(5)
-        z0_codes, z0_scales = quantise("z0", z0_grouped[:].rearrange("p m t -> p (m t)"), M)
+        z0_codes, z0_scales = quantise("z0_low", z0_grouped[0][:].rearrange("p m t -> p (m t)"), HALF)
         w0_codes, w0_scales = quantise("w0", w0_rounded[:].rearrange("p n t -> p (n t)"), N)
         w_quantised = {(0, side): (w0_codes[:, BANK * side : BANK * (side + 1)], w0_scales[:, BANK * side : BANK * (side + 1)]) for side in range(2)}
 
         y_banks = [bank("y_acc", j) for j in range(8)]
 
-        def second_product(b, half, codes, scales):
-            for j in range(4):
+        def second_product(b, half, codes, scales, banks=range(4)):
+            for j in banks:
                 w_codes, w_scales = w_quantised[b, j // 2]
                 for i in range(2):
                     n_cols = slice(P * (2 * (j % 2) + i), P * (2 * (j % 2) + i + 1))
@@ -291,9 +295,7 @@ def tile_list_zeolite_ring_check_kernel(
                         stop=(b == 1 and i == 1),
                     )
 
-        for half in range(2):
-            m_cols = slice(HALF * half, HALF * (half + 1))
-            second_product(0, half, z0_codes[:, m_cols], z0_scales[:, m_cols])
+        second_product(0, 0, z0_codes[:], z0_scales[:])
 
         site4 = placed("site4", [P, M], F32, AT_Z0_GROUPED)
         read_site(4, 0, M, site4[:])
@@ -309,7 +311,7 @@ def tile_list_zeolite_ring_check_kernel(
         read_site(6, 0, M, site6[:])
 
         shared = sbuf("shared", [P, 2 * HALF], F32)
-        low_tile = sbuf("low_grouped", [P, 4 * HALF], BF16)
+        low_tile = placed("low_grouped", [P, 4 * HALF], BF16, AT_LOW_GROUPED)
         low_grouped = low_tile[:]
         high_tile = sbuf("high_grouped", [P, 4 * HALF], BF16)
         grouped = (low_grouped, high_tile[:])
@@ -330,11 +332,14 @@ def tile_list_zeolite_ring_check_kernel(
         read_facing(6, HALF, HALF, site6[:, HALF:M], shared[:, 0:HALF])
         read_facing(7, HALF, HALF, site6[:, 0:HALF], shared[:, HALF : 2 * HALF])
         low_codes, low_scales = quantise("low", low_grouped, HALF)
-        w_quantised[1, 1] = quantise("w11", w1_rounded[1][:].rearrange("p n t -> p (n t)"), BANK, tag="low_grouped")
+        w_quantised[1, 1] = quantise("w11", w1_rounded[1][:].rearrange("p n t -> p (n t)"), BANK, AT_LOW_GROUPED - 1)
         second_product(1, 0, low_codes[:], low_scales[:])
+        z0_high = quantise("z0_high", z0_grouped[1][:].rearrange("p m t -> p (m t)"), HALF, AT_LOW_GROUPED + 1)
         weave(nc.scalar.copy, 1, 1, shared[:, 0 : 2 * HALF].rearrange("p (e m) -> p e m", e=2))
         high_codes, high_scales = quantise("high", high_tile[:], HALF)
-        second_product(1, 1, high_codes[:], high_scales[:])
+        for j in range(4):
+            second_product(0, 1, z0_high[0][:], z0_high[1][:], [j])
+            second_product(1, 1, high_codes[:], high_scales[:], [j])
 
         out_rows = out.rearrange("(c p) m -> p c m", p=P)
         for half in range(2):
@@ -342,7 +347,7 @@ def tile_list_zeolite_ring_check_kernel(
             for j in range(4):
                 bounded = placed("bounded", [P, 2, HALF], F32, AT_W_RAW1, bufs=4)
                 result = placed("result", [P, 2, HALF], F32, AT_W_RAW1 + 8, bufs=8)
-                for i0, count in ((0, 1), (1, 1)) if (half, j) == (1, 3) else ((0, 2),):
+                for i0, count in ((0, 1), (1, 1)) if (half, j) in ((0, 0), (1, 3)) else ((0, 2),):
                     tiles = slice(i0, i0 + count)
                     rows = slice(2 * j + i0, 2 * j + i0 + count)
                     nc.scalar.activation(

@@ -41,13 +41,15 @@ AT_W_RAW0 = 20
 AT_TAB_S = 24
 AT_TAB_W0 = 30
 AT_W4_UP = 36
-AT_WGS_DEALT = 38
-AT_W_RAW1 = 54
+AT_W_RAW1 = 38
+AT_WGS_DEALT = 54
 AT_IDEAL_UP = 70
 AT_TARGET = 78
 AT_W_ROUNDED = 94
 AT_Z0_GROUPED = 110
 AT_LOW_GROUPED = 117
+AT_H7 = 120
+AT_SITE4 = 124
 
 
 def tile_list_zeolite_ring_check_kernel(
@@ -167,14 +169,15 @@ def tile_list_zeolite_ring_check_kernel(
                     )
             nc.scalar.copy(dst, h_acc[:, 0:width])
 
-        h0_first = placed("h0_first", [P, FIRST], F32, AT_WGS_DEALT)
-        h0_rest = placed("h0_rest", [P, S - FIRST], F32, AT_W_RAW1)
+        h0_first = placed("h0_first", [P, FIRST], F32, AT_W_RAW1)
+        h0_rest = placed("h0_rest", [P, S - FIRST], F32, AT_IDEAL_UP - 1.5)
         first_product(0, 0, FIRST, P, 0, h0_first[:])
         first_product(0, FIRST, BANK - FIRST, P, 1, h0_rest[:, 0 : BANK - FIRST])
         first_product(0, BANK, BANK, BANK, 2, h0_rest[:, BANK - FIRST :])
-        h_tiles = {1: placed("h1", [P, S], F32, AT_IDEAL_UP), 2: placed("h2", [P, S], F32, AT_TARGET)}
-        for c in range(3, ROW_TILES):
+        h_tiles = {1: sbuf("h1", [P, S], F32), 2: placed("h2", [P, S], F32, AT_TARGET)}
+        for c in range(3, ROW_TILES - 1):
             h_tiles[c] = sbuf("h%d" % c, [P, S], F32)
+        h_tiles[7] = placed("h7", [P, S], F32, AT_H7)
         for c in range(1, ROW_TILES):
             for part in range(2):
                 first_product(c, BANK * part, BANK, BANK, (2 * c + part + 1) % 4, h_tiles[c][:, BANK * part : BANK * (part + 1)])
@@ -193,17 +196,17 @@ def tile_list_zeolite_ring_check_kernel(
 
         w_raw = [placed("w_raw0", [P, 4, N], F32, AT_W_RAW0), placed("w_raw1", [P, 4, N], F32, AT_W_RAW1)]
         nc.sync.dma_start(w_raw[0][:], w[0:PASS, :].rearrange("(p t) n -> p t n", t=4))
-        wgs_dealt = placed("wgs_dealt", [P, 4, S], F32, AT_WGS_DEALT)
-        for t in range(4):
-            for q in range(4):
-                nc.sync.dma_start(
-                    wgs_dealt[32 * q : 32 * (q + 1), t, :], wgs.rearrange("(g t i) j -> t g i j", t=4, i=8)[t]
-                )
         for t in range(4):
             nc.sync.dma_start(w_raw[1][:, t, :], dealt_rows(w, t))
         ideal_up = placed("ideal_up", [P, 4, M], F32, AT_IDEAL_UP)
         for t in range(4):
             nc.sync.dma_start(ideal_up[:, t, :], dealt_rows(ideal, t))
+        wgs_dealt = placed("wgs_dealt", [P, 4, S], F32, AT_WGS_DEALT)
+        for q in range(4):
+            for t in range(4):
+                nc.sync.dma_start(
+                    wgs_dealt[32 * q : 32 * (q + 1), t, :], wgs.rearrange("(g t i) j -> t g i j", t=4, i=8)[t]
+                )
         target_sb = placed("target_sb", [P, ROW_TILES, M], F32, AT_TARGET)
         nc.sync.dma_start(target_sb[:], target.rearrange("(c p) m -> p c m", p=P))
 
@@ -274,7 +277,6 @@ def tile_list_zeolite_ring_check_kernel(
             nc.vector.tensor_tensor(dst, pages[c % PAGES][:].indirect(idx4[:, entries(m0, width)]), site_part, ALU.add)
 
         scatter(5)
-        z0_codes, z0_scales = quantise("z0_low", z0_grouped[0][:].rearrange("p m t -> p (m t)"), HALF)
         w0_codes, w0_scales = quantise("w0", w0_rounded[:].rearrange("p n t -> p (n t)"), N)
         w_quantised = {(0, side): (w0_codes[:, BANK * side : BANK * (side + 1)], w0_scales[:, BANK * side : BANK * (side + 1)]) for side in range(2)}
 
@@ -295,9 +297,8 @@ def tile_list_zeolite_ring_check_kernel(
                         stop=(b == 1 and i == 1),
                     )
 
-        second_product(0, 0, z0_codes[:], z0_scales[:])
 
-        site4 = placed("site4", [P, M], F32, AT_Z0_GROUPED)
+        site4 = placed("site4", [P, M], F32, AT_SITE4)
         read_site(4, 0, M, site4[:])
         scatter(6)
         z45 = placed("z45", [P, 2, M], F32, AT_W_ROUNDED + 6)
@@ -307,10 +308,12 @@ def tile_list_zeolite_ring_check_kernel(
         read_facing(4, 0, M, site4[:], z45[:, 0, :])
         read_facing(5, 0, M, site5[:], z45[:, 1, :])
         scatter(7)
-        site6 = placed("site6", [P, M], F32, AT_Z0_GROUPED)
+        site6 = placed("site6", [P, M], F32, AT_SITE4)
         read_site(6, 0, M, site6[:])
+        z0_codes, z0_scales = quantise("z0_low", z0_grouped[0][:].rearrange("p m t -> p (m t)"), HALF, AT_H7)
+        second_product(0, 0, z0_codes[:], z0_scales[:])
 
-        shared = sbuf("shared", [P, 2 * HALF], F32)
+        shared = placed("z67_high", [P, 2 * HALF], F32, AT_IDEAL_UP + 6)
         low_tile = placed("low_grouped", [P, 4 * HALF], BF16, AT_LOW_GROUPED)
         low_grouped = low_tile[:]
         high_tile = sbuf("high_grouped", [P, 4 * HALF], BF16)
@@ -323,14 +326,14 @@ def tile_list_zeolite_ring_check_kernel(
 
         for half in range(2):
             weave(nc.scalar.copy, half, 0, z45[:, :, HALF * half : HALF * (half + 1)])
-        z67_low = sbuf("z67_low", [P, 2, HALF], F32)
-        read_site(7, 0, HALF, shared[:, 0:HALF])
+        z67_low = placed("z67_low", [P, 2, HALF], F32, AT_H7 + 2)
+        site7 = sbuf("site7", [P, M], F32)
+        read_site(7, 0, M, site7[:])
         read_facing(6, 0, HALF, site6[:, 0:HALF], z67_low[:, 0, :])
-        read_facing(7, 0, HALF, shared[:, 0:HALF], z67_low[:, 1, :])
+        read_facing(7, 0, HALF, site7[:, 0:HALF], z67_low[:, 1, :])
         weave(nc.scalar.copy, 0, 1, z67_low[:])
-        read_site(7, HALF, HALF, site6[:, 0:HALF])
         read_facing(6, HALF, HALF, site6[:, HALF:M], shared[:, 0:HALF])
-        read_facing(7, HALF, HALF, site6[:, 0:HALF], shared[:, HALF : 2 * HALF])
+        read_facing(7, HALF, HALF, site7[:, HALF:M], shared[:, HALF : 2 * HALF])
         low_codes, low_scales = quantise("low", low_grouped, HALF)
         w_quantised[1, 1] = quantise("w11", w1_rounded[1][:].rearrange("p n t -> p (n t)"), BANK, AT_LOW_GROUPED - 1)
         second_product(1, 0, low_codes[:], low_scales[:])
@@ -345,15 +348,19 @@ def tile_list_zeolite_ring_check_kernel(
         for half in range(2):
             m_cols = slice(HALF * half, HALF * (half + 1))
             for j in range(4):
-                bounded = placed("bounded", [P, 2, HALF], F32, AT_W_RAW1, bufs=4)
-                result = placed("result", [P, 2, HALF], F32, AT_W_RAW1 + 8, bufs=8)
-                for i0, count in ((0, 1), (1, 1)) if (half, j) in ((0, 0), (1, 3)) else ((0, 2),):
-                    tiles = slice(i0, i0 + count)
-                    rows = slice(2 * j + i0, 2 * j + i0 + count)
-                    nc.scalar.activation(
-                        bounded[:, tiles, :].rearrange("p i m -> p (i m)"),
-                        y_banks[4 * half + j][:, HALF * i0 : HALF * (i0 + count)],
-                        ACT.Tanh,
-                    )
-                    nc.vector.tensor_tensor(result[:, tiles, :], bounded[:, tiles, :], target_sb[:, rows, m_cols], ALU.subtract)
-                    nc.sync.dma_start(out_rows[:, rows, m_cols], result[:, tiles, :])
+                bounded = placed("bounded", [P, BANK], F32, AT_W_RAW1, bufs=4)
+                result = placed("result", [P, BANK], F32, AT_W_RAW1 + 8, bufs=8)
+                pieces = {(0, 0): (HALF, HALF), (1, 3): (HALF, P, P)}.get((half, j), (BANK,))
+                for number, width in enumerate(pieces):
+                    first = sum(pieces[:number])
+                    cols = slice(first, first + width)
+                    nc.scalar.activation(bounded[:, cols], y_banks[4 * half + j][:, cols], ACT.Tanh)
+                    if width == BANK:
+                        place = (slice(None), slice(2 * j, 2 * j + 2), m_cols)
+                        shaped = [tile[:].rearrange("p (i m) -> p i m", i=2) for tile in (result, bounded)]
+                    else:
+                        m0 = HALF * half + first % HALF
+                        place = (slice(None), 2 * j + first // HALF, slice(m0, m0 + width))
+                        shaped = [tile[:, cols] for tile in (result, bounded)]
+                    nc.vector.tensor_tensor(shaped[0], shaped[1], target_sb[place], ALU.subtract)
+                    nc.sync.dma_start(out_rows[place], shaped[0])

@@ -35,12 +35,9 @@ AT_PICKED = 3.5
 AT_W4_LOW = 4
 AT_IDEAL_LOW = 9
 AT_TAB_W1 = 16
-AT_DEALT_S = 17
-AT_DEALT_W = 18
 AT_W_RAW0 = 20
 AT_TAB_S = 24
 AT_TAB_W0 = 30
-AT_W4_UP = 36
 AT_W_RAW1 = 38
 AT_WGS_DEALT = 54
 AT_IDEAL_UP = 70
@@ -126,30 +123,15 @@ def tile_list_zeolite_ring_check_kernel(
 
         wgs_sb = placed("wgs_sb", [P, S], F32, AT_WGS)
         nc.sync.dma_start(wgs_sb[:], wgs)
-        w4_low = placed("w4_low", [P, 2, 2 * (PASS - P)], U8, AT_W4_LOW)
-        nc.sync.dma_start(w4_low[:].bitcast(I32), w4_words_p[:, :, 2 * P : 2 * PASS].bitcast(I32))
-        w4_up = placed("w4_up", [P, 2, 2 * PASS], U8, AT_W4_UP)
-        nc.sync.dma_start(w4_up[:].bitcast(I32), w4_words_p[:, :, 2 * PASS : 2 * H].bitcast(I32))
+        w4_rest = placed("w4_rest", [P, 2, 2 * (H - P)], U8, AT_W4_LOW)
+        nc.sync.dma_start(w4_rest[:].bitcast(I32), w4_words_p[:, :, 2 * P : 2 * H].bitcast(I32))
         ideal_low = placed("ideal_low", [P, 4, M], F32, AT_IDEAL_LOW)
         nc.sync.dma_start(ideal_low[:], ideal[0:PASS, :].rearrange("(c p) m -> p c m", p=P))
-
-        dealt_w = placed("dealt_w", [P, 4, 2, 2 * P], U8, AT_DEALT_W)
-        dealt_s = placed("dealt_s", [P, 4, 2, P], U8, AT_DEALT_S)
-        nc.vector.tensor_copy(
-            dealt_w[:].rearrange("p t a n -> p (t a n)").bitcast(I32).rearrange("p (t ag w) -> p t ag w", t=4, w=4),
-            w4_up[:].rearrange("p a n -> p (a n)").bitcast(I32).rearrange("p (ag t w) -> p t ag w", t=4, w=4),
-        )
-        nc.vector.tensor_copy(
-            dealt_s[:].rearrange("p t a n -> p (t a n)").bitcast(I32).rearrange("p (t a g w) -> p t a g w", t=4, a=2, w=2),
-            w4_s[:, :, PASS:H].bitcast(I32).rearrange("p a (g t w) -> p t a g w", t=4, w=2),
-        )
 
         def stationary(c, a):
             if c == 0:
                 return w4_first[:, a, :], w4_s[:, a, 0:P]
-            if c < 4:
-                return w4_low[:, a, 2 * P * (c - 1) : 2 * P * c], w4_s[:, a, P * c : P * (c + 1)]
-            return dealt_w[:, c - 4, a, :], dealt_s[:, c - 4, a, :]
+            return w4_rest[:, a, 2 * P * (c - 1) : 2 * P * c], w4_s[:, a, P * c : P * (c + 1)]
 
         def first_product(c, j0, width, step, number, dst):
             h_acc = bank("h_acc", number)
@@ -174,13 +156,34 @@ def tile_list_zeolite_ring_check_kernel(
         first_product(0, 0, FIRST, P, 0, h0_first[:])
         first_product(0, FIRST, BANK - FIRST, P, 1, h0_rest[:, 0 : BANK - FIRST])
         first_product(0, BANK, BANK, BANK, 2, h0_rest[:, BANK - FIRST :])
-        h_tiles = {1: sbuf("h1", [P, S], F32), 2: placed("h2", [P, S], F32, AT_TARGET)}
-        for c in range(3, ROW_TILES - 1):
+        h_tiles = dict()
+        for c in range(1, ROW_TILES - 1):
             h_tiles[c] = sbuf("h%d" % c, [P, S], F32)
         h_tiles[7] = placed("h7", [P, S], F32, AT_H7)
-        for c in range(1, ROW_TILES):
+        for c in range(1, 4):
             for part in range(2):
                 first_product(c, BANK * part, BANK, BANK, (2 * c + part + 1) % 4, h_tiles[c][:, BANK * part : BANK * (part + 1)])
+        h_turned = placed("h_turned", [P, S // P, 4, P], F32, AT_TARGET)
+        for block in range(S // P):
+            j_cols = slice(P * block, P * (block + 1))
+            h_acc = bank("h_acc", block % 2)
+            for a in range(2):
+                nc.tensor.matmul_mx(
+                    out=h_acc[:],
+                    lhsT=v_w[a][:, j_cols].bitcast(FP8X4),
+                    lhsT_scale=v_s[:, a, j_cols],
+                    rhs=w4_rest[:, a, 2 * (PASS - P) : 2 * (H - P)].bitcast(FP4X4),
+                    rhs_scale=w4_s[:, a, PASS:H],
+                    start=(a == 0),
+                    stop=(a == 1),
+                )
+            nc.scalar.copy(h_turned[:, block], h_acc[:].rearrange("j (p t) -> j t p", t=4))
+        for t in range(4):
+            for part in range(2):
+                h_back = bank("h_back", 2 + part)
+                for i in range(4):
+                    nc.tensor.transpose(h_back[:, P * i : P * (i + 1)], h_turned[:, 4 * part + i, t, :], ident[:])
+                nc.scalar.copy(h_tiles[4 + t][:, BANK * part : BANK * (part + 1)], h_back[:])
 
         nc.vector.tensor_tensor(pages[0][:].indirect(idx2[:, entries(0, FIRST)]), h0_first[:], wgs_first[:], ALU.mult)
         nc.vector.tensor_tensor(
@@ -191,22 +194,14 @@ def tile_list_zeolite_ring_check_kernel(
         for c in range(4):
             nc.scalar.activation(minus_ideal[:, c, :], ideal_low[:, c, :], ACT.Copy, scale=-1.0)
 
-        def dealt_rows(matrix, t):
-            return matrix[PASS:H, :].rearrange("(g t i) n -> t g i n", t=4, i=8)[t]
-
         w_raw = [placed("w_raw0", [P, 4, N], F32, AT_W_RAW0), placed("w_raw1", [P, 4, N], F32, AT_W_RAW1)]
-        nc.sync.dma_start(w_raw[0][:], w[0:PASS, :].rearrange("(p t) n -> p t n", t=4))
-        for t in range(4):
-            nc.sync.dma_start(w_raw[1][:, t, :], dealt_rows(w, t))
+        for b in range(2):
+            nc.sync.dma_start(w_raw[b][:], w[PASS * b : PASS * (b + 1), :].rearrange("(p t) n -> p t n", t=4))
         ideal_up = placed("ideal_up", [P, 4, M], F32, AT_IDEAL_UP)
-        for t in range(4):
-            nc.sync.dma_start(ideal_up[:, t, :], dealt_rows(ideal, t))
+        nc.sync.dma_start(ideal_up[:], ideal[PASS:H, :].rearrange("(p t) m -> p t m", t=4))
         wgs_dealt = placed("wgs_dealt", [P, 4, S], F32, AT_WGS_DEALT)
-        for q in range(4):
-            for t in range(4):
-                nc.sync.dma_start(
-                    wgs_dealt[32 * q : 32 * (q + 1), t, :], wgs.rearrange("(g t i) j -> t g i j", t=4, i=8)[t]
-                )
+        for q in (0, 2, 1, 3):
+            nc.sync.dma_start(wgs_dealt[32 * q : 32 * (q + 1)], wgs.rearrange("(p t) j -> p t j", t=4))
         target_sb = placed("target_sb", [P, ROW_TILES, M], F32, AT_TARGET)
         nc.sync.dma_start(target_sb[:], target.rearrange("(c p) m -> p c m", p=P))
 

@@ -1,7 +1,6 @@
 from contextlib import ExitStack
 
 import concourse.mybir as mybir
-from concourse.masks import make_identity
 
 K, H, N, T, S, T2, M = 1024, 1024, 1024, 2048, 1024, 2048, 512
 FLOPS = 2 * K * H * S + 2 * H * N * M
@@ -25,6 +24,7 @@ ROW_TILES = H // P
 PAGES = 3
 PER_COLUMN = 16
 ALIGN = 64
+EARLY = 2 * P
 FIRST = 256
 
 Z_BANK = 4
@@ -44,9 +44,8 @@ AT_IDEAL_UP = 70
 AT_TARGET = 78
 AT_W_ROUNDED = 94
 AT_Z0_GROUPED = 110
-AT_LOW_GROUPED = 117
-AT_H7 = 120
-AT_SITE4 = 124
+AT_H7 = 114
+AT_SITE4 = 118
 
 
 def tile_list_zeolite_ring_check_kernel(
@@ -78,7 +77,7 @@ def tile_list_zeolite_ring_check_kernel(
         tab_s = placed("tab_s", [P, T], U8, AT_TAB_S)
         tab_w = [placed("tab_w0", [P, T], I32, AT_TAB_W0), placed("tab_w1", [P, T], I32, AT_TAB_W1)]
         w4_words_p = w4_words.rearrange("a p n -> p a n")
-        w4_first = sbuf("w4_first", [P, 2, 2 * P], U8)
+        w4_first = sbuf("w4_first", [P, 2, 2 * EARLY], U8)
         wgs_first = sbuf("wgs_first", [P, FIRST], F32)
         nc.sync.dma_start(idx[:], offs)
         nc.sync.dma_start(tab_s[96:128, :].bitcast(I32), tab_scales.rearrange("a q n -> q a n").bitcast(I32))
@@ -86,14 +85,14 @@ def tile_list_zeolite_ring_check_kernel(
         nc.sync.dma_start(idx2[:], offs2)
         nc.sync.dma_start(idx3[:], offs3)
         nc.sync.dma_start(tab_w[1][:], tab_words[1].rearrange("p n t -> p (n t)").bitcast(I32))
-        nc.sync.dma_start(w4_first[:].bitcast(I32), w4_words_p[:, :, 0 : 2 * P].bitcast(I32))
+        nc.sync.dma_start(w4_first[:].bitcast(I32), w4_words_p[:, :, 0 : 2 * EARLY].bitcast(I32))
         nc.sync.dma_start(wgs_first[:], wgs[:, 0:FIRST])
         nc.sync.dma_start(idx4[:], offs4)
 
         w4_s = sbuf("w4_s", [P, 2, H], U8)
         v_s = sbuf("v_s", [P, 2, S], U8)
-        nc.gpsimd.memset(tab_s[0:96, :].bitcast(I32), 0)
         nc.gpsimd.memset(w4_s[:].bitcast(I32), 0)
+        nc.gpsimd.memset(tab_s[0:96, :].bitcast(I32), 0)
         nc.vector.memset(v_s[:].bitcast(I32), 0)
         for g in range(4):
             nc.gpsimd.dma_start(
@@ -102,8 +101,8 @@ def tile_list_zeolite_ring_check_kernel(
             )
         pages = [sbuf("page%d" % i, [P, T2], F32) for i in range(PAGES)]
         nc.vector.memset(pages[0][:], 0.0)
-        ident = sbuf("ident", [P, P], F32)
-        make_identity(nc, ident[:])
+        offset = sbuf("offset", [P, P], F32)
+        nc.gpsimd.iota(offset[:], [[1, P]], base=0, channel_multiplier=-1, allow_small_or_imprecise_dtypes=True)
         for i in range(1, PAGES):
             nc.gpsimd.memset(pages[i][:], 0.0)
 
@@ -123,15 +122,14 @@ def tile_list_zeolite_ring_check_kernel(
 
         wgs_sb = placed("wgs_sb", [P, S], F32, AT_WGS)
         nc.sync.dma_start(wgs_sb[:], wgs)
-        w4_rest = placed("w4_rest", [P, 2, 2 * (H - P)], U8, AT_W4_LOW)
-        nc.sync.dma_start(w4_rest[:].bitcast(I32), w4_words_p[:, :, 2 * P : 2 * H].bitcast(I32))
+        w4_rest = placed("w4_rest", [P, 2, 2 * (H - EARLY)], U8, AT_W4_LOW)
+        nc.sync.dma_start(w4_rest[:].bitcast(I32), w4_words_p[:, :, 2 * EARLY : 2 * H].bitcast(I32))
         ideal_low = placed("ideal_low", [P, 4, M], F32, AT_IDEAL_LOW)
         nc.sync.dma_start(ideal_low[:], ideal[0:PASS, :].rearrange("(c p) m -> p c m", p=P))
 
         def stationary(c, a):
-            if c == 0:
-                return w4_first[:, a, :], w4_s[:, a, 0:P]
-            return w4_rest[:, a, 2 * P * (c - 1) : 2 * P * c], w4_s[:, a, P * c : P * (c + 1)]
+            words, first = (w4_first, P * c) if P * c < EARLY else (w4_rest, P * c - EARLY)
+            return words[:, a, 2 * first : 2 * (first + P)], w4_s[:, a, P * c : P * (c + 1)]
 
         def first_product(c, j0, width, step, number, dst):
             h_acc = bank("h_acc", number)
@@ -151,7 +149,7 @@ def tile_list_zeolite_ring_check_kernel(
                     )
             nc.scalar.copy(dst, h_acc[:, 0:width])
 
-        h0_first = placed("h0_first", [P, FIRST], F32, AT_W_RAW1)
+        h0_first = placed("h0_first", [P, FIRST], F32, AT_W_RAW1 - 0.5)
         h0_rest = placed("h0_rest", [P, S - FIRST], F32, AT_IDEAL_UP - 1.5)
         first_product(0, 0, FIRST, P, 0, h0_first[:])
         first_product(0, FIRST, BANK - FIRST, P, 1, h0_rest[:, 0 : BANK - FIRST])
@@ -163,6 +161,10 @@ def tile_list_zeolite_ring_check_kernel(
         for c in range(1, 4):
             for part in range(2):
                 first_product(c, BANK * part, BANK, BANK, (2 * c + part + 1) % 4, h_tiles[c][:, BANK * part : BANK * (part + 1)])
+        distance = placed("distance", [P, P], F32, AT_W_RAW1 - 0.5)
+        nc.scalar.activation(distance[:], offset[:], ACT.Abs)
+        ident = sbuf("ident", [P, P], F32)
+        nc.scalar.activation(ident[:], distance[:], ACT.Relu, scale=-1.0, bias=1.0)
         h_turned = placed("h_turned", [P, S // P, 4, P], F32, AT_TARGET)
         for block in range(S // P):
             j_cols = slice(P * block, P * (block + 1))
@@ -172,7 +174,7 @@ def tile_list_zeolite_ring_check_kernel(
                     out=h_acc[:],
                     lhsT=v_w[a][:, j_cols].bitcast(FP8X4),
                     lhsT_scale=v_s[:, a, j_cols],
-                    rhs=w4_rest[:, a, 2 * (PASS - P) : 2 * (H - P)].bitcast(FP4X4),
+                    rhs=w4_rest[:, a, 2 * (PASS - EARLY) : 2 * (H - EARLY)].bitcast(FP4X4),
                     rhs_scale=w4_s[:, a, PASS:H],
                     start=(a == 0),
                     stop=(a == 1),
@@ -309,7 +311,7 @@ def tile_list_zeolite_ring_check_kernel(
         second_product(0, 0, z0_codes[:], z0_scales[:])
 
         shared = placed("z67_high", [P, 2 * HALF], F32, AT_IDEAL_UP + 6)
-        low_tile = placed("low_grouped", [P, 4 * HALF], BF16, AT_LOW_GROUPED)
+        low_tile = sbuf("low_grouped", [P, 4 * HALF], BF16)
         low_grouped = low_tile[:]
         high_tile = sbuf("high_grouped", [P, 4 * HALF], BF16)
         grouped = (low_grouped, high_tile[:])
@@ -330,9 +332,9 @@ def tile_list_zeolite_ring_check_kernel(
         read_facing(6, HALF, HALF, site6[:, HALF:M], shared[:, 0:HALF])
         read_facing(7, HALF, HALF, site7[:, HALF:M], shared[:, HALF : 2 * HALF])
         low_codes, low_scales = quantise("low", low_grouped, HALF)
-        w_quantised[1, 1] = quantise("w11", w1_rounded[1][:].rearrange("p n t -> p (n t)"), BANK, AT_LOW_GROUPED - 1)
+        w_quantised[1, 1] = quantise("w11", w1_rounded[1][:].rearrange("p n t -> p (n t)"), BANK, AT_H7 + 1)
         second_product(1, 0, low_codes[:], low_scales[:])
-        z0_high = quantise("z0_high", z0_grouped[1][:].rearrange("p m t -> p (m t)"), HALF, AT_LOW_GROUPED + 1)
+        z0_high = quantise("z0_high", z0_grouped[1][:].rearrange("p m t -> p (m t)"), HALF, AT_H7 + 3)
         weave(nc.scalar.copy, 1, 1, shared[:, 0 : 2 * HALF].rearrange("p (e m) -> p e m", e=2))
         high_codes, high_scales = quantise("high", high_tile[:], HALF)
         for j in range(4):

@@ -94,10 +94,9 @@ def tile_list_zeolite_ring_check_kernel(
         nc.gpsimd.memset(w4_s[:].bitcast(I32), 0)
         nc.gpsimd.memset(tab_s[0:96, :].bitcast(I32), 0)
         nc.vector.memset(v_s[:].bitcast(I32), 0)
-        for g in range(4):
+        for r in range(4):
             nc.gpsimd.dma_start(
-                w4_s[32 * g : 32 * g + 4, :, :].bitcast(I32),
-                w4_scales[:, 4 * g : 4 * g + 4, :].rearrange("a r n -> r a n").bitcast(I32),
+                w4_s[r:128:32, :, :].bitcast(I32), w4_scales.rearrange("a (g r) n -> r g a n", r=4)[r].bitcast(I32)
             )
         pages = [sbuf("page%d" % i, [P, T2], F32) for i in range(PAGES)]
         nc.vector.memset(pages[0][:], 0.0)
@@ -108,7 +107,7 @@ def tile_list_zeolite_ring_check_kernel(
 
         picked_s = placed("picked_s", [P, S], U8, AT_PICKED)
         nc.vector.tensor_copy(picked_s[:], tab_s[:].indirect(idx[:]))
-        for g in range(4):
+        for g in (0, 2, 1, 3):
             nc.scalar.dma_start(
                 v_s[32 * g : 32 * g + 4, :, :].bitcast(I32),
                 picked_s[96 + 8 * g : 96 + 8 * g + 8, :].bitcast(I32),

@@ -92,7 +92,7 @@ def tile_list_zeolite_ring_check_kernel(
         w4_s = sbuf("w4_s", [P, 2, H], U8)
         v_s = sbuf("v_s", [P, 2, S], U8)
         nc.gpsimd.memset(w4_s[:].bitcast(I32), 0)
-        nc.gpsimd.memset(tab_s[0:96, :].bitcast(I32), 0)
+        nc.vector.memset(tab_s[0:96, :].bitcast(I32), 0)
         nc.vector.memset(v_s[:].bitcast(I32), 0)
         for r in range(4):
             nc.gpsimd.dma_start(

@@ -78,7 +78,7 @@ def tile_list_zeolite_ring_check_kernel(
         tab_w = [placed("tab_w0", [P, T], I32, AT_TAB_W0), placed("tab_w1", [P, T], I32, AT_TAB_W1)]
         w4_words_p = w4_words.rearrange("a p n -> p a n")
         w4_first = sbuf("w4_first", [P, 2, 2 * EARLY], U8)
-        wgs_first = sbuf("wgs_first", [P, FIRST], F32)
+        wgs_first = placed("wgs_first", [P, FIRST], F32, AT_TAB_S)
         nc.sync.dma_start(idx[:], offs)
         nc.sync.dma_start(tab_s[96:128, :].bitcast(I32), tab_scales.rearrange("a q n -> q a n").bitcast(I32))
         nc.sync.dma_start(tab_w[0][:], tab_words[0].rearrange("p n t -> p (n t)").bitcast(I32))
@@ -86,22 +86,22 @@ def tile_list_zeolite_ring_check_kernel(
         nc.sync.dma_start(idx3[:], offs3)
         nc.sync.dma_start(tab_w[1][:], tab_words[1].rearrange("p n t -> p (n t)").bitcast(I32))
         nc.sync.dma_start(w4_first[:].bitcast(I32), w4_words_p[:, :, 0 : 2 * EARLY].bitcast(I32))
-        nc.sync.dma_start(wgs_first[:], wgs[:, 0:FIRST])
         nc.sync.dma_start(idx4[:], offs4)
 
-        w4_s = sbuf("w4_s", [P, 2, H], U8)
+        w4_scale_rows = w4_scales.rearrange("a (g r) n -> r g a n", r=4)
+        w4_s_first = sbuf("w4_s_first", [P, 2, EARLY], U8)
         v_s = sbuf("v_s", [P, 2, S], U8)
-        nc.gpsimd.memset(w4_s[:].bitcast(I32), 0)
+        nc.gpsimd.memset(w4_s_first[:].bitcast(I32), 0)
         nc.vector.memset(tab_s[0:96, :].bitcast(I32), 0)
         nc.vector.memset(v_s[:].bitcast(I32), 0)
         for r in range(4):
-            nc.gpsimd.dma_start(
-                w4_s[r:128:32, :, :].bitcast(I32), w4_scales.rearrange("a (g r) n -> r g a n", r=4)[r].bitcast(I32)
-            )
+            nc.gpsimd.dma_start(w4_s_first[r:128:32, :, :].bitcast(I32), w4_scale_rows[r][:, :, 0:EARLY].bitcast(I32))
         pages = [sbuf("page%d" % i, [P, T2], F32) for i in range(PAGES)]
         nc.vector.memset(pages[0][:], 0.0)
         offset = sbuf("offset", [P, P], F32)
         nc.gpsimd.iota(offset[:], [[1, P]], base=0, channel_multiplier=-1, allow_small_or_imprecise_dtypes=True)
+        w4_s_rest = sbuf("w4_s_rest", [P, 2, H - EARLY], U8)
+        nc.gpsimd.memset(w4_s_rest[:].bitcast(I32), 0)
         for i in range(1, PAGES):
             nc.gpsimd.memset(pages[i][:], 0.0)
 
@@ -112,6 +112,9 @@ def tile_list_zeolite_ring_check_kernel(
                 v_s[32 * g : 32 * g + 4, :, :].bitcast(I32),
                 picked_s[96 + 8 * g : 96 + 8 * g + 8, :].bitcast(I32),
             )
+        nc.scalar.dma_start(wgs_first[:], wgs[:, 0:FIRST])
+        for r in range(4):
+            nc.sync.dma_start(w4_s_rest[r:128:32, :, :].bitcast(I32), w4_scale_rows[r][:, :, EARLY:H].bitcast(I32))
         v_w = [sbuf("v_w%d" % a, [P, S], U32) for a in range(2)]
         nc.vector.tensor_copy(v_w[0][:], tab_w[0][:].bitcast(U32).indirect(idx[:]))
         for first, count in ((0, FIRST), (FIRST, S - FIRST)):
@@ -127,8 +130,8 @@ def tile_list_zeolite_ring_check_kernel(
         nc.sync.dma_start(ideal_low[:], ideal[0:PASS, :].rearrange("(c p) m -> p c m", p=P))
 
         def stationary(c, a):
-            words, first = (w4_first, P * c) if P * c < EARLY else (w4_rest, P * c - EARLY)
-            return words[:, a, 2 * first : 2 * (first + P)], w4_s[:, a, P * c : P * (c + 1)]
+            words, scales, first = (w4_first, w4_s_first, P * c) if P * c < EARLY else (w4_rest, w4_s_rest, P * c - EARLY)
+            return words[:, a, 2 * first : 2 * (first + P)], scales[:, a, first : first + P]
 
         def first_product(c, j0, width, step, number, dst):
             h_acc = bank("h_acc", number)
@@ -150,9 +153,22 @@ def tile_list_zeolite_ring_check_kernel(
 
         h0_first = placed("h0_first", [P, FIRST], F32, AT_W_RAW1 - 0.5)
         h0_rest = placed("h0_rest", [P, S - FIRST], F32, AT_IDEAL_UP - 1.5)
-        first_product(0, 0, FIRST, P, 0, h0_first[:])
-        first_product(0, FIRST, BANK - FIRST, P, 1, h0_rest[:, 0 : BANK - FIRST])
-        first_product(0, BANK, BANK, BANK, 2, h0_rest[:, BANK - FIRST :])
+        first_product(0, 0, FIRST, FIRST, 0, h0_first[:])
+        rest = ((FIRST, BANK, bank("h_acc", 1)), (FIRST + BANK, S - FIRST - BANK, bank("h_acc", 2)))
+        for a in range(2):
+            words, scales = stationary(0, a)
+            for j0, width, h_acc in rest:
+                nc.tensor.matmul_mx(
+                    out=h_acc[:, 0:width],
+                    lhsT=words.bitcast(FP4X4),
+                    lhsT_scale=scales,
+                    rhs=v_w[a][:, j0 : j0 + width].bitcast(FP8X4),
+                    rhs_scale=v_s[:, a, j0 : j0 + width],
+                    start=(a == 0),
+                    stop=(a == 1),
+                )
+        for j0, width, h_acc in rest:
+            nc.scalar.copy(h0_rest[:, j0 - FIRST : j0 - FIRST + width], h_acc[:, 0:width])
         h_tiles = dict()
         for c in range(1, ROW_TILES - 1):
             h_tiles[c] = sbuf("h%d" % c, [P, S], F32)
@@ -174,7 +190,7 @@ def tile_list_zeolite_ring_check_kernel(
                     lhsT=v_w[a][:, j_cols].bitcast(FP8X4),
                     lhsT_scale=v_s[:, a, j_cols],
                     rhs=w4_rest[:, a, 2 * (PASS - EARLY) : 2 * (H - EARLY)].bitcast(FP4X4),
-                    rhs_scale=w4_s[:, a, PASS:H],
+                    rhs_scale=w4_s_rest[:, a, PASS - EARLY : H - EARLY],
                     start=(a == 0),
                     stop=(a == 1),
                 )

@@ -88,9 +88,22 @@ def tile_list_zeolite_ring_check_kernel(
         nc.sync.dma_start(w4_first[:].bitcast(I32), w4_words_p[:, :, 0 : 2 * EARLY].bitcast(I32))
         nc.sync.dma_start(idx4[:], offs4)
 
+        offset = sbuf("offset", [P, P], F32)
+        nc.gpsimd.iota(offset[:], [[1, P]], base=0, channel_multiplier=-1, allow_small_or_imprecise_dtypes=True)
+        distance = sbuf("distance", [P, P], F32)
+        nc.scalar.activation(distance[:], offset[:], ACT.Abs)
+        ident = sbuf("ident", [P, P], F32)
+        nc.scalar.activation(ident[:], distance[:], ACT.Relu, scale=-1.0, bias=1.0)
         w4_scale_rows = w4_scales.rearrange("a (g r) n -> r g a n", r=4)
         w4_s_first = sbuf("w4_s_first", [P, 2, EARLY], U8)
-        v_s = sbuf("v_s", [P, 2, S], U8)
+        v_s = sbuf("v_s", [P, 2 * S], U8)
+        v_s_first = v_s[:, 0 : 2 * FIRST].rearrange("p (a j) -> p a j", a=2)
+        v_s_rest = v_s[:, 2 * FIRST : 2 * S].rearrange("p (a j) -> p a j", a=2)
+
+        def v_scales(a, j0, width):
+            plane, first = (v_s_first, j0) if j0 < FIRST else (v_s_rest, j0 - FIRST)
+            return plane[:, a, first : first + width]
+
         nc.gpsimd.memset(w4_s_first[:].bitcast(I32), 0)
         nc.vector.memset(tab_s[0:96, :].bitcast(I32), 0)
         nc.vector.memset(v_s[:].bitcast(I32), 0)
@@ -98,21 +111,23 @@ def tile_list_zeolite_ring_check_kernel(
             nc.gpsimd.dma_start(w4_s_first[r:128:32, :, :].bitcast(I32), w4_scale_rows[r][:, :, 0:EARLY].bitcast(I32))
         pages = [sbuf("page%d" % i, [P, T2], F32) for i in range(PAGES)]
         nc.vector.memset(pages[0][:], 0.0)
-        offset = sbuf("offset", [P, P], F32)
-        nc.gpsimd.iota(offset[:], [[1, P]], base=0, channel_multiplier=-1, allow_small_or_imprecise_dtypes=True)
         w4_s_rest = sbuf("w4_s_rest", [P, 2, H - EARLY], U8)
         nc.gpsimd.memset(w4_s_rest[:].bitcast(I32), 0)
         for i in range(1, PAGES):
             nc.gpsimd.memset(pages[i][:], 0.0)
 
-        picked_s = placed("picked_s", [P, S], U8, AT_PICKED)
-        nc.vector.tensor_copy(picked_s[:], tab_s[:].indirect(idx[:]))
-        for g in (0, 2, 1, 3):
-            nc.scalar.dma_start(
-                v_s[32 * g : 32 * g + 4, :, :].bitcast(I32),
-                picked_s[96 + 8 * g : 96 + 8 * g + 8, :].bitcast(I32),
-            )
-        nc.scalar.dma_start(wgs_first[:], wgs[:, 0:FIRST])
+        picked_s = placed("picked_s", [P, S - FIRST], U8, AT_W4_LOW)
+        picked_first = placed("picked_first", [P, FIRST], U8, AT_PICKED)
+        for picked, plane, first in ((picked_first, v_s_first, 0), (picked_s, v_s_rest, FIRST)):
+            count = picked.shape[1]
+            nc.vector.tensor_copy(picked[:], tab_s[:].indirect(idx[:, entries(first, count)]))
+            if first > 0:
+                nc.scalar.dma_start(wgs_first[:], wgs[:, 0:FIRST])
+            for g in (0, 2, 1, 3):
+                (nc.scalar if first == 0 else nc.sync).dma_start(
+                    plane[32 * g : 32 * g + 4, :, :].bitcast(I32),
+                    picked[96 + 8 * g : 96 + 8 * g + 8, :].bitcast(I32),
+                )
         for r in range(4):
             nc.sync.dma_start(w4_s_rest[r:128:32, :, :].bitcast(I32), w4_scale_rows[r][:, :, EARLY:H].bitcast(I32))
         v_w = [sbuf("v_w%d" % a, [P, S], U32) for a in range(2)]
@@ -133,53 +148,45 @@ def tile_list_zeolite_ring_check_kernel(
             words, scales, first = (w4_first, w4_s_first, P * c) if P * c < EARLY else (w4_rest, w4_s_rest, P * c - EARLY)
             return words[:, a, 2 * first : 2 * (first + P)], scales[:, a, first : first + P]
 
-        def first_product(c, j0, width, step, number, dst):
-            h_acc = bank("h_acc", number)
-            pieces = width // step
+        def first_product(c, groups):
+            accs = [bank("h_acc", number) for number, dst, pieces in groups]
             for a in range(2):
                 words, scales = stationary(c, a)
-                for i in range(pieces):
-                    j_cols = slice(j0 + step * i, j0 + step * (i + 1))
-                    nc.tensor.matmul_mx(
-                        out=h_acc[:, step * i : step * (i + 1)],
-                        lhsT=words.bitcast(FP4X4),
-                        lhsT_scale=scales,
-                        rhs=v_w[a][:, j_cols].bitcast(FP8X4),
-                        rhs_scale=v_s[:, a, j_cols],
-                        start=(a == 0 and i == 0),
-                        stop=(a == 1 and i == pieces - 1),
-                    )
-            nc.scalar.copy(dst, h_acc[:, 0:width])
+                for h_acc, (number, dst, pieces) in zip(accs, groups):
+                    for i, (j0, width) in enumerate(pieces):
+                        at = j0 - pieces[0][0]
+                        nc.tensor.matmul_mx(
+                            out=h_acc[:, at : at + width],
+                            lhsT=words.bitcast(FP4X4),
+                            lhsT_scale=scales,
+                            rhs=v_w[a][:, j0 : j0 + width].bitcast(FP8X4),
+                            rhs_scale=v_scales(a, j0, width),
+                            start=(a == 0 and i == 0),
+                            stop=(a == 1 and i == len(pieces) - 1),
+                        )
+            for h_acc, (number, dst, pieces) in zip(accs, groups):
+                nc.scalar.copy(dst, h_acc[:, 0 : sum(width for j0, width in pieces)])
 
         h0_first = placed("h0_first", [P, FIRST], F32, AT_W_RAW1 - 0.5)
-        h0_rest = placed("h0_rest", [P, S - FIRST], F32, AT_IDEAL_UP - 1.5)
-        first_product(0, 0, FIRST, FIRST, 0, h0_first[:])
-        rest = ((FIRST, BANK, bank("h_acc", 1)), (FIRST + BANK, S - FIRST - BANK, bank("h_acc", 2)))
-        for a in range(2):
-            words, scales = stationary(0, a)
-            for j0, width, h_acc in rest:
-                nc.tensor.matmul_mx(
-                    out=h_acc[:, 0:width],
-                    lhsT=words.bitcast(FP4X4),
-                    lhsT_scale=scales,
-                    rhs=v_w[a][:, j0 : j0 + width].bitcast(FP8X4),
-                    rhs_scale=v_s[:, a, j0 : j0 + width],
-                    start=(a == 0),
-                    stop=(a == 1),
-                )
-        for j0, width, h_acc in rest:
-            nc.scalar.copy(h0_rest[:, j0 - FIRST : j0 - FIRST + width], h_acc[:, 0:width])
+        h_first = [h0_first, sbuf("h1_first", [P, FIRST], F32)]
+        h_rest = [placed("h0_rest", [P, S - FIRST], F32, AT_IDEAL_UP - 1.5), sbuf("h1_rest", [P, S - FIRST], F32)]
+        for c in range(2):
+            first_product(c, [(c, h_first[c][:], [(0, FIRST)])])
+        for c in range(2):
+            first_product(
+                c,
+                [
+                    (2 - 2 * c, h_rest[c][:, 0:BANK], [(FIRST, BANK)]),
+                    (3 - 2 * c, h_rest[c][:, BANK:], [(FIRST + BANK, S - FIRST - BANK)]),
+                ],
+            )
         h_tiles = dict()
-        for c in range(1, ROW_TILES - 1):
+        for c in range(2, ROW_TILES - 1):
             h_tiles[c] = sbuf("h%d" % c, [P, S], F32)
         h_tiles[7] = placed("h7", [P, S], F32, AT_H7)
-        for c in range(1, 4):
-            for part in range(2):
-                first_product(c, BANK * part, BANK, BANK, (2 * c + part + 1) % 4, h_tiles[c][:, BANK * part : BANK * (part + 1)])
-        distance = placed("distance", [P, P], F32, AT_W_RAW1 - 0.5)
-        nc.scalar.activation(distance[:], offset[:], ACT.Abs)
-        ident = sbuf("ident", [P, P], F32)
-        nc.scalar.activation(ident[:], distance[:], ACT.Relu, scale=-1.0, bias=1.0)
+        for c in range(2, 4):
+            first_product(c, [(2, h_tiles[c][:, 0:BANK], [(0, FIRST), (FIRST, BANK - FIRST)])])
+            first_product(c, [(3, h_tiles[c][:, BANK:], [(BANK, BANK)])])
         h_turned = placed("h_turned", [P, S // P, 4, P], F32, AT_TARGET)
         for block in range(S // P):
             j_cols = slice(P * block, P * (block + 1))
@@ -188,7 +195,7 @@ def tile_list_zeolite_ring_check_kernel(
                 nc.tensor.matmul_mx(
                     out=h_acc[:],
                     lhsT=v_w[a][:, j_cols].bitcast(FP8X4),
-                    lhsT_scale=v_s[:, a, j_cols],
+                    lhsT_scale=v_scales(a, P * block, P),
                     rhs=w4_rest[:, a, 2 * (PASS - EARLY) : 2 * (H - EARLY)].bitcast(FP4X4),
                     rhs_scale=w4_s_rest[:, a, PASS - EARLY : H - EARLY],
                     start=(a == 0),
@@ -202,10 +209,12 @@ def tile_list_zeolite_ring_check_kernel(
                     nc.tensor.transpose(h_back[:, P * i : P * (i + 1)], h_turned[:, 4 * part + i, t, :], ident[:])
                 nc.scalar.copy(h_tiles[4 + t][:, BANK * part : BANK * (part + 1)], h_back[:])
 
-        nc.vector.tensor_tensor(pages[0][:].indirect(idx2[:, entries(0, FIRST)]), h0_first[:], wgs_first[:], ALU.mult)
-        nc.vector.tensor_tensor(
-            pages[0][:].indirect(idx2[:, entries(FIRST, S - FIRST)]), h0_rest[:], wgs_sb[:, FIRST:S], ALU.mult
-        )
+        for c in range(2):
+            nc.vector.tensor_tensor(pages[c][:].indirect(idx2[:, entries(0, FIRST)]), h_first[c][:], wgs_first[:], ALU.mult)
+        for c in range(2):
+            nc.vector.tensor_tensor(
+                pages[c][:].indirect(idx2[:, entries(FIRST, S - FIRST)]), h_rest[c][:], wgs_sb[:, FIRST:S], ALU.mult
+            )
 
         minus_ideal = sbuf("minus_ideal", [P, 4, M], F32)
         for c in range(4):
@@ -248,7 +257,8 @@ def tile_list_zeolite_ring_check_kernel(
 
         z0_rows = sbuf("z0_rows", [P, M // P, 2, P, 2], BF16)
         for c in range(4):
-            scatter(c + 1)
+            if c > 0:
+                scatter(c + 1)
             site = sbuf("site", [P, M], F32, bufs=4)
             facing = sbuf("facing", [P, M], F32, bufs=4)
             nc.vector.tensor_copy(site[:], pages[c % PAGES][:].indirect(idx3[:]))

@@ -46,6 +46,7 @@ AT_W_ROUNDED = 94
 AT_Z0_GROUPED = 110
 AT_H7 = 114
 AT_SITE4 = 118
+AT_PAGE2 = 120
 
 
 def tile_list_zeolite_ring_check_kernel(
@@ -109,12 +110,11 @@ def tile_list_zeolite_ring_check_kernel(
         nc.vector.memset(v_s[:].bitcast(I32), 0)
         for r in range(4):
             nc.gpsimd.dma_start(w4_s_first[r:128:32, :, :].bitcast(I32), w4_scale_rows[r][:, :, 0:EARLY].bitcast(I32))
-        pages = [sbuf("page%d" % i, [P, T2], F32) for i in range(PAGES)]
+        pages = [sbuf("page0", [P, T2], F32), sbuf("page1", [P, T2], F32), placed("page2", [P, T2], F32, AT_PAGE2)]
         nc.vector.memset(pages[0][:], 0.0)
         w4_s_rest = sbuf("w4_s_rest", [P, 2, H - EARLY], U8)
         nc.gpsimd.memset(w4_s_rest[:].bitcast(I32), 0)
-        for i in range(1, PAGES):
-            nc.gpsimd.memset(pages[i][:], 0.0)
+        nc.gpsimd.memset(pages[1][:], 0.0)
 
         picked_s = placed("picked_s", [P, S - FIRST], U8, AT_W4_LOW)
         picked_first = placed("picked_first", [P, FIRST], U8, AT_PICKED)
@@ -169,7 +169,7 @@ def tile_list_zeolite_ring_check_kernel(
 
         h0_first = placed("h0_first", [P, FIRST], F32, AT_W_RAW1 - 0.5)
         h_first = [h0_first, sbuf("h1_first", [P, FIRST], F32)]
-        h_rest = [placed("h0_rest", [P, S - FIRST], F32, AT_IDEAL_UP - 1.5), sbuf("h1_rest", [P, S - FIRST], F32)]
+        h_rest = [placed("h0_rest", [P, S - FIRST], F32, AT_IDEAL_UP - 1.5), placed("h1_rest", [P, S - FIRST], F32, AT_PAGE2)]
         for c in range(2):
             first_product(c, [(c, h_first[c][:], [(0, FIRST)])])
         for c in range(2):
@@ -216,6 +216,7 @@ def tile_list_zeolite_ring_check_kernel(
                 pages[c][:].indirect(idx2[:, entries(FIRST, S - FIRST)]), h_rest[c][:], wgs_sb[:, FIRST:S], ALU.mult
             )
 
+        nc.gpsimd.memset(pages[2][:], 0.0)
         minus_ideal = sbuf("minus_ideal", [P, 4, M], F32)
         for c in range(4):
             nc.scalar.activation(minus_ideal[:, c, :], ideal_low[:, c, :], ACT.Copy, scale=-1.0)

@@ -82,9 +82,9 @@ def tile_list_zeolite_ring_check_kernel(
         wgs_first = placed("wgs_first", [P, FIRST], F32, AT_TAB_S)
         nc.sync.dma_start(idx[:], offs)
         nc.sync.dma_start(tab_s[96:128, :].bitcast(I32), tab_scales.rearrange("a q n -> q a n").bitcast(I32))
-        nc.sync.dma_start(tab_w[0][:], tab_words[0].rearrange("p n t -> p (n t)").bitcast(I32))
         nc.sync.dma_start(idx2[:], offs2)
         nc.sync.dma_start(idx3[:], offs3)
+        nc.sync.dma_start(tab_w[0][:], tab_words[0].rearrange("p n t -> p (n t)").bitcast(I32))
         nc.sync.dma_start(tab_w[1][:], tab_words[1].rearrange("p n t -> p (n t)").bitcast(I32))
         nc.sync.dma_start(w4_first[:].bitcast(I32), w4_words_p[:, :, 0 : 2 * EARLY].bitcast(I32))
         nc.sync.dma_start(idx4[:], offs4)

@@ -173,13 +173,8 @@ def tile_list_zeolite_ring_check_kernel(
         for c in range(2):
             first_product(c, [(c, h_first[c][:], [(0, FIRST)])])
         for c in range(2):
-            first_product(
-                c,
-                [
-                    (2 - 2 * c, h_rest[c][:, 0:BANK], [(FIRST, BANK)]),
-                    (3 - 2 * c, h_rest[c][:, BANK:], [(FIRST + BANK, S - FIRST - BANK)]),
-                ],
-            )
+            first_product(c, [(2 - 2 * c, h_rest[c][:, 0:BANK], [(FIRST, BANK)])])
+            first_product(c, [(3 - 2 * c, h_rest[c][:, BANK:], [(FIRST + BANK, S - FIRST - BANK)])])
         h_tiles = dict()
         for c in range(2, ROW_TILES - 1):
             h_tiles[c] = sbuf("h%d" % c, [P, S], F32)

@@ -21,7 +21,8 @@ BANK = 512
 PASS = 512
 HALF = M // 2
 ROW_TILES = H // P
-PAGES = 3
+PAGE_OF = (0, 1, 2, 0, 1, 3, 2, 0)
+QUARTER = M // 4
 PER_COLUMN = 16
 ALIGN = 64
 EARLY = 2 * P
@@ -45,8 +46,22 @@ AT_TARGET = 78
 AT_W_ROUNDED = 94
 AT_Z0_GROUPED = 110
 AT_H7 = 114
-AT_SITE4 = 118
 AT_PAGE2 = 120
+AT_H5 = 128
+AT_H6 = 132
+AT_PAGE3 = AT_WGS
+AT_SITE_LOW = AT_IDEAL_LOW
+AT_Z45_LOW = 12
+AT_Z67_LOW = 14
+AT_SITE7_LOW = 16
+AT_LOW_GROUPED = 17
+AT_LAST_GROUPED = 19
+AT_TARGET_TURNED = AT_W_RAW0
+AT_BOUNDED_LOW = 28
+AT_RESULT_LOW = AT_W_RAW1
+AT_BOUNDED_HIGH = 46
+AT_RESULT_HIGH = 54
+AT_Z_HIGH = 62
 
 
 def tile_list_zeolite_ring_check_kernel(
@@ -110,7 +125,8 @@ def tile_list_zeolite_ring_check_kernel(
         nc.vector.memset(v_s[:].bitcast(I32), 0)
         for r in range(4):
             nc.gpsimd.dma_start(w4_s_first[r:128:32, :, :].bitcast(I32), w4_scale_rows[r][:, :, 0:EARLY].bitcast(I32))
-        pages = [sbuf("page0", [P, T2], F32), sbuf("page1", [P, T2], F32), placed("page2", [P, T2], F32, AT_PAGE2)]
+        pages = [sbuf("page0", [P, T2], F32), sbuf("page1", [P, T2], F32)]
+        pages = pages + [placed("page2", [P, T2], F32, AT_PAGE2), placed("page3", [P, T2], F32, AT_PAGE3)]
         nc.vector.memset(pages[0][:], 0.0)
         w4_s_rest = sbuf("w4_s_rest", [P, 2, H - EARLY], U8)
         nc.gpsimd.memset(w4_s_rest[:].bitcast(I32), 0)
@@ -176,9 +192,10 @@ def tile_list_zeolite_ring_check_kernel(
             first_product(c, [(2 - 2 * c, h_rest[c][:, 0:BANK], [(FIRST, BANK)])])
             first_product(c, [(3 - 2 * c, h_rest[c][:, BANK:], [(FIRST + BANK, S - FIRST - BANK)])])
         h_tiles = dict()
-        for c in range(2, ROW_TILES - 1):
+        for c in range(2, 5):
             h_tiles[c] = sbuf("h%d" % c, [P, S], F32)
-        h_tiles[7] = placed("h7", [P, S], F32, AT_H7)
+        for c, kib in ((5, AT_H5), (6, AT_H6), (7, AT_H7)):
+            h_tiles[c] = placed("h%d" % c, [P, S], F32, kib)
         for c in range(2, 4):
             first_product(c, [(2, h_tiles[c][:, 0:BANK], [(0, FIRST), (FIRST, BANK - FIRST)])])
             first_product(c, [(3, h_tiles[c][:, BANK:], [(BANK, BANK)])])
@@ -227,38 +244,50 @@ def tile_list_zeolite_ring_check_kernel(
         target_sb = placed("target_sb", [P, ROW_TILES, M], F32, AT_TARGET)
         nc.sync.dma_start(target_sb[:], target.rearrange("(c p) m -> p c m", p=P))
 
-        w0_rounded = placed("w0_rounded", [P, N, 4], BF16, AT_W_ROUNDED)
-        w1_rounded = [placed("w1_rounded%d" % side, [P, BANK, 4], BF16, AT_W_ROUNDED + 8 + 4 * side) for side in range(2)]
+        w_rounded = dict()
         for b in range(2):
             for side in range(2):
-                n_cols = slice(BANK * side, BANK * (side + 1))
-                rounded = w0_rounded[:, n_cols, :] if b == 0 else w1_rounded[side][:]
+                w_rounded[b, side] = placed("w_rounded%d%d" % (b, side), [P, BANK, 4], BF16, AT_W_ROUNDED + 8 * b + 4 * side)
                 nc.scalar.copy(
-                    rounded.rearrange("p (c i) t -> p c t i", i=4),
-                    w_raw[b][:, :, n_cols].rearrange("p t (c i) -> p c t i", i=4),
+                    w_rounded[b, side][:].rearrange("p (c i) t -> p c t i", i=4),
+                    w_raw[b][:, :, BANK * side : BANK * (side + 1)].rearrange("p t (c i) -> p c t i", i=4),
                 )
 
-        def quantise(name, grouped, width, kib=None):
-            if kib is None:
-                codes = sbuf(name + "_codes", [P, width], U32)
-            else:
-                codes = placed(name + "_codes", [P, width], U32, kib)
-            scales = sbuf(name + "_scales", [P, width], U8)
-            nc.vector.quantize_mx(out=codes[:].bitcast(FP8X4), scales=scales[:], in_=grouped)
+        def quantise(name, grouped, kib=None):
+            width = grouped.shape[1]
+            codes = sbuf(name + "_codes", [P, width], U32)
+            scales = sbuf(name + "_scales", [P, width], U8) if kib is None else placed(name + "_scales", [P, width], U8, kib)
+            nc.vector.quantize_mx(out=codes[:].bitcast(FP8X4), scales=scales[:], in_=grouped.rearrange("p n t -> p (n t)"))
             return codes, scales
+
+        def multiply(acc, stationary_side, moving_side, start, stop):
+            nc.tensor.matmul_mx(
+                out=acc,
+                lhsT=stationary_side[0].bitcast(FP8X4),
+                lhsT_scale=stationary_side[1],
+                rhs=moving_side[0].bitcast(FP8X4),
+                rhs_scale=moving_side[1],
+                start=start,
+                stop=stop,
+            )
+
+        def columns(quantised, first, count):
+            return quantised[0][:, first : first + count], quantised[1][:, first : first + count]
 
         def scatter(c):
             weights = wgs_sb[:] if c < 4 else wgs_dealt[:, c - 4, :]
-            nc.vector.tensor_tensor(pages[c % PAGES][:].indirect(idx2[:]), h_tiles[c][:], weights, ALU.mult)
+            nc.vector.tensor_tensor(pages[PAGE_OF[c]][:].indirect(idx2[:]), h_tiles[c][:], weights, ALU.mult)
 
         z0_rows = sbuf("z0_rows", [P, M // P, 2, P, 2], BF16)
         for c in range(4):
-            if c > 0:
-                scatter(c + 1)
+            if c == 2:
+                scatter(2)
+                scatter(3)
+                nc.gpsimd.memset(pages[3][:], 0.0)
             site = sbuf("site", [P, M], F32, bufs=4)
             facing = sbuf("facing", [P, M], F32, bufs=4)
-            nc.vector.tensor_copy(site[:], pages[c % PAGES][:].indirect(idx3[:]))
-            nc.vector.tensor_copy(facing[:], pages[c % PAGES][:].indirect(idx4[:]))
+            nc.vector.tensor_copy(site[:], pages[PAGE_OF[c]][:].indirect(idx3[:]))
+            nc.vector.tensor_copy(facing[:], pages[PAGE_OF[c]][:].indirect(idx4[:]))
             z_acc = bank("z_acc", Z_BANK + c % 2)
             terms = (minus_ideal[:, c, :], site[:], facing[:])
             for number, term in enumerate(terms):
@@ -286,99 +315,173 @@ def tile_list_zeolite_ring_check_kernel(
                 turned[:, 0 : 2 * P].rearrange("p (u m) -> p m u", u=2),
             )
 
-        def read_site(c, m0, width, dst):
+        minus_target = dict()
+        for side in range(2):
+            for q in range(2):
+                turned = bank("target_turned", q + 2 * side)
+                for i in range(4):
+                    nc.tensor.transpose(turned[:, P * i : P * (i + 1)], target_sb[:, 4 * side + i, P * q : P * (q + 1)], ident[:])
+                minus_target[q, side] = placed("minus_target%d%d" % (q, side), [P, BANK], F32, AT_TARGET_TURNED + 2 * (q + 2 * side))
+                nc.scalar.activation(minus_target[q, side][:], turned[:], ACT.Copy, scale=-1.0)
+        out_banks = [bank("out_acc", 4 + j) for j in range(4)]
+
+        def add_turned(j, q, tiles, opening):
+            for i in range(2):
+                n0 = P * (2 * (j % 2) + i)
+                nc.tensor.matmul(
+                    out_banks[j][:, HALF * i + P * q : HALF * i + P * (q + 1)],
+                    tiles[q, j // 2][:, n0 : n0 + P],
+                    ident[:],
+                    start=(opening and i == 0 and q == 0),
+                    stop=(not opening and i == 1 and q == 1),
+                    is_transpose=True,
+                )
+
+        for j in range(4):
+            for q in range(2):
+                add_turned(j, q, minus_target, True)
+
+        def read_site(c, m0, width, kib, name):
+            dst = placed(name, [P, width], F32, kib)
             nc.vector.tensor_tensor(
-                dst, pages[c % PAGES][:].indirect(idx3[:, entries(m0, width)]), ideal_up[:, c - 4, m0 : m0 + width], ALU.subtract
+                dst[:], pages[PAGE_OF[c]][:].indirect(idx3[:, entries(m0, width)]), ideal_up[:, c - 4, m0 : m0 + width], ALU.subtract
             )
+            return dst
 
         def read_facing(c, m0, width, site_part, dst):
-            nc.vector.tensor_tensor(dst, pages[c % PAGES][:].indirect(idx4[:, entries(m0, width)]), site_part, ALU.add)
+            nc.vector.tensor_tensor(dst, pages[PAGE_OF[c]][:].indirect(idx4[:, entries(m0, width)]), site_part, ALU.add)
 
+        def weave(grouped, z_tiles):
+            nc.scalar.copy(grouped, z_tiles.rearrange("p e m -> p m e"))
+
+        low_grouped = placed("low_grouped", [P, HALF, 4], BF16, AT_LOW_GROUPED)
+        z45_low = placed("z45_low", [P, 2, HALF], F32, AT_Z45_LOW)
+        z67_low = [placed("z67_low%d" % q, [P, 2, QUARTER], F32, AT_Z67_LOW + q) for q in range(2)]
+        scatter(4)
         scatter(5)
-        w0_codes, w0_scales = quantise("w0", w0_rounded[:].rearrange("p n t -> p (n t)"), N)
-        w_quantised = {(0, side): (w0_codes[:, BANK * side : BANK * (side + 1)], w0_scales[:, BANK * side : BANK * (side + 1)]) for side in range(2)}
-
-        y_banks = [bank("y_acc", j) for j in range(8)]
-
-        def second_product(b, half, codes, scales, banks=range(4)):
-            for j in banks:
-                w_codes, w_scales = w_quantised[b, j // 2]
-                for i in range(2):
-                    n_cols = slice(P * (2 * (j % 2) + i), P * (2 * (j % 2) + i + 1))
-                    nc.tensor.matmul_mx(
-                        out=y_banks[4 * half + j][:, HALF * i : HALF * (i + 1)],
-                        lhsT=w_codes[:, n_cols].bitcast(FP8X4),
-                        lhsT_scale=w_scales[:, n_cols],
-                        rhs=codes.bitcast(FP8X4),
-                        rhs_scale=scales,
-                        start=(b == 0 and i == 0),
-                        stop=(b == 1 and i == 1),
-                    )
-
-
-        site4 = placed("site4", [P, M], F32, AT_SITE4)
-        read_site(4, 0, M, site4[:])
+        site4 = read_site(4, 0, HALF, AT_SITE_LOW, "site4")
+        w0 = [quantise("w0_left", w_rounded[0, 0][:], AT_H5)]
         scatter(6)
-        z45 = placed("z45", [P, 2, M], F32, AT_W_ROUNDED + 6)
-        w_quantised[1, 0] = quantise("w10", w1_rounded[0][:].rearrange("p n t -> p (n t)"), BANK)
-        site5 = sbuf("site5", [P, M], F32)
-        read_site(5, 0, M, site5[:])
-        read_facing(4, 0, M, site4[:], z45[:, 0, :])
-        read_facing(5, 0, M, site5[:], z45[:, 1, :])
+        site5 = read_site(5, 0, HALF, AT_SITE_LOW + 1, "site5")
+        read_facing(4, 0, HALF, site4[:], z45_low[:, 0, :])
+        site6 = read_site(6, 0, HALF, AT_SITE_LOW + 2, "site6")
+        read_facing(5, 0, HALF, site5[:], z45_low[:, 1, :])
+        weave(low_grouped[:, :, 0:2], z45_low[:])
+        w1_left = quantise("w1_left", w_rounded[1, 0][:], AT_H6)
+        for q in range(2):
+            read_facing(6, QUARTER * q, QUARTER, site6[:, QUARTER * q : QUARTER * (q + 1)], z67_low[q][:, 0, :])
         scatter(7)
-        site6 = placed("site6", [P, M], F32, AT_SITE4)
-        read_site(6, 0, M, site6[:])
-        z0_codes, z0_scales = quantise("z0_low", z0_grouped[0][:].rearrange("p m t -> p (m t)"), HALF, AT_H7)
-        second_product(0, 0, z0_codes[:], z0_scales[:])
+        z0_low = quantise("z0_low", z0_grouped[0][:], AT_SITE_LOW + 2)
+        yt_banks = dict()
+        for side in range(2):
+            for q in range(2):
+                yt_banks[q, side] = bank("yt_acc", q + 2 * side)
+        for q in range(2):
+            multiply(yt_banks[q, 0][:], columns(z0_low, P * q, P), columns(w0[0], 0, BANK), True, False)
+        site7 = [read_site(7, QUARTER * q, QUARTER, AT_SITE7_LOW + 0.5 * q, "site7_%d" % q) for q in range(2)]
+        for q in range(2):
+            read_facing(7, QUARTER * q, QUARTER, site7[q][:], z67_low[q][:, 1, :])
+        for q in range(2):
+            weave(low_grouped[:, QUARTER * q : QUARTER * (q + 1), 2:4], z67_low[q][:])
+        w1_right = [quantise("w1_right0", w_rounded[1, 1][:, 0:HALF, :], AT_SITE7_LOW)]
+        z1 = [quantise("z1_0", low_grouped[:, 0:QUARTER, :])]
+        multiply(yt_banks[0, 0][:], columns(z1[0], 0, P), columns(w1_left, 0, BANK), False, True)
+        w1_right.append(quantise("w1_right1", w_rounded[1, 1][:, HALF:BANK, :], AT_Z67_LOW))
+        z1.append(quantise("z1_1", low_grouped[:, QUARTER:HALF, :]))
+        multiply(yt_banks[1, 0][:], columns(z1[1], 0, P), columns(w1_left, 0, BANK), False, True)
+        w0.append(quantise("w0_right", w_rounded[0, 1][:], AT_Z67_LOW + 1))
+        for q in range(2):
+            for part in range(2):
+                acc = yt_banks[q, 1][:, HALF * part : HALF * (part + 1)]
+                multiply(acc, columns(z1[q], 0, P), columns(w1_right[part], 0, HALF), part == 0, False)
+            multiply(yt_banks[q, 1][:], columns(z0_low, P * q, P), columns(w0[1], 0, BANK), False, True)
+        z0_third = quantise("z0_third", z0_grouped[1][:, 0:QUARTER, :], AT_Z67_LOW + 1.5)
 
-        shared = placed("z67_high", [P, 2 * HALF], F32, AT_IDEAL_UP + 6)
-        low_tile = sbuf("low_grouped", [P, 4 * HALF], BF16)
-        low_grouped = low_tile[:]
-        high_tile = sbuf("high_grouped", [P, 4 * HALF], BF16)
-        grouped = (low_grouped, high_tile[:])
-
-        def weave(engine_copy, half, u, z_pair):
-            engine_copy(
-                grouped[half].rearrange("p (m t) -> p m t", t=4)[:, :, 2 * u : 2 * u + 2], z_pair.rearrange("p e m -> p m e")
-            )
-
-        for half in range(2):
-            weave(nc.scalar.copy, half, 0, z45[:, :, HALF * half : HALF * (half + 1)])
-        z67_low = placed("z67_low", [P, 2, HALF], F32, AT_H7 + 2)
-        site7 = sbuf("site7", [P, M], F32)
-        read_site(7, 0, M, site7[:])
-        read_facing(6, 0, HALF, site6[:, 0:HALF], z67_low[:, 0, :])
-        read_facing(7, 0, HALF, site7[:, 0:HALF], z67_low[:, 1, :])
-        weave(nc.scalar.copy, 0, 1, z67_low[:])
-        read_facing(6, HALF, HALF, site6[:, HALF:M], shared[:, 0:HALF])
-        read_facing(7, HALF, HALF, site7[:, HALF:M], shared[:, HALF : 2 * HALF])
-        low_codes, low_scales = quantise("low", low_grouped, HALF)
-        w_quantised[1, 1] = quantise("w11", w1_rounded[1][:].rearrange("p n t -> p (n t)"), BANK, AT_H7 + 1)
-        second_product(1, 0, low_codes[:], low_scales[:])
-        z0_high = quantise("z0_high", z0_grouped[1][:].rearrange("p m t -> p (m t)"), HALF, AT_H7 + 3)
-        weave(nc.scalar.copy, 1, 1, shared[:, 0 : 2 * HALF].rearrange("p (e m) -> p e m", e=2))
-        high_codes, high_scales = quantise("high", high_tile[:], HALF)
-        for j in range(4):
-            second_product(0, 1, z0_high[0][:], z0_high[1][:], [j])
-            second_product(1, 1, high_codes[:], high_scales[:], [j])
-
+        bounded_low = dict()
+        for side in range(2):
+            for q in range(2):
+                bounded_low[q, side] = placed("bounded_low%d%d" % (q, side), [P, BANK], F32, AT_BOUNDED_LOW + 2 * (q + 2 * side))
+                nc.scalar.activation(bounded_low[q, side][:], yt_banks[q, side][:], ACT.Tanh)
+                for j in (2 * side, 2 * side + 1):
+                    add_turned(j, q, bounded_low, False)
         out_rows = out.rearrange("(c p) m -> p c m", p=P)
-        for half in range(2):
-            m_cols = slice(HALF * half, HALF * (half + 1))
-            for j in range(4):
-                bounded = placed("bounded", [P, BANK], F32, AT_W_RAW1, bufs=4)
-                result = placed("result", [P, BANK], F32, AT_W_RAW1 + 8, bufs=8)
-                pieces = {(0, 0): (HALF, HALF), (1, 3): (HALF, P, P)}.get((half, j), (BANK,))
-                for number, width in enumerate(pieces):
-                    first = sum(pieces[:number])
-                    cols = slice(first, first + width)
-                    nc.scalar.activation(bounded[:, cols], y_banks[4 * half + j][:, cols], ACT.Tanh)
-                    if width == BANK:
-                        place = (slice(None), slice(2 * j, 2 * j + 2), m_cols)
-                        shaped = [tile[:].rearrange("p (i m) -> p i m", i=2) for tile in (result, bounded)]
-                    else:
-                        m0 = HALF * half + first % HALF
-                        place = (slice(None), 2 * j + first // HALF, slice(m0, m0 + width))
-                        shaped = [tile[:, cols] for tile in (result, bounded)]
-                    nc.vector.tensor_tensor(shaped[0], shaped[1], target_sb[place], ALU.subtract)
-                    nc.sync.dma_start(out_rows[place], shaped[0])
+
+        def finish_low(j):
+            result = placed("result_low%d" % j, [P, 2, HALF], F32, AT_RESULT_LOW + 2 * j)
+            nc.scalar.copy(result[:], out_banks[j][:].rearrange("p (i m) -> p i m", i=2))
+            nc.sync.dma_start(out_rows[:, 2 * j : 2 * j + 2, 0:HALF], result[:])
+
+        def w_block(b, block):
+            if b == 0:
+                return columns(w0[block // 4], P * (block % 4), P)
+            if block < 4:
+                return columns(w1_left, P * block, P)
+            return columns(w1_right[(block - 4) // 2], P * (block % 2), P)
+
+        blocks_in = {2: 4, 3: 2}
+        y_banks = dict()
+
+        def high_product(b, q, moving_side):
+            count = blocks_in[q]
+            for j in range(ROW_TILES // count):
+                if b == 0:
+                    y_banks[q, j] = bank("y_acc", 4 * (q - 2) + j)
+                for i in range(count):
+                    acc = y_banks[q, j][:, P * i : P * (i + 1)]
+                    multiply(acc, w_block(b, count * j + i), moving_side, b == 0 and i == 0, b == 1 and i == count - 1)
+
+        def high_sites(q):
+            return [read_site(c, QUARTER * q, QUARTER, AT_LOW_GROUPED + 0.5 * (c - 4), "site_high%d" % c) for c in range(4, 8)]
+
+        def bound_high(q, j, pieces):
+            count = blocks_in[q]
+            bounded = placed("bounded_high%d%d" % (q, j), [P, count, P], F32, AT_BOUNDED_HIGH + 4 * (q - 2) + 0.5 * count * j)
+            for first, many in pieces:
+                nc.scalar.activation(
+                    bounded[:, first : first + many, :].rearrange("p i m -> p (i m)"),
+                    y_banks[q, j][:, P * first : P * (first + many)],
+                    ACT.Tanh,
+                )
+            return bounded
+
+        def finish_high(q, j, bounded, pieces):
+            count = blocks_in[q]
+            result = placed("result_high%d%d" % (q, j), [P, count, P], F32, AT_RESULT_HIGH + 4 * (q - 2) + 0.5 * count * j)
+            for first, many in pieces:
+                place = (slice(None), slice(count * j + first, count * j + first + many), slice(QUARTER * q, QUARTER * (q + 1)))
+                piece = result[:, first : first + many, :]
+                nc.vector.tensor_tensor(piece, bounded[:, first : first + many, :], target_sb[place], ALU.subtract)
+                nc.sync.dma_start(out_rows[place], piece)
+
+        whole = ((0, 4),)
+        sites = high_sites(2)
+        z_third = placed("z_third", [P, 4, QUARTER], F32, AT_Z_HIGH)
+        for c in range(4, 8):
+            read_facing(c, QUARTER * 2, QUARTER, sites[c - 4][:], z_third[:, c - 4, :])
+        finish_low(0)
+        finish_low(1)
+        third_grouped = placed("third_grouped", [P, QUARTER, 4], BF16, AT_BOUNDED_LOW + 4)
+        weave(third_grouped[:], z_third[:])
+        finish_low(2)
+        finish_low(3)
+        high_product(0, 2, columns(z0_third, 0, QUARTER))
+        sites = high_sites(3)
+        z1.append(quantise("z1_2", third_grouped[:], AT_LAST_GROUPED))
+        high_product(1, 2, columns(z1[2], 0, QUARTER))
+        z_last = [placed("z_last%d" % u, [P, 2, QUARTER], F32, AT_Z_HIGH + u) for u in range(2)]
+        for c in range(4, 8):
+            if c == 6:
+                z0_last = quantise("z0_last", z0_grouped[1][:, QUARTER:HALF, :], AT_BOUNDED_LOW + 4)
+                high_product(0, 3, columns(z0_last, 0, QUARTER))
+            read_facing(c, QUARTER * 3, QUARTER, sites[c - 4][:], z_last[(c - 4) // 2][:, c % 2, :])
+        last_grouped = placed("last_grouped", [P, QUARTER, 4], BF16, AT_LAST_GROUPED)
+        bounded_left = bound_high(2, 0, whole)
+        for u in range(2):
+            weave(last_grouped[:, :, 2 * u : 2 * u + 2], z_last[u][:])
+        bounded_right = bound_high(2, 1, whole)
+        finish_high(2, 0, bounded_left, whole)
+        z1.append(quantise("z1_3", last_grouped[:]))
+        high_product(1, 3, columns(z1[3], 0, QUARTER))
+        finish_high(2, 1, bounded_right, whole)
+        for j in range(4):
+            finish_high(3, j, bound_high(3, j, ((0, 2),)), ((0, 2),))

@@ -453,7 +453,7 @@ def tile_list_zeolite_ring_check_kernel(
                 nc.vector.tensor_tensor(piece, bounded[:, first : first + many, :], target_sb[place], ALU.subtract)
                 nc.sync.dma_start(out_rows[place], piece)
 
-        whole = ((0, 4),)
+        whole, halves = ((0, 4),), ((0, 2), (2, 2))
         sites = high_sites(2)
         z_third = placed("z_third", [P, 4, QUARTER], F32, AT_Z_HIGH)
         for c in range(4, 8):
@@ -478,10 +478,11 @@ def tile_list_zeolite_ring_check_kernel(
         bounded_left = bound_high(2, 0, whole)
         for u in range(2):
             weave(last_grouped[:, :, 2 * u : 2 * u + 2], z_last[u][:])
-        bounded_right = bound_high(2, 1, whole)
+        bounded_right = bound_high(2, 1, halves)
         finish_high(2, 0, bounded_left, whole)
         z1.append(quantise("z1_3", last_grouped[:]))
         high_product(1, 3, columns(z1[3], 0, QUARTER))
-        finish_high(2, 1, bounded_right, whole)
+        finish_high(2, 1, bounded_right, halves)
         for j in range(4):
-            finish_high(3, j, bound_high(3, j, ((0, 2),)), ((0, 2),))
+            pieces = ((0, 2),) if j < 3 else ((0, 1), (1, 1))
+            finish_high(3, j, bound_high(3, j, pieces), pieces)

@@ -274,9 +274,10 @@ def tile_list_zeolite_ring_check_kernel(
         def columns(quantised, first, count):
             return quantised[0][:, first : first + count], quantised[1][:, first : first + count]
 
-        def scatter(c):
+        def scatter(c, first=0, count=S):
             weights = wgs_sb[:] if c < 4 else wgs_dealt[:, c - 4, :]
-            nc.vector.tensor_tensor(pages[PAGE_OF[c]][:].indirect(idx2[:]), h_tiles[c][:], weights, ALU.mult)
+            cols = slice(first, first + count)
+            nc.vector.tensor_tensor(pages[PAGE_OF[c]][:].indirect(idx2[:, entries(first, count)]), h_tiles[c][:, cols], weights[:, cols], ALU.mult)
 
         z0_rows = sbuf("z0_rows", [P, M // P, 2, P, 2], BF16)
         for c in range(4):
@@ -367,11 +368,15 @@ def tile_list_zeolite_ring_check_kernel(
         site6 = read_site(6, 0, HALF, AT_SITE_LOW + 2, "site6")
         read_facing(5, 0, HALF, site5[:], z45_low[:, 1, :])
         weave(low_grouped[:, :, 0:2], z45_low[:])
-        w1_left = quantise("w1_left", w_rounded[1, 0][:], AT_H6)
         for q in range(2):
             read_facing(6, QUARTER * q, QUARTER, site6[:, QUARTER * q : QUARTER * (q + 1)], z67_low[q][:, 0, :])
-        scatter(7)
-        z0_low = quantise("z0_low", z0_grouped[0][:], AT_SITE_LOW + 2)
+        scatter(7, 0, S - FIRST)
+        w1_left = quantise("w1_left", w_rounded[1, 0][:], AT_SITE_LOW + 2)
+        for number in (2, 3):
+            unread = bank("unread", number)
+            multiply(unread[:], columns(w0[0], 0, P), columns(w1_left, 0, BANK), True, True)
+        scatter(7, S - FIRST, FIRST)
+        z0_low = quantise("z0_low", z0_grouped[0][:], AT_W_ROUNDED + 8)
         yt_banks = dict()
         for side in range(2):
             for q in range(2):

@@ -96,12 +96,12 @@ def tile_list_zeolite_ring_check_kernel(
         w4_first = sbuf("w4_first", [P, 2, 2 * EARLY], U8)
         wgs_first = placed("wgs_first", [P, FIRST], F32, AT_TAB_S)
         nc.sync.dma_start(idx[:], offs)
-        nc.sync.dma_start(tab_s[96:128, :].bitcast(I32), tab_scales.rearrange("a q n -> q a n").bitcast(I32))
+        nc.scalar.dma_start(tab_s[96:128, :].bitcast(I32), tab_scales.rearrange("a q n -> q a n").bitcast(I32))
         nc.sync.dma_start(idx2[:], offs2)
         nc.sync.dma_start(idx3[:], offs3)
-        nc.sync.dma_start(tab_w[0][:], tab_words[0].rearrange("p n t -> p (n t)").bitcast(I32))
-        nc.sync.dma_start(tab_w[1][:], tab_words[1].rearrange("p n t -> p (n t)").bitcast(I32))
-        nc.sync.dma_start(w4_first[:].bitcast(I32), w4_words_p[:, :, 0 : 2 * EARLY].bitcast(I32))
+        nc.scalar.dma_start(tab_w[0][:], tab_words[0].rearrange("p n t -> p (n t)").bitcast(I32))
+        nc.scalar.dma_start(tab_w[1][:], tab_words[1].rearrange("p n t -> p (n t)").bitcast(I32))
+        nc.scalar.dma_start(w4_first[:].bitcast(I32), w4_words_p[:, :, 0 : 2 * EARLY].bitcast(I32))
         nc.sync.dma_start(idx4[:], offs4)
 
         offset = sbuf("offset", [P, P], F32)
@@ -140,7 +140,7 @@ def tile_list_zeolite_ring_check_kernel(
             if first > 0:
                 nc.scalar.dma_start(wgs_first[:], wgs[:, 0:FIRST])
             for g in (0, 2, 1, 3):
-                (nc.scalar if first == 0 else nc.sync).dma_start(
+                nc.sync.dma_start(
                     plane[32 * g : 32 * g + 4, :, :].bitcast(I32),
                     picked[96 + 8 * g : 96 + 8 * g + 8, :].bitcast(I32),
                 )

@@ -21,14 +21,15 @@ BANK = 512
 PASS = 512
 HALF = M // 2
 ROW_TILES = H // P
-PAGE_OF = (0, 1, 2, 0, 1, 3, 2, 0)
+PAGE_OF = (0, 1, 0, 2, 1, 3, 0, 2)
 QUARTER = M // 4
 PER_COLUMN = 16
 ALIGN = 64
 EARLY = 2 * P
 FIRST = 256
+PIECE = 256
 
-Z_BANK = 4
+Z_BANK = 0
 TURN_BANK = 6
 
 AT_WGS = 0
@@ -36,32 +37,33 @@ AT_PICKED = 3.5
 AT_W4_LOW = 4
 AT_IDEAL_LOW = 9
 AT_TAB_W1 = 16
-AT_W_RAW0 = 20
+AT_W_RIGHT = 54
 AT_TAB_S = 24
 AT_TAB_W0 = 30
-AT_W_RAW1 = 38
-AT_WGS_DEALT = 54
+AT_W_LEFT = 38
+AT_WGS_DEALT = 20
 AT_IDEAL_UP = 70
 AT_TARGET = 78
 AT_W_ROUNDED = 94
 AT_Z0_GROUPED = 110
 AT_H7 = 114
 AT_PAGE2 = 120
-AT_H5 = 128
-AT_H6 = 132
-AT_PAGE3 = AT_WGS
-AT_SITE_LOW = AT_IDEAL_LOW
+AT_PAGE3 = 128
+AT_H1_REST = 126.5
+AT_H5 = 136
+AT_H6 = 140
+AT_V_W = 144
 AT_Z45_LOW = 12
 AT_Z67_LOW = 14
 AT_SITE7_LOW = 16
-AT_LOW_GROUPED = 17
+AT_LOW_GROUPED = AT_W_RIGHT
 AT_LAST_GROUPED = 19
-AT_TARGET_TURNED = AT_W_RAW0
-AT_BOUNDED_LOW = 28
-AT_RESULT_LOW = AT_W_RAW1
+AT_TARGET_TURNED = AT_W_RIGHT
+AT_BOUNDED_LOW = 62
+AT_RESULT_LOW = AT_W_LEFT
 AT_BOUNDED_HIGH = 46
-AT_RESULT_HIGH = 54
-AT_Z_HIGH = 62
+AT_RESULT_HIGH = 20
+AT_Z_HIGH = 28
 
 
 def tile_list_zeolite_ring_check_kernel(
@@ -128,7 +130,7 @@ def tile_list_zeolite_ring_check_kernel(
         pages = [sbuf("page0", [P, T2], F32), sbuf("page1", [P, T2], F32)]
         pages = pages + [placed("page2", [P, T2], F32, AT_PAGE2), placed("page3", [P, T2], F32, AT_PAGE3)]
         nc.vector.memset(pages[0][:], 0.0)
-        w4_s_rest = sbuf("w4_s_rest", [P, 2, H - EARLY], U8)
+        w4_s_rest = placed("w4_s_rest", [P, 2, H - EARLY], U8, AT_W_ROUNDED + 3.25)
         nc.gpsimd.memset(w4_s_rest[:].bitcast(I32), 0)
         nc.gpsimd.memset(pages[1][:], 0.0)
 
@@ -146,7 +148,7 @@ def tile_list_zeolite_ring_check_kernel(
                 )
         for r in range(4):
             nc.sync.dma_start(w4_s_rest[r:128:32, :, :].bitcast(I32), w4_scale_rows[r][:, :, EARLY:H].bitcast(I32))
-        v_w = [sbuf("v_w%d" % a, [P, S], U32) for a in range(2)]
+        v_w = [placed("v_w%d" % a, [P, S], U32, AT_V_W + 4 * a) for a in range(2)]
         nc.vector.tensor_copy(v_w[0][:], tab_w[0][:].bitcast(U32).indirect(idx[:]))
         for first, count in ((0, FIRST), (FIRST, S - FIRST)):
             nc.vector.tensor_copy(
@@ -183,22 +185,24 @@ def tile_list_zeolite_ring_check_kernel(
             for h_acc, (number, dst, pieces) in zip(accs, groups):
                 nc.scalar.copy(dst, h_acc[:, 0 : sum(width for j0, width in pieces)])
 
-        h0_first = placed("h0_first", [P, FIRST], F32, AT_W_RAW1 - 0.5)
-        h_first = [h0_first, sbuf("h1_first", [P, FIRST], F32)]
-        h_rest = [placed("h0_rest", [P, S - FIRST], F32, AT_IDEAL_UP - 1.5), placed("h1_rest", [P, S - FIRST], F32, AT_PAGE2)]
+        h0_first = placed("h0_first", [P, FIRST], F32, AT_WGS_DEALT + 15)
+        h_first = [h0_first, placed("h1_first", [P, FIRST], F32, AT_W_LEFT + 7.5)]
+        h_rest = [placed("h0_rest", [P, S - FIRST], F32, AT_IDEAL_UP - 1.5), placed("h1_rest", [P, S - FIRST], F32, AT_H1_REST)]
         for c in range(2):
             first_product(c, [(c, h_first[c][:], [(0, FIRST)])])
         for c in range(2):
             first_product(c, [(2 - 2 * c, h_rest[c][:, 0:BANK], [(FIRST, BANK)])])
             first_product(c, [(3 - 2 * c, h_rest[c][:, BANK:], [(FIRST + BANK, S - FIRST - BANK)])])
         h_tiles = dict()
-        for c in range(2, 5):
-            h_tiles[c] = sbuf("h%d" % c, [P, S], F32)
+        h_tiles[2] = sbuf("h2", [P, S], F32)
         for c, kib in ((5, AT_H5), (6, AT_H6), (7, AT_H7)):
             h_tiles[c] = placed("h%d" % c, [P, S], F32, kib)
-        for c in range(2, 4):
-            first_product(c, [(2, h_tiles[c][:, 0:BANK], [(0, FIRST), (FIRST, BANK - FIRST)])])
-            first_product(c, [(3, h_tiles[c][:, BANK:], [(BANK, BANK)])])
+
+        def natural_tile(c, number):
+            first_product(c, [(number + 1, h_tiles[c][:, BANK:], [(BANK, BANK)])])
+            first_product(c, [(number, h_tiles[c][:, 0:BANK], [(0, FIRST), (FIRST, BANK - FIRST)])])
+
+        natural_tile(2, 2)
         h_turned = placed("h_turned", [P, S // P, 4, P], F32, AT_TARGET)
         for block in range(S // P):
             j_cols = slice(P * block, P * (block + 1))
@@ -214,12 +218,43 @@ def tile_list_zeolite_ring_check_kernel(
                     stop=(a == 1),
                 )
             nc.scalar.copy(h_turned[:, block], h_acc[:].rearrange("j (p t) -> j t p", t=4))
-        for t in range(4):
+        w_rounded = dict()
+
+        def load_w(dst, b, side):
+            cols = slice(BANK * side, BANK * (side + 1))
+            nc.sync.dma_start(dst, w[PASS * b : PASS * (b + 1), cols].rearrange("(p t) n -> p t n", t=4))
+
+        def round_w(raw, b, side):
+            w_rounded[b, side] = placed("w_rounded%d%d" % (b, side), [P, BANK, 4], BF16, AT_W_ROUNDED + 8 * side + 4 * b)
+            nc.scalar.copy(
+                w_rounded[b, side][:].rearrange("p (c i) t -> p c t i", i=4),
+                raw.rearrange("p t (c i) -> p c t i", i=4),
+            )
+
+        w_left = [placed("w_left%d" % b, [P, 4, BANK], F32, AT_W_LEFT + 8 * b) for b in range(2)]
+        for b in range(2):
+            load_w(w_left[b][:], b, 0)
+
+        def turn_back(c, part, number, width=BANK):
+            h_back = bank("h_back", number)
+            for i in range(4):
+                nc.tensor.transpose(h_back[:, P * i : P * (i + 1)], h_turned[:, 4 * part + i, c - 4, :], ident[:])
+            for first in range(0, BANK, width):
+                at = BANK * part + first
+                nc.scalar.copy(h_tiles[c][:, at : at + width], h_back[:, first : first + width])
+
+        for c in (3, 4):
+            h_tiles[c] = placed("h%d" % c, [P, S], F32, AT_W_LEFT + 8 + 4 * (c - 3))
+        for c in (6, 7):
             for part in range(2):
-                h_back = bank("h_back", 2 + part)
-                for i in range(4):
-                    nc.tensor.transpose(h_back[:, P * i : P * (i + 1)], h_turned[:, 4 * part + i, t, :], ident[:])
-                nc.scalar.copy(h_tiles[4 + t][:, BANK * part : BANK * (part + 1)], h_back[:])
+                turn_back(c, part, 2 + part)
+        for b in range(2):
+            round_w(w_left[b][:], b, 0)
+        natural_tile(3, 0)
+        turn_back(4, 0, 4, PIECE)
+        turn_back(5, 0, 1)
+        turn_back(4, 1, 5)
+        turn_back(5, 1, 0)
 
         for c in range(2):
             nc.vector.tensor_tensor(pages[c][:].indirect(idx2[:, entries(0, FIRST)]), h_first[c][:], wgs_first[:], ALU.mult)
@@ -229,29 +264,29 @@ def tile_list_zeolite_ring_check_kernel(
             )
 
         nc.gpsimd.memset(pages[2][:], 0.0)
+        nc.gpsimd.memset(pages[3][:], 0.0)
         minus_ideal = sbuf("minus_ideal", [P, 4, M], F32)
         for c in range(4):
             nc.scalar.activation(minus_ideal[:, c, :], ideal_low[:, c, :], ACT.Copy, scale=-1.0)
 
-        w_raw = [placed("w_raw0", [P, 4, N], F32, AT_W_RAW0), placed("w_raw1", [P, 4, N], F32, AT_W_RAW1)]
-        for b in range(2):
-            nc.sync.dma_start(w_raw[b][:], w[PASS * b : PASS * (b + 1), :].rearrange("(p t) n -> p t n", t=4))
-        ideal_up = placed("ideal_up", [P, 4, M], F32, AT_IDEAL_UP)
-        nc.sync.dma_start(ideal_up[:], ideal[PASS:H, :].rearrange("(p t) m -> p t m", t=4))
         wgs_dealt = placed("wgs_dealt", [P, 4, S], F32, AT_WGS_DEALT)
-        for q in (0, 2, 1, 3):
-            nc.sync.dma_start(wgs_dealt[32 * q : 32 * (q + 1)], wgs.rearrange("(p t) j -> p t j", t=4))
+        ideal_up = placed("ideal_up", [P, 4, M], F32, AT_IDEAL_UP)
+        for u in range(2):
+            for q in (0, 2, 1, 3):
+                nc.sync.dma_start(
+                    wgs_dealt[32 * q : 32 * (q + 1), 2 * u : 2 * u + 2, :],
+                    wgs.rearrange("(p t) j -> p t j", t=4)[:, 2 * u : 2 * u + 2, :],
+                )
+            if u == 0:
+                nc.sync.dma_start(ideal_up[:], ideal[PASS:H, :].rearrange("(p t) m -> p t m", t=4))
+        w_right = placed("w_right", [P, 2, 4, BANK], F32, AT_W_RIGHT)
+        for b in (1, 0):
+            load_w(w_right[:, b], b, 1)
         target_sb = placed("target_sb", [P, ROW_TILES, M], F32, AT_TARGET)
         nc.sync.dma_start(target_sb[:], target.rearrange("(c p) m -> p c m", p=P))
 
-        w_rounded = dict()
-        for b in range(2):
-            for side in range(2):
-                w_rounded[b, side] = placed("w_rounded%d%d" % (b, side), [P, BANK, 4], BF16, AT_W_ROUNDED + 8 * b + 4 * side)
-                nc.scalar.copy(
-                    w_rounded[b, side][:].rearrange("p (c i) t -> p c t i", i=4),
-                    w_raw[b][:, :, BANK * side : BANK * (side + 1)].rearrange("p t (c i) -> p c t i", i=4),
-                )
+        for b in (1, 0):
+            round_w(w_right[:, b], b, 1)
 
         def quantise(name, grouped, kib=None):
             width = grouped.shape[1]
@@ -280,22 +315,16 @@ def tile_list_zeolite_ring_check_kernel(
             nc.vector.tensor_tensor(pages[PAGE_OF[c]][:].indirect(idx2[:, entries(first, count)]), h_tiles[c][:, cols], weights[:, cols], ALU.mult)
 
         z0_rows = sbuf("z0_rows", [P, M // P, 2, P, 2], BF16)
-        for c in range(4):
-            if c == 2:
-                scatter(2)
-                scatter(3)
-                nc.gpsimd.memset(pages[3][:], 0.0)
-            site = sbuf("site", [P, M], F32, bufs=4)
-            facing = sbuf("facing", [P, M], F32, bufs=4)
-            nc.vector.tensor_copy(site[:], pages[PAGE_OF[c]][:].indirect(idx3[:]))
-            nc.vector.tensor_copy(facing[:], pages[PAGE_OF[c]][:].indirect(idx4[:]))
+
+        def sum_and_turn(c, sites, facings):
             z_acc = bank("z_acc", Z_BANK + c % 2)
-            terms = (minus_ideal[:, c, :], site[:], facing[:])
-            for number, term in enumerate(terms):
+            terms = ([minus_ideal[:, c, :]], sites, facings)
+            for number, pieces in enumerate(terms):
+                blocks = [piece[:, P * i : P * (i + 1)] for piece in pieces for i in range(piece.shape[1] // P)]
                 for j in range(4):
                     nc.tensor.matmul(
                         z_acc[:, P * j : P * (j + 1)],
-                        term[:, P * j : P * (j + 1)],
+                        blocks[j],
                         ident[:],
                         start=(number == 0 and j == 0),
                         stop=(number == 2 and j == 3),
@@ -305,6 +334,32 @@ def tile_list_zeolite_ring_check_kernel(
                 z0_rows[:, :, :, 32 * c : 32 * (c + 1), :],
                 z_acc[:].rearrange("m (j p u e) -> m j u p e", j=4, u=2, e=2),
             )
+
+        def spent(c, piece, width=PIECE):
+            return h_tiles[c][:, PIECE * piece : PIECE * piece + width]
+
+        for c in range(2):
+            site = placed("site%d" % c, [P, M], F32, AT_V_W + 4 * c)
+            facing = placed("facing%d" % c, [P, M], F32, AT_V_W + 4 * c + 2)
+            nc.vector.tensor_copy(site[:], pages[PAGE_OF[c]][:].indirect(idx3[:]))
+            nc.vector.tensor_copy(facing[:], pages[PAGE_OF[c]][:].indirect(idx4[:]))
+            sum_and_turn(c, [site[:]], [facing[:]])
+        scatter(2)
+        scatter(3, 0, 2 * PIECE)
+        turns = []
+        for c in range(3, 7):
+            turns = turns + [(c + 1, 0), (c, 2), (c + 1, 1), (c, 3)]
+        before = (3, 0)
+        for c in (2, 3):
+            reads = []
+            for i, (offsets, half) in enumerate(((idx3, 0), (idx4, 0), (idx3, 1), (idx4, 1))):
+                tile_number, piece = turns[4 * (c - 2) + i]
+                scatter(tile_number, PIECE * piece, PIECE)
+                dst = spent(before[0], before[1])
+                nc.vector.tensor_copy(dst, pages[PAGE_OF[c]][:].indirect(offsets[:, entries(HALF * half, HALF)]))
+                reads.append(dst)
+                before = (tile_number, piece)
+            sum_and_turn(c, reads[0::2], reads[1::2])
         z0_grouped = [placed("z0_grouped%d" % half, [P, HALF, 4], BF16, AT_Z0_GROUPED + 2 * half) for half in range(2)]
         pairs = z0_rows[:].rearrange("m j u p e -> m j u (p e)").bitcast(F32)
         for j in range(M // P):
@@ -343,9 +398,11 @@ def tile_list_zeolite_ring_check_kernel(
                 add_turned(j, q, minus_target, True)
 
         def read_site(c, m0, width, kib, name):
-            dst = placed(name, [P, width], F32, kib)
+            return read_site_into(c, m0, width, placed(name, [P, width], F32, kib)[:])
+
+        def read_site_into(c, m0, width, dst):
             nc.vector.tensor_tensor(
-                dst[:], pages[PAGE_OF[c]][:].indirect(idx3[:, entries(m0, width)]), ideal_up[:, c - 4, m0 : m0 + width], ALU.subtract
+                dst, pages[PAGE_OF[c]][:].indirect(idx3[:, entries(m0, width)]), ideal_up[:, c - 4, m0 : m0 + width], ALU.subtract
             )
             return dst
 
@@ -358,25 +415,29 @@ def tile_list_zeolite_ring_check_kernel(
         low_grouped = placed("low_grouped", [P, HALF, 4], BF16, AT_LOW_GROUPED)
         z45_low = placed("z45_low", [P, 2, HALF], F32, AT_Z45_LOW)
         z67_low = [placed("z67_low%d" % q, [P, 2, QUARTER], F32, AT_Z67_LOW + q) for q in range(2)]
-        scatter(4)
-        scatter(5)
-        site4 = read_site(4, 0, HALF, AT_SITE_LOW, "site4")
-        w0 = [quantise("w0_left", w_rounded[0, 0][:], AT_H5)]
-        scatter(6)
-        site5 = read_site(5, 0, HALF, AT_SITE_LOW + 1, "site5")
-        read_facing(4, 0, HALF, site4[:], z45_low[:, 0, :])
-        site6 = read_site(6, 0, HALF, AT_SITE_LOW + 2, "site6")
-        read_facing(5, 0, HALF, site5[:], z45_low[:, 1, :])
+        for c in (4, 5):
+            sites = []
+            for i in range(4):
+                tile_number, piece = turns[4 * (c - 2) + i]
+                scatter(tile_number, PIECE * piece, PIECE)
+                if i < 2:
+                    sites.append(read_site_into(c, QUARTER * i, QUARTER, spent(before[0], before[1], QUARTER)))
+                else:
+                    q = i - 2
+                    read_facing(c, QUARTER * q, QUARTER, sites[q], z45_low[:, c - 4, QUARTER * q : QUARTER * (q + 1)])
+                before = (tile_number, piece)
         weave(low_grouped[:, :, 0:2], z45_low[:])
+        scatter(7, 2 * PIECE, PIECE)
+        site6 = read_site_into(6, 0, HALF, spent(6, 3))
+        w0 = [quantise("w0_left", w_rounded[0, 0][:], AT_H5)]
         for q in range(2):
             read_facing(6, QUARTER * q, QUARTER, site6[:, QUARTER * q : QUARTER * (q + 1)], z67_low[q][:, 0, :])
-        scatter(7, 0, S - FIRST)
-        w1_left = quantise("w1_left", w_rounded[1, 0][:], AT_SITE_LOW + 2)
+        w1_left = quantise("w1_left", w_rounded[1, 0][:], AT_H6)
         for number in (2, 3):
             unread = bank("unread", number)
             multiply(unread[:], columns(w0[0], 0, P), columns(w1_left, 0, BANK), True, True)
         scatter(7, S - FIRST, FIRST)
-        z0_low = quantise("z0_low", z0_grouped[0][:], AT_W_ROUNDED + 8)
+        z0_low = quantise("z0_low", z0_grouped[0][:], AT_W_ROUNDED + 4)
         yt_banks = dict()
         for side in range(2):
             for q in range(2):
@@ -385,7 +446,7 @@ def tile_list_zeolite_ring_check_kernel(
             multiply(yt_banks[q, 0][:], columns(z0_low, P * q, P), columns(w0[0], 0, BANK), True, False)
         site7 = [read_site(7, QUARTER * q, QUARTER, AT_SITE7_LOW + 0.5 * q, "site7_%d" % q) for q in range(2)]
         for q in range(2):
-            read_facing(7, QUARTER * q, QUARTER, site7[q][:], z67_low[q][:, 1, :])
+            read_facing(7, QUARTER * q, QUARTER, site7[q], z67_low[q][:, 1, :])
         for q in range(2):
             weave(low_grouped[:, QUARTER * q : QUARTER * (q + 1), 2:4], z67_low[q][:])
         w1_right = [quantise("w1_right0", w_rounded[1, 1][:, 0:HALF, :], AT_SITE7_LOW)]
@@ -462,7 +523,7 @@ def tile_list_zeolite_ring_check_kernel(
         sites = high_sites(2)
         z_third = placed("z_third", [P, 4, QUARTER], F32, AT_Z_HIGH)
         for c in range(4, 8):
-            read_facing(c, QUARTER * 2, QUARTER, sites[c - 4][:], z_third[:, c - 4, :])
+            read_facing(c, QUARTER * 2, QUARTER, sites[c - 4], z_third[:, c - 4, :])
         finish_low(0)
         finish_low(1)
         third_grouped = placed("third_grouped", [P, QUARTER, 4], BF16, AT_BOUNDED_LOW + 4)
@@ -478,7 +539,7 @@ def tile_list_zeolite_ring_check_kernel(
             if c == 6:
                 z0_last = quantise("z0_last", z0_grouped[1][:, QUARTER:HALF, :], AT_BOUNDED_LOW + 4)
                 high_product(0, 3, columns(z0_last, 0, QUARTER))
-            read_facing(c, QUARTER * 3, QUARTER, sites[c - 4][:], z_last[(c - 4) // 2][:, c % 2, :])
+            read_facing(c, QUARTER * 3, QUARTER, sites[c - 4], z_last[(c - 4) // 2][:, c % 2, :])
         last_grouped = placed("last_grouped", [P, QUARTER, 4], BF16, AT_LAST_GROUPED)
         bounded_left = bound_high(2, 0, whole)
         for u in range(2):

@@ -29,7 +29,7 @@ EARLY = 2 * P
 FIRST = 256
 PIECE = 256
 
-Z_BANK = 0
+Z_BANK = 6
 TURN_BANK = 6
 
 AT_WGS = 0
@@ -48,11 +48,14 @@ AT_W_ROUNDED = 94
 AT_Z0_GROUPED = 110
 AT_H7 = 114
 AT_PAGE2 = 120
-AT_PAGE3 = 128
-AT_H1_REST = 126.5
-AT_H5 = 136
-AT_H6 = 140
-AT_V_W = 144
+AT_PAGE3 = AT_WGS
+AT_H1_REST = AT_PAGE2
+AT_H4 = AT_W_LEFT
+AT_H5 = AT_W_LEFT + 4
+AT_READS2 = AT_W_LEFT + 8
+AT_H6 = 128
+AT_V_W = 132
+AT_H7_FIRST = 140
 AT_Z45_LOW = 12
 AT_Z67_LOW = 14
 AT_SITE7_LOW = 16
@@ -194,13 +197,19 @@ def tile_list_zeolite_ring_check_kernel(
             first_product(c, [(2 - 2 * c, h_rest[c][:, 0:BANK], [(FIRST, BANK)])])
             first_product(c, [(3 - 2 * c, h_rest[c][:, BANK:], [(FIRST + BANK, S - FIRST - BANK)])])
         h_tiles = dict()
-        h_tiles[2] = sbuf("h2", [P, S], F32)
-        for c, kib in ((5, AT_H5), (6, AT_H6), (7, AT_H7)):
+        for c in (2, 3):
+            h_tiles[c] = sbuf("h%d" % c, [P, S], F32)
+        for c, kib in ((4, AT_H4), (5, AT_H5), (6, AT_H6), (7, AT_H7)):
             h_tiles[c] = placed("h%d" % c, [P, S], F32, kib)
 
+        h7_first = placed("h7_first", [P, PIECE], F32, AT_H7_FIRST)
+
+        def h_piece(c, first, count):
+            return h7_first[:] if (c, first) == (7, 0) else h_tiles[c][:, first : first + count]
+
         def natural_tile(c, number):
-            first_product(c, [(number + 1, h_tiles[c][:, BANK:], [(BANK, BANK)])])
             first_product(c, [(number, h_tiles[c][:, 0:BANK], [(0, FIRST), (FIRST, BANK - FIRST)])])
+            first_product(c, [(number + 1, h_tiles[c][:, BANK:], [(BANK, BANK)])])
 
         natural_tile(2, 2)
         h_turned = placed("h_turned", [P, S // P, 4, P], F32, AT_TARGET)
@@ -231,30 +240,34 @@ def tile_list_zeolite_ring_check_kernel(
                 raw.rearrange("p t (c i) -> p c t i", i=4),
             )
 
-        w_left = [placed("w_left%d" % b, [P, 4, BANK], F32, AT_W_LEFT + 8 * b) for b in range(2)]
+        w_left = placed("w_left", [P, 2, 4, BANK], F32, AT_W_LEFT)
         for b in range(2):
-            load_w(w_left[b][:], b, 0)
+            load_w(w_left[:, b], b, 0)
 
-        def turn_back(c, part, number, width=BANK):
+        def turn_back(c, part, number):
             h_back = bank("h_back", number)
             for i in range(4):
                 nc.tensor.transpose(h_back[:, P * i : P * (i + 1)], h_turned[:, 4 * part + i, c - 4, :], ident[:])
-            for first in range(0, BANK, width):
-                at = BANK * part + first
-                nc.scalar.copy(h_tiles[c][:, at : at + width], h_back[:, first : first + width])
+            return h_back
 
-        for c in (3, 4):
-            h_tiles[c] = placed("h%d" % c, [P, S], F32, AT_W_LEFT + 8 + 4 * (c - 3))
-        for c in (6, 7):
-            for part in range(2):
-                turn_back(c, part, 2 + part)
-        for b in range(2):
-            round_w(w_left[b][:], b, 0)
+        def copy_back(c, part, h_back, first=0, width=BANK):
+            nc.scalar.copy(h_piece(c, BANK * part + first, width), h_back[:, first : first + width])
+
         natural_tile(3, 0)
-        turn_back(4, 0, 4, PIECE)
-        turn_back(5, 0, 1)
-        turn_back(4, 1, 5)
-        turn_back(5, 1, 0)
+        for part in range(2):
+            copy_back(6, part, turn_back(6, part, 2 + part))
+        first_half = turn_back(7, 0, 2)
+        for first in (0, PIECE):
+            copy_back(7, 0, first_half, first, PIECE)
+        copy_back(7, 1, turn_back(7, 1, 3))
+        for b in range(2):
+            round_w(w_left[:, b], b, 0)
+        first_halves = [turn_back(c, 0, c) for c in (4, 5)]
+        for first in (0, PIECE):
+            for c in (4, 5):
+                copy_back(c, 0, first_halves[c - 4], first, PIECE)
+        for c in (4, 5):
+            copy_back(c, 1, turn_back(c, 1, c + 2))
 
         for c in range(2):
             nc.vector.tensor_tensor(pages[c][:].indirect(idx2[:, entries(0, FIRST)]), h_first[c][:], wgs_first[:], ALU.mult)
@@ -264,7 +277,6 @@ def tile_list_zeolite_ring_check_kernel(
             )
 
         nc.gpsimd.memset(pages[2][:], 0.0)
-        nc.gpsimd.memset(pages[3][:], 0.0)
         minus_ideal = sbuf("minus_ideal", [P, 4, M], F32)
         for c in range(4):
             nc.scalar.activation(minus_ideal[:, c, :], ideal_low[:, c, :], ACT.Copy, scale=-1.0)
@@ -284,9 +296,6 @@ def tile_list_zeolite_ring_check_kernel(
             load_w(w_right[:, b], b, 1)
         target_sb = placed("target_sb", [P, ROW_TILES, M], F32, AT_TARGET)
         nc.sync.dma_start(target_sb[:], target.rearrange("(c p) m -> p c m", p=P))
-
-        for b in (1, 0):
-            round_w(w_right[:, b], b, 1)
 
         def quantise(name, grouped, kib=None):
             width = grouped.shape[1]
@@ -312,7 +321,7 @@ def tile_list_zeolite_ring_check_kernel(
         def scatter(c, first=0, count=S):
             weights = wgs_sb[:] if c < 4 else wgs_dealt[:, c - 4, :]
             cols = slice(first, first + count)
-            nc.vector.tensor_tensor(pages[PAGE_OF[c]][:].indirect(idx2[:, entries(first, count)]), h_tiles[c][:, cols], weights[:, cols], ALU.mult)
+            nc.vector.tensor_tensor(pages[PAGE_OF[c]][:].indirect(idx2[:, entries(first, count)]), h_piece(c, first, count), weights[:, cols], ALU.mult)
 
         z0_rows = sbuf("z0_rows", [P, M // P, 2, P, 2], BF16)
 
@@ -338,28 +347,34 @@ def tile_list_zeolite_ring_check_kernel(
         def spent(c, piece, width=PIECE):
             return h_tiles[c][:, PIECE * piece : PIECE * piece + width]
 
-        for c in range(2):
-            site = placed("site%d" % c, [P, M], F32, AT_V_W + 4 * c)
-            facing = placed("facing%d" % c, [P, M], F32, AT_V_W + 4 * c + 2)
-            nc.vector.tensor_copy(site[:], pages[PAGE_OF[c]][:].indirect(idx3[:]))
-            nc.vector.tensor_copy(facing[:], pages[PAGE_OF[c]][:].indirect(idx4[:]))
-            sum_and_turn(c, [site[:]], [facing[:]])
-        scatter(2)
-        scatter(3, 0, 2 * PIECE)
-        turns = []
-        for c in range(3, 7):
-            turns = turns + [(c + 1, 0), (c, 2), (c + 1, 1), (c, 3)]
-        before = (3, 0)
-        for c in (2, 3):
+        def read_plain(c, offsets, m0, dst):
+            nc.vector.tensor_copy(dst, pages[PAGE_OF[c]][:].indirect(offsets[:, entries(m0, dst.shape[1])]))
+            return dst
+
+        def scatter_piece(turn):
+            scatter(turn[0], PIECE * turn[1], PIECE)
+
+        turns = [(c, piece) for piece in range(4) for c in (2, 3)]
+        turns = turns + [(4, 0), (5, 0), (4, 1), (5, 1), (4, 2), (5, 2), (4, 3)]
+        turns = turns + [(6, 0), (5, 3), (6, 1), (7, 0), (6, 2), (7, 1), (6, 3), (7, 2)]
+        for pair, kib in ((0, AT_V_W), (1, AT_READS2)):
+            c = 2 * pair
+            site = placed("site%d" % c, [P, M], F32, kib)
+            facing = placed("facing%d" % c, [P, M], F32, kib + 2)
+            sum_and_turn(c, [read_plain(c, idx3, 0, site[:])], [read_plain(c, idx4, 0, facing[:])])
             reads = []
-            for i, (offsets, half) in enumerate(((idx3, 0), (idx4, 0), (idx3, 1), (idx4, 1))):
-                tile_number, piece = turns[4 * (c - 2) + i]
-                scatter(tile_number, PIECE * piece, PIECE)
-                dst = spent(before[0], before[1])
-                nc.vector.tensor_copy(dst, pages[PAGE_OF[c]][:].indirect(offsets[:, entries(HALF * half, HALF)]))
-                reads.append(dst)
-                before = (tile_number, piece)
-            sum_and_turn(c, reads[0::2], reads[1::2])
+            for i in range(8):
+                if i > 0:
+                    scatter_piece(turns[8 * pair + i - 1])
+                if i < 2:
+                    dst = placed("early%d%d" % (pair, i), [P, QUARTER], F32, kib + 4 + 0.5 * i)[:]
+                else:
+                    dst = spent(turns[8 * pair + i - 2][0], turns[8 * pair + i - 2][1], QUARTER)
+                reads.append(read_plain(c + 1, (idx3, idx4)[i % 2], QUARTER * (i // 2), dst))
+            sum_and_turn(c + 1, reads[0::2], reads[1::2])
+            if pair == 0:
+                scatter_piece(turns[7])
+                nc.gpsimd.memset(pages[3][:], 0.0)
         z0_grouped = [placed("z0_grouped%d" % half, [P, HALF, 4], BF16, AT_Z0_GROUPED + 2 * half) for half in range(2)]
         pairs = z0_rows[:].rearrange("m j u p e -> m j u (p e)").bitcast(F32)
         for j in range(M // P):
@@ -370,6 +385,9 @@ def tile_list_zeolite_ring_check_kernel(
                 z0_grouped[j // 2][:, P * (j % 2) : P * (j % 2 + 1), :].bitcast(F32),
                 turned[:, 0 : 2 * P].rearrange("p (u m) -> p m u", u=2),
             )
+
+        for b in (1, 0):
+            round_w(w_right[:, b], b, 1)
 
         minus_target = dict()
         for side in range(2):
@@ -415,24 +433,26 @@ def tile_list_zeolite_ring_check_kernel(
         low_grouped = placed("low_grouped", [P, HALF, 4], BF16, AT_LOW_GROUPED)
         z45_low = placed("z45_low", [P, 2, HALF], F32, AT_Z45_LOW)
         z67_low = [placed("z67_low%d" % q, [P, 2, QUARTER], F32, AT_Z67_LOW + q) for q in range(2)]
-        for c in (4, 5):
-            sites = []
-            for i in range(4):
-                tile_number, piece = turns[4 * (c - 2) + i]
-                scatter(tile_number, PIECE * piece, PIECE)
-                if i < 2:
-                    sites.append(read_site_into(c, QUARTER * i, QUARTER, spent(before[0], before[1], QUARTER)))
-                else:
-                    q = i - 2
-                    read_facing(c, QUARTER * q, QUARTER, sites[q], z45_low[:, c - 4, QUARTER * q : QUARTER * (q + 1)])
-                before = (tile_number, piece)
+        site4 = []
+        for q in range(2):
+            scatter_piece(turns[15 + q])
+            site4.append(read_site_into(4, QUARTER * q, QUARTER, spent(turns[14 + q][0], turns[14 + q][1], QUARTER)))
+        for q in range(2):
+            scatter_piece(turns[17 + q])
+            read_facing(4, QUARTER * q, QUARTER, site4[q], z45_low[:, 0, QUARTER * q : QUARTER * (q + 1)])
+        scatter_piece(turns[19])
+        site5 = read_site(5, 0, HALF, AT_H7_FIRST, "site5")
+        for q in range(2):
+            scatter_piece(turns[20 + q])
+            cols = slice(QUARTER * q, QUARTER * (q + 1))
+            read_facing(5, QUARTER * q, QUARTER, site5[:, cols], z45_low[:, 1, cols])
         weave(low_grouped[:, :, 0:2], z45_low[:])
         scatter(7, 2 * PIECE, PIECE)
         site6 = read_site_into(6, 0, HALF, spent(6, 3))
-        w0 = [quantise("w0_left", w_rounded[0, 0][:], AT_H5)]
+        w0 = [quantise("w0_left", w_rounded[0, 0][:], AT_H7_FIRST)]
         for q in range(2):
             read_facing(6, QUARTER * q, QUARTER, site6[:, QUARTER * q : QUARTER * (q + 1)], z67_low[q][:, 0, :])
-        w1_left = quantise("w1_left", w_rounded[1, 0][:], AT_H6)
+        w1_left = quantise("w1_left", w_rounded[1, 0][:], AT_H7_FIRST + 0.5)
         for number in (2, 3):
             unread = bank("unread", number)
             multiply(unread[:], columns(w0[0], 0, P), columns(w1_left, 0, BANK), True, True)

@@ -21,12 +21,13 @@ BANK = 512
 PASS = 512
 HALF = M // 2
 ROW_TILES = H // P
-PAGE_OF = (0, 1, 0, 2, 1, 3, 0, 2)
+PAGE_OF = (0, 1, 2, 0, 1, 3, 2, 0)
 QUARTER = M // 4
 PER_COLUMN = 16
 ALIGN = 64
 EARLY = 2 * P
 FIRST = 256
+BLOCKS_FIRST = 4
 PIECE = 256
 
 Z_BANK = 6
@@ -34,7 +35,6 @@ TURN_BANK = 6
 
 AT_WGS = 0
 AT_PICKED = 3.5
-AT_W4_LOW = 4
 AT_IDEAL_LOW = 9
 AT_TAB_W1 = 16
 AT_W_RIGHT = 54
@@ -54,8 +54,11 @@ AT_H4 = AT_W_LEFT
 AT_H5 = AT_W_LEFT + 4
 AT_READS2 = AT_W_LEFT + 8
 AT_H6 = 128
-AT_V_W = 132
-AT_H7_FIRST = 140
+AT_PICKED_REST = 134
+AT_W4_HIGH = AT_PICKED_REST - 1.75
+AT_W4_MIDDLE = AT_PICKED_REST + 0.5
+AT_READS0 = AT_W4_MIDDLE + 1
+AT_H7_FIRST = 141
 AT_Z45_LOW = 12
 AT_Z67_LOW = 14
 AT_SITE7_LOW = 16
@@ -137,7 +140,7 @@ def tile_list_zeolite_ring_check_kernel(
         nc.gpsimd.memset(w4_s_rest[:].bitcast(I32), 0)
         nc.gpsimd.memset(pages[1][:], 0.0)
 
-        picked_s = placed("picked_s", [P, S - FIRST], U8, AT_W4_LOW)
+        picked_s = placed("picked_s", [P, S - FIRST], U8, AT_PICKED_REST)
         picked_first = placed("picked_first", [P, FIRST], U8, AT_PICKED)
         for picked, plane, first in ((picked_first, v_s_first, 0), (picked_s, v_s_rest, FIRST)):
             count = picked.shape[1]
@@ -151,7 +154,7 @@ def tile_list_zeolite_ring_check_kernel(
                 )
         for r in range(4):
             nc.sync.dma_start(w4_s_rest[r:128:32, :, :].bitcast(I32), w4_scale_rows[r][:, :, EARLY:H].bitcast(I32))
-        v_w = [placed("v_w%d" % a, [P, S], U32, AT_V_W + 4 * a) for a in range(2)]
+        v_w = [sbuf("v_w%d" % a, [P, S], U32) for a in range(2)]
         nc.vector.tensor_copy(v_w[0][:], tab_w[0][:].bitcast(U32).indirect(idx[:]))
         for first, count in ((0, FIRST), (FIRST, S - FIRST)):
             nc.vector.tensor_copy(
@@ -160,13 +163,16 @@ def tile_list_zeolite_ring_check_kernel(
 
         wgs_sb = placed("wgs_sb", [P, S], F32, AT_WGS)
         nc.sync.dma_start(wgs_sb[:], wgs)
-        w4_rest = placed("w4_rest", [P, 2, 2 * (H - EARLY)], U8, AT_W4_LOW)
-        nc.sync.dma_start(w4_rest[:].bitcast(I32), w4_words_p[:, :, 2 * EARLY : 2 * H].bitcast(I32))
+        w4_room = placed("w4_middle", [P, 6 * 1024], U8, AT_W4_MIDDLE)
+        w4_middle = w4_room[:, 0 : 4 * EARLY].rearrange("p (a n) -> p a n", a=2)
+        nc.sync.dma_start(w4_middle.bitcast(I32), w4_words_p[:, :, 2 * EARLY : 2 * PASS].bitcast(I32))
+        w4_high = placed("w4_high", [P, 2, 2 * PASS], U8, AT_W4_HIGH)
+        nc.sync.dma_start(w4_high[:].bitcast(I32), w4_words_p[:, :, 2 * PASS : 2 * H].bitcast(I32))
         ideal_low = placed("ideal_low", [P, 4, M], F32, AT_IDEAL_LOW)
         nc.sync.dma_start(ideal_low[:], ideal[0:PASS, :].rearrange("(c p) m -> p c m", p=P))
 
         def stationary(c, a):
-            words, scales, first = (w4_first, w4_s_first, P * c) if P * c < EARLY else (w4_rest, w4_s_rest, P * c - EARLY)
+            words, scales, first = (w4_first, w4_s_first, P * c) if P * c < EARLY else (w4_middle, w4_s_rest, P * c - EARLY)
             return words[:, a, 2 * first : 2 * (first + P)], scales[:, a, first : first + P]
 
         def first_product(c, groups):
@@ -211,9 +217,11 @@ def tile_list_zeolite_ring_check_kernel(
             first_product(c, [(number, h_tiles[c][:, 0:BANK], [(0, FIRST), (FIRST, BANK - FIRST)])])
             first_product(c, [(number + 1, h_tiles[c][:, BANK:], [(BANK, BANK)])])
 
-        natural_tile(2, 2)
+        natural_tile(3, 2)
         h_turned = placed("h_turned", [P, S // P, 4, P], F32, AT_TARGET)
         for block in range(S // P):
+            if block == BLOCKS_FIRST:
+                natural_tile(2, 0)
             j_cols = slice(P * block, P * (block + 1))
             h_acc = bank("h_acc", block % 2)
             for a in range(2):
@@ -221,7 +229,7 @@ def tile_list_zeolite_ring_check_kernel(
                     out=h_acc[:],
                     lhsT=v_w[a][:, j_cols].bitcast(FP8X4),
                     lhsT_scale=v_scales(a, P * block, P),
-                    rhs=w4_rest[:, a, 2 * (PASS - EARLY) : 2 * (H - EARLY)].bitcast(FP4X4),
+                    rhs=w4_high[:, a, :].bitcast(FP4X4),
                     rhs_scale=w4_s_rest[:, a, PASS - EARLY : H - EARLY],
                     start=(a == 0),
                     stop=(a == 1),
@@ -253,7 +261,6 @@ def tile_list_zeolite_ring_check_kernel(
         def copy_back(c, part, h_back, first=0, width=BANK):
             nc.scalar.copy(h_piece(c, BANK * part + first, width), h_back[:, first : first + width])
 
-        natural_tile(3, 0)
         for part in range(2):
             copy_back(6, part, turn_back(6, part, 2 + part))
         first_half = turn_back(7, 0, 2)
@@ -357,7 +364,7 @@ def tile_list_zeolite_ring_check_kernel(
         turns = [(c, piece) for piece in range(4) for c in (2, 3)]
         turns = turns + [(4, 0), (5, 0), (4, 1), (5, 1), (4, 2), (5, 2), (4, 3)]
         turns = turns + [(6, 0), (5, 3), (6, 1), (7, 0), (6, 2), (7, 1), (6, 3), (7, 2)]
-        for pair, kib in ((0, AT_V_W), (1, AT_READS2)):
+        for pair, kib in ((0, AT_READS0), (1, AT_READS2)):
             c = 2 * pair
             site = placed("site%d" % c, [P, M], F32, kib)
             facing = placed("facing%d" % c, [P, M], F32, kib + 2)
@@ -452,7 +459,7 @@ def tile_list_zeolite_ring_check_kernel(
         w0 = [quantise("w0_left", w_rounded[0, 0][:], AT_H7_FIRST)]
         for q in range(2):
             read_facing(6, QUARTER * q, QUARTER, site6[:, QUARTER * q : QUARTER * (q + 1)], z67_low[q][:, 0, :])
-        w1_left = quantise("w1_left", w_rounded[1, 0][:], AT_H7_FIRST + 0.5)
+        w1_left = quantise("w1_left", w_rounded[1, 0][:], AT_H6)
         for number in (2, 3):
             unread = bank("unread", number)
             multiply(unread[:], columns(w0[0], 0, P), columns(w1_left, 0, BANK), True, True)

@@ -59,6 +59,7 @@ AT_W4_HIGH = AT_PICKED_REST - 1.75
 AT_W4_MIDDLE = AT_PICKED_REST + 0.5
 AT_READS0 = AT_W4_MIDDLE + 1
 AT_H7_FIRST = 141
+AT_Z0_ROWS = 142
 AT_Z45_LOW = 12
 AT_Z67_LOW = 14
 AT_SITE7_LOW = 16
@@ -208,9 +209,12 @@ def tile_list_zeolite_ring_check_kernel(
         for c, kib in ((4, AT_H4), (5, AT_H5), (6, AT_H6), (7, AT_H7)):
             h_tiles[c] = placed("h%d" % c, [P, S], F32, kib)
 
+        h7_last = placed("h7_last", [P, PIECE], F32, AT_Z0_ROWS)
         h7_first = placed("h7_first", [P, PIECE], F32, AT_H7_FIRST)
 
         def h_piece(c, first, count):
+            if (c, first) == (7, S - PIECE):
+                return h7_last[:]
             return h7_first[:] if (c, first) == (7, 0) else h_tiles[c][:, first : first + count]
 
         def natural_tile(c, number):
@@ -248,6 +252,9 @@ def tile_list_zeolite_ring_check_kernel(
                 raw.rearrange("p t (c i) -> p c t i", i=4),
             )
 
+        wgs_dealt = placed("wgs_dealt", [P, 4, S], F32, AT_WGS_DEALT)
+        for q in (0, 2, 1, 3):
+            nc.sync.dma_start(wgs_dealt[32 * q : 32 * (q + 1)], wgs.rearrange("(p t) j -> p t j", t=4))
         w_left = placed("w_left", [P, 2, 4, BANK], F32, AT_W_LEFT)
         for b in range(2):
             load_w(w_left[:, b], b, 0)
@@ -266,7 +273,8 @@ def tile_list_zeolite_ring_check_kernel(
         first_half = turn_back(7, 0, 2)
         for first in (0, PIECE):
             copy_back(7, 0, first_half, first, PIECE)
-        copy_back(7, 1, turn_back(7, 1, 3))
+        h7_back = turn_back(7, 1, 0)
+        copy_back(7, 1, h7_back, 0, PIECE)
         for b in range(2):
             round_w(w_left[:, b], b, 0)
         first_halves = [turn_back(c, 0, c) for c in (4, 5)]
@@ -288,25 +296,17 @@ def tile_list_zeolite_ring_check_kernel(
         for c in range(4):
             nc.scalar.activation(minus_ideal[:, c, :], ideal_low[:, c, :], ACT.Copy, scale=-1.0)
 
-        wgs_dealt = placed("wgs_dealt", [P, 4, S], F32, AT_WGS_DEALT)
         ideal_up = placed("ideal_up", [P, 4, M], F32, AT_IDEAL_UP)
-        for u in range(2):
-            for q in (0, 2, 1, 3):
-                nc.sync.dma_start(
-                    wgs_dealt[32 * q : 32 * (q + 1), 2 * u : 2 * u + 2, :],
-                    wgs.rearrange("(p t) j -> p t j", t=4)[:, 2 * u : 2 * u + 2, :],
-                )
-            if u == 0:
-                nc.sync.dma_start(ideal_up[:], ideal[PASS:H, :].rearrange("(p t) m -> p t m", t=4))
+        nc.sync.dma_start(ideal_up[:], ideal[PASS:H, :].rearrange("(p t) m -> p t m", t=4))
         w_right = placed("w_right", [P, 2, 4, BANK], F32, AT_W_RIGHT)
         for b in (1, 0):
             load_w(w_right[:, b], b, 1)
         target_sb = placed("target_sb", [P, ROW_TILES, M], F32, AT_TARGET)
         nc.sync.dma_start(target_sb[:], target.rearrange("(c p) m -> p c m", p=P))
 
-        def quantise(name, grouped, kib=None):
+        def quantise(name, grouped, kib=None, codes_kib=None):
             width = grouped.shape[1]
-            codes = sbuf(name + "_codes", [P, width], U32)
+            codes = sbuf(name + "_codes", [P, width], U32) if codes_kib is None else placed(name + "_codes", [P, width], U32, codes_kib)
             scales = sbuf(name + "_scales", [P, width], U8) if kib is None else placed(name + "_scales", [P, width], U8, kib)
             nc.vector.quantize_mx(out=codes[:].bitcast(FP8X4), scales=scales[:], in_=grouped.rearrange("p n t -> p (n t)"))
             return codes, scales
@@ -330,7 +330,7 @@ def tile_list_zeolite_ring_check_kernel(
             cols = slice(first, first + count)
             nc.vector.tensor_tensor(pages[PAGE_OF[c]][:].indirect(idx2[:, entries(first, count)]), h_piece(c, first, count), weights[:, cols], ALU.mult)
 
-        z0_rows = sbuf("z0_rows", [P, M // P, 2, P, 2], BF16)
+        z0_rows = [placed("z0_rows%d" % half, [P, 2, 2, P, 2], BF16, AT_Z0_ROWS + 2 * half) for half in range(2)]
 
         def sum_and_turn(c, sites, facings):
             z_acc = bank("z_acc", Z_BANK + c % 2)
@@ -346,10 +346,11 @@ def tile_list_zeolite_ring_check_kernel(
                         stop=(number == 2 and j == 3),
                         is_transpose=True,
                     )
-            nc.scalar.copy(
-                z0_rows[:, :, :, 32 * c : 32 * (c + 1), :],
-                z_acc[:].rearrange("m (j p u e) -> m j u p e", j=4, u=2, e=2),
-            )
+            for half in range(2):
+                nc.scalar.copy(
+                    z0_rows[half][:, :, :, 32 * c : 32 * (c + 1), :],
+                    z_acc[:, HALF * half : HALF * (half + 1)].rearrange("m (j p u e) -> m j u p e", j=2, u=2, e=2),
+                )
 
         def spent(c, piece, width=PIECE):
             return h_tiles[c][:, PIECE * piece : PIECE * piece + width]
@@ -383,11 +384,13 @@ def tile_list_zeolite_ring_check_kernel(
                 scatter_piece(turns[7])
                 nc.gpsimd.memset(pages[3][:], 0.0)
         z0_grouped = [placed("z0_grouped%d" % half, [P, HALF, 4], BF16, AT_Z0_GROUPED + 2 * half) for half in range(2)]
-        pairs = z0_rows[:].rearrange("m j u p e -> m j u (p e)").bitcast(F32)
         for j in range(M // P):
-            turned = bank("turned", TURN_BANK + j % 2)
+            if j == 2:
+                copy_back(7, 1, h7_back, PIECE, PIECE)
+            pairs = z0_rows[j // 2][:].rearrange("m j u p e -> m j u (p e)").bitcast(F32)
+            turned = bank("turned", TURN_BANK + (j == 1))
             for u in range(2):
-                nc.tensor.transpose(turned[:, P * u : P * (u + 1)], pairs[:, j, u, :], ident[:])
+                nc.tensor.transpose(turned[:, P * u : P * (u + 1)], pairs[:, j % 2, u, :], ident[:])
             nc.scalar.copy(
                 z0_grouped[j // 2][:, P * (j % 2) : P * (j % 2 + 1), :].bitcast(F32),
                 turned[:, 0 : 2 * P].rearrange("p (u m) -> p m u", u=2),
@@ -459,18 +462,19 @@ def tile_list_zeolite_ring_check_kernel(
         w0 = [quantise("w0_left", w_rounded[0, 0][:], AT_H7_FIRST)]
         for q in range(2):
             read_facing(6, QUARTER * q, QUARTER, site6[:, QUARTER * q : QUARTER * (q + 1)], z67_low[q][:, 0, :])
-        w1_left = quantise("w1_left", w_rounded[1, 0][:], AT_H6)
-        for number in (2, 3):
-            unread = bank("unread", number)
-            multiply(unread[:], columns(w0[0], 0, P), columns(w1_left, 0, BANK), True, True)
-        scatter(7, S - FIRST, FIRST)
-        z0_low = quantise("z0_low", z0_grouped[0][:], AT_W_ROUNDED + 4)
+        z0_low = quantise("z0_low", z0_grouped[0][:], AT_H7_FIRST + 0.5)
         yt_banks = dict()
         for side in range(2):
-            for q in range(2):
-                yt_banks[q, side] = bank("yt_acc", q + 2 * side)
+            unread = bank("unread", 2 + side)
+            if side == 0:
+                for q in range(2):
+                    yt_banks[q, 0] = bank("yt_acc", q)
+                    multiply(yt_banks[q, 0][:], columns(z0_low, P * q, P), columns(w0[0], 0, BANK), True, False)
+                scatter(7, S - FIRST, FIRST)
+                w1_left = quantise("w1_left", w_rounded[1, 0][:], None, AT_Z0_ROWS + 2)
+            multiply(unread[:], columns(w0[0], 0, P), columns(w1_left, 0, BANK), True, True)
         for q in range(2):
-            multiply(yt_banks[q, 0][:], columns(z0_low, P * q, P), columns(w0[0], 0, BANK), True, False)
+            yt_banks[q, 1] = bank("yt_acc", q + 2)
         site7 = [read_site(7, QUARTER * q, QUARTER, AT_SITE7_LOW + 0.5 * q, "site7_%d" % q) for q in range(2)]
         for q in range(2):
             read_facing(7, QUARTER * q, QUARTER, site7[q], z67_low[q][:, 1, :])

@@ -464,15 +464,11 @@ def tile_list_zeolite_ring_check_kernel(
             read_facing(6, QUARTER * q, QUARTER, site6[:, QUARTER * q : QUARTER * (q + 1)], z67_low[q][:, 0, :])
         z0_low = quantise("z0_low", z0_grouped[0][:], AT_H7_FIRST + 0.5)
         yt_banks = dict()
-        for side in range(2):
-            unread = bank("unread", 2 + side)
-            if side == 0:
-                for q in range(2):
-                    yt_banks[q, 0] = bank("yt_acc", q)
-                    multiply(yt_banks[q, 0][:], columns(z0_low, P * q, P), columns(w0[0], 0, BANK), True, False)
-                scatter(7, S - FIRST, FIRST)
-                w1_left = quantise("w1_left", w_rounded[1, 0][:], None, AT_Z0_ROWS + 2)
-            multiply(unread[:], columns(w0[0], 0, P), columns(w1_left, 0, BANK), True, True)
+        for q in range(2):
+            yt_banks[q, 0] = bank("yt_acc", q)
+            multiply(yt_banks[q, 0][:], columns(z0_low, P * q, P), columns(w0[0], 0, BANK), True, False)
+        scatter(7, S - FIRST, FIRST)
+        w1_left = quantise("w1_left", w_rounded[1, 0][:], None, AT_Z0_ROWS + 2)
         for q in range(2):
             yt_banks[q, 1] = bank("yt_acc", q + 2)
         site7 = [read_site(7, QUARTER * q, QUARTER, AT_SITE7_LOW + 0.5 * q, "site7_%d" % q) for q in range(2)]

from contextlib import ExitStack

import concourse.mybir as mybir

K, H, N, T, S, T2, M = 1024, 1024, 1024, 2048, 1024, 2048, 512
FLOPS = 2 * K * H * S + 2 * H * N * M

F32 = mybir.dt.float32
BF16 = mybir.dt.bfloat16
I32 = mybir.dt.int32
U32 = mybir.dt.uint32
U16 = mybir.dt.uint16
U8 = mybir.dt.uint8
FP8X4 = mybir.dt.float8_e4m3fn_x4
FP4X4 = mybir.dt.float4_e2m1fn_x4
ALU = mybir.AluOpType
ACT = mybir.ActivationFunctionType

P = 128
BANK = 512
PASS = 512
HALF = M // 2
ROW_TILES = H // P
PAGE_OF = (0, 1, 2, 0, 1, 3, 2, 0)
QUARTER = M // 4
PER_COLUMN = 16
ALIGN = 64
EARLY = 2 * P
FIRST = 256
BLOCKS_FIRST = 4
PIECE = 256

Z_BANK = 6
TURN_BANK = 6

AT_WGS = 0
AT_PICKED = 3.5
AT_IDEAL_LOW = 9
AT_TAB_W1 = 16
AT_W_RIGHT = 54
AT_TAB_S = 24
AT_TAB_W0 = 30
AT_W_LEFT = 38
AT_WGS_DEALT = 20
AT_IDEAL_UP = 70
AT_TARGET = 78
AT_W_ROUNDED = 94
AT_Z0_GROUPED = 110
AT_H7 = 114
AT_PAGE2 = 120
AT_PAGE3 = AT_WGS
AT_H1_REST = AT_PAGE2
AT_H4 = AT_W_LEFT
AT_H5 = AT_W_LEFT + 4
AT_READS2 = AT_W_LEFT + 8
AT_H6 = 128
AT_PICKED_REST = 134
AT_W4_HIGH = AT_PICKED_REST - 1.75
AT_W4_MIDDLE = AT_PICKED_REST + 0.5
AT_READS0 = AT_W4_MIDDLE + 1
AT_H7_FIRST = 141
AT_Z0_ROWS = 142
AT_Z45_LOW = 12
AT_Z67_LOW = 14
AT_SITE7_LOW = 16
AT_LOW_GROUPED = AT_W_RIGHT
AT_LAST_GROUPED = 19
AT_TARGET_TURNED = AT_W_RIGHT
AT_BOUNDED_LOW = 62
AT_RESULT_LOW = AT_W_LEFT
AT_BOUNDED_HIGH = 46
AT_RESULT_HIGH = 20
AT_Z_HIGH = 28


def tile_list_zeolite_ring_check_kernel(
    tc, tab_words, tab_scales, w4_words, w4_scales, w, wgs, ideal, target, offs, offs2, offs3, offs4, out
):
    nc = tc.nc
    with ExitStack() as ctx:
        lists = ctx.enter_context(tc.tile_pool(name="lists", bufs=1))
        sb = ctx.enter_context(tc.tile_pool(name="sb", bufs=1))
        staged = ctx.enter_context(tc.tile_pool(name="staged", bufs=1))
        psum = ctx.enter_context(tc.psum_pool(name="psum", bufs=1))

        def sbuf(name, shape, dtype, tag=None, bufs=1):
            return sb.tile(shape, dtype, name=name, tag=tag or name, bufs=bufs, align_bytes=ALIGN)

        def placed(name, shape, dtype, kib, bufs=1):
            return staged.tile(shape, dtype, name=name, tag=name, bufs=bufs, align_bytes=ALIGN, offset=int(1024 * kib))

        def bank(name, number):
            return psum.tile([P, BANK], F32, name=name, tag="bank%d" % number)

        def entries(first, count):
            return slice(first // PER_COLUMN, (first + count) // PER_COLUMN)

        idx = lists.tile([P, S // PER_COLUMN], U16, name="idx")
        idx2 = lists.tile([P, S // PER_COLUMN], U16, name="idx2")
        idx3 = lists.tile([P, M // PER_COLUMN], U16, name="idx3")
        idx4 = lists.tile([P, M // PER_COLUMN], U16, name="idx4")
        tab_s = placed("tab_s", [P, T], U8, AT_TAB_S)
        tab_w = [placed("tab_w0", [P, T], I32, AT_TAB_W0), placed("tab_w1", [P, T], I32, AT_TAB_W1)]
        w4_words_p = w4_words.rearrange("a p n -> p a n")
        w4_first = sbuf("w4_first", [P, 2, 2 * EARLY], U8)
        wgs_first = placed("wgs_first", [P, FIRST], F32, AT_TAB_S)
        nc.sync.dma_start(idx[:], offs)
        nc.scalar.dma_start(tab_s[96:128, :].bitcast(I32), tab_scales.rearrange("a q n -> q a n").bitcast(I32))
        nc.sync.dma_start(idx2[:], offs2)
        nc.sync.dma_start(idx3[:], offs3)
        nc.scalar.dma_start(tab_w[0][:], tab_words[0].rearrange("p n t -> p (n t)").bitcast(I32))
        nc.scalar.dma_start(tab_w[1][:], tab_words[1].rearrange("p n t -> p (n t)").bitcast(I32))
        nc.scalar.dma_start(w4_first[:].bitcast(I32), w4_words_p[:, :, 0 : 2 * EARLY].bitcast(I32))
        nc.sync.dma_start(idx4[:], offs4)

        offset = sbuf("offset", [P, P], F32)
        nc.gpsimd.iota(offset[:], [[1, P]], base=0, channel_multiplier=-1, allow_small_or_imprecise_dtypes=True)
        distance = sbuf("distance", [P, P], F32)
        nc.scalar.activation(distance[:], offset[:], ACT.Abs)
        ident = sbuf("ident", [P, P], F32)
        nc.scalar.activation(ident[:], distance[:], ACT.Relu, scale=-1.0, bias=1.0)
        w4_scale_rows = w4_scales.rearrange("a (g r) n -> r g a n", r=4)
        w4_s_first = sbuf("w4_s_first", [P, 2, EARLY], U8)
        v_s = sbuf("v_s", [P, 2 * S], U8)
        v_s_first = v_s[:, 0 : 2 * FIRST].rearrange("p (a j) -> p a j", a=2)
        v_s_rest = v_s[:, 2 * FIRST : 2 * S].rearrange("p (a j) -> p a j", a=2)

        def v_scales(a, j0, width):
            plane, first = (v_s_first, j0) if j0 < FIRST else (v_s_rest, j0 - FIRST)
            return plane[:, a, first : first + width]

        nc.gpsimd.memset(w4_s_first[:].bitcast(I32), 0)
        nc.vector.memset(tab_s[0:96, :].bitcast(I32), 0)
        nc.vector.memset(v_s[:].bitcast(I32), 0)
        for r in range(4):
            nc.gpsimd.dma_start(w4_s_first[r:128:32, :, :].bitcast(I32), w4_scale_rows[r][:, :, 0:EARLY].bitcast(I32))
        pages = [sbuf("page0", [P, T2], F32), sbuf("page1", [P, T2], F32)]
        pages = pages + [placed("page2", [P, T2], F32, AT_PAGE2), placed("page3", [P, T2], F32, AT_PAGE3)]
        nc.vector.memset(pages[0][:], 0.0)
        w4_s_rest = placed("w4_s_rest", [P, 2, H - EARLY], U8, AT_W_ROUNDED + 3.25)
        nc.gpsimd.memset(w4_s_rest[:].bitcast(I32), 0)
        nc.gpsimd.memset(pages[1][:], 0.0)

        picked_s = placed("picked_s", [P, S - FIRST], U8, AT_PICKED_REST)
        picked_first = placed("picked_first", [P, FIRST], U8, AT_PICKED)
        for picked, plane, first in ((picked_first, v_s_first, 0), (picked_s, v_s_rest, FIRST)):
            count = picked.shape[1]
            nc.vector.tensor_copy(picked[:], tab_s[:].indirect(idx[:, entries(first, count)]))
            if first > 0:
                nc.scalar.dma_start(wgs_first[:], wgs[:, 0:FIRST])
            for g in (0, 2, 1, 3):
                nc.sync.dma_start(
                    plane[32 * g : 32 * g + 4, :, :].bitcast(I32),
                    picked[96 + 8 * g : 96 + 8 * g + 8, :].bitcast(I32),
                )
        for r in range(4):
            nc.sync.dma_start(w4_s_rest[r:128:32, :, :].bitcast(I32), w4_scale_rows[r][:, :, EARLY:H].bitcast(I32))
        v_w = [sbuf("v_w%d" % a, [P, S], U32) for a in range(2)]
        nc.vector.tensor_copy(v_w[0][:], tab_w[0][:].bitcast(U32).indirect(idx[:]))
        for first, count in ((0, FIRST), (FIRST, S - FIRST)):
            nc.vector.tensor_copy(
                v_w[1][:, first : first + count], tab_w[1][:].bitcast(U32).indirect(idx[:, entries(first, count)])
            )

        wgs_sb = placed("wgs_sb", [P, S], F32, AT_WGS)
        nc.sync.dma_start(wgs_sb[:], wgs)
        w4_room = placed("w4_middle", [P, 6 * 1024], U8, AT_W4_MIDDLE)
        w4_middle = w4_room[:, 0 : 4 * EARLY].rearrange("p (a n) -> p a n", a=2)
        nc.sync.dma_start(w4_middle.bitcast(I32), w4_words_p[:, :, 2 * EARLY : 2 * PASS].bitcast(I32))
        w4_high = placed("w4_high", [P, 2, 2 * PASS], U8, AT_W4_HIGH)
        nc.sync.dma_start(w4_high[:].bitcast(I32), w4_words_p[:, :, 2 * PASS : 2 * H].bitcast(I32))
        ideal_low = placed("ideal_low", [P, 4, M], F32, AT_IDEAL_LOW)
        nc.sync.dma_start(ideal_low[:], ideal[0:PASS, :].rearrange("(c p) m -> p c m", p=P))

        def stationary(c, a):
            words, scales, first = (w4_first, w4_s_first, P * c) if P * c < EARLY else (w4_middle, w4_s_rest, P * c - EARLY)
            return words[:, a, 2 * first : 2 * (first + P)], scales[:, a, first : first + P]

        def first_product(c, groups):
            accs = [bank("h_acc", number) for number, dst, pieces in groups]
            for a in range(2):
                words, scales = stationary(c, a)
                for h_acc, (number, dst, pieces) in zip(accs, groups):
                    for i, (j0, width) in enumerate(pieces):
                        at = j0 - pieces[0][0]
                        nc.tensor.matmul_mx(
                            out=h_acc[:, at : at + width],
                            lhsT=words.bitcast(FP4X4),
                            lhsT_scale=scales,
                            rhs=v_w[a][:, j0 : j0 + width].bitcast(FP8X4),
                            rhs_scale=v_scales(a, j0, width),
                            start=(a == 0 and i == 0),
                            stop=(a == 1 and i == len(pieces) - 1),
                        )
            for h_acc, (number, dst, pieces) in zip(accs, groups):
                nc.scalar.copy(dst, h_acc[:, 0 : sum(width for j0, width in pieces)])

        h0_first = placed("h0_first", [P, FIRST], F32, AT_WGS_DEALT + 15)
        h_first = [h0_first, placed("h1_first", [P, FIRST], F32, AT_W_LEFT + 7.5)]
        h_rest = [placed("h0_rest", [P, S - FIRST], F32, AT_IDEAL_UP - 1.5), placed("h1_rest", [P, S - FIRST], F32, AT_H1_REST)]
        for c in range(2):
            first_product(c, [(c, h_first[c][:], [(0, FIRST)])])
        for c in range(2):
            first_product(c, [(2 - 2 * c, h_rest[c][:, 0:BANK], [(FIRST, BANK)])])
            first_product(c, [(3 - 2 * c, h_rest[c][:, BANK:], [(FIRST + BANK, S - FIRST - BANK)])])
        h_tiles = dict()
        for c in (2, 3):
            h_tiles[c] = sbuf("h%d" % c, [P, S], F32)
        for c, kib in ((4, AT_H4), (5, AT_H5), (6, AT_H6), (7, AT_H7)):
            h_tiles[c] = placed("h%d" % c, [P, S], F32, kib)

        h7_last = placed("h7_last", [P, PIECE], F32, AT_Z0_ROWS)
        h7_first = placed("h7_first", [P, PIECE], F32, AT_H7_FIRST)

        def h_piece(c, first, count):
            if (c, first) == (7, S - PIECE):
                return h7_last[:]
            return h7_first[:] if (c, first) == (7, 0) else h_tiles[c][:, first : first + count]

        def natural_tile(c, number):
            first_product(c, [(number, h_tiles[c][:, 0:BANK], [(0, FIRST), (FIRST, BANK - FIRST)])])
            first_product(c, [(number + 1, h_tiles[c][:, BANK:], [(BANK, BANK)])])

        natural_tile(3, 2)
        h_turned = placed("h_turned", [P, S // P, 4, P], F32, AT_TARGET)
        for block in range(S // P):
            if block == BLOCKS_FIRST:
                natural_tile(2, 0)
            j_cols = slice(P * block, P * (block + 1))
            h_acc = bank("h_acc", block % 2)
            for a in range(2):
                nc.tensor.matmul_mx(
                    out=h_acc[:],
                    lhsT=v_w[a][:, j_cols].bitcast(FP8X4),
                    lhsT_scale=v_scales(a, P * block, P),
                    rhs=w4_high[:, a, :].bitcast(FP4X4),
                    rhs_scale=w4_s_rest[:, a, PASS - EARLY : H - EARLY],
                    start=(a == 0),
                    stop=(a == 1),
                )
            nc.scalar.copy(h_turned[:, block], h_acc[:].rearrange("j (p t) -> j t p", t=4))
        w_rounded = dict()

        def load_w(dst, b, side):
            cols = slice(BANK * side, BANK * (side + 1))
            nc.sync.dma_start(dst, w[PASS * b : PASS * (b + 1), cols].rearrange("(p t) n -> p t n", t=4))

        def round_w(raw, b, side):
            w_rounded[b, side] = placed("w_rounded%d%d" % (b, side), [P, BANK, 4], BF16, AT_W_ROUNDED + 8 * side + 4 * b)
            nc.scalar.copy(
                w_rounded[b, side][:].rearrange("p (c i) t -> p c t i", i=4),
                raw.rearrange("p t (c i) -> p c t i", i=4),
            )

        wgs_dealt = placed("wgs_dealt", [P, 4, S], F32, AT_WGS_DEALT)
        for q in (0, 2, 1, 3):
            nc.sync.dma_start(wgs_dealt[32 * q : 32 * (q + 1)], wgs.rearrange("(p t) j -> p t j", t=4))
        w_left = placed("w_left", [P, 2, 4, BANK], F32, AT_W_LEFT)
        for b in range(2):
            load_w(w_left[:, b], b, 0)

        def turn_back(c, part, number):
            h_back = bank("h_back", number)
            for i in range(4):
                nc.tensor.transpose(h_back[:, P * i : P * (i + 1)], h_turned[:, 4 * part + i, c - 4, :], ident[:])
            return h_back

        def copy_back(c, part, h_back, first=0, width=BANK):
            nc.scalar.copy(h_piece(c, BANK * part + first, width), h_back[:, first : first + width])

        for part in range(2):
            copy_back(6, part, turn_back(6, part, 2 + part))
        first_half = turn_back(7, 0, 2)
        for first in (0, PIECE):
            copy_back(7, 0, first_half, first, PIECE)
        h7_back = turn_back(7, 1, 0)
        copy_back(7, 1, h7_back, 0, PIECE)
        for b in range(2):
            round_w(w_left[:, b], b, 0)
        first_halves = [turn_back(c, 0, c) for c in (4, 5)]
        for first in (0, PIECE):
            for c in (4, 5):
                copy_back(c, 0, first_halves[c - 4], first, PIECE)
        for c in (4, 5):
            copy_back(c, 1, turn_back(c, 1, c + 2))

        for c in range(2):
            nc.vector.tensor_tensor(pages[c][:].indirect(idx2[:, entries(0, FIRST)]), h_first[c][:], wgs_first[:], ALU.mult)
        for c in range(2):
            nc.vector.tensor_tensor(
                pages[c][:].indirect(idx2[:, entries(FIRST, S - FIRST)]), h_rest[c][:], wgs_sb[:, FIRST:S], ALU.mult
            )

        nc.gpsimd.memset(pages[2][:], 0.0)
        minus_ideal = sbuf("minus_ideal", [P, 4, M], F32)
        for c in range(4):
            nc.scalar.activation(minus_ideal[:, c, :], ideal_low[:, c, :], ACT.Copy, scale=-1.0)

        ideal_up = placed("ideal_up", [P, 4, M], F32, AT_IDEAL_UP)
        nc.sync.dma_start(ideal_up[:], ideal[PASS:H, :].rearrange("(p t) m -> p t m", t=4))
        w_right = placed("w_right", [P, 2, 4, BANK], F32, AT_W_RIGHT)
        for b in (1, 0):
            load_w(w_right[:, b], b, 1)
        target_sb = placed("target_sb", [P, ROW_TILES, M], F32, AT_TARGET)
        nc.sync.dma_start(target_sb[:], target.rearrange("(c p) m -> p c m", p=P))

        def quantise(name, grouped, kib=None, codes_kib=None):
            width = grouped.shape[1]
            codes = sbuf(name + "_codes", [P, width], U32) if codes_kib is None else placed(name + "_codes", [P, width], U32, codes_kib)
            scales = sbuf(name + "_scales", [P, width], U8) if kib is None else placed(name + "_scales", [P, width], U8, kib)
            nc.vector.quantize_mx(out=codes[:].bitcast(FP8X4), scales=scales[:], in_=grouped.rearrange("p n t -> p (n t)"))
            return codes, scales

        def multiply(acc, stationary_side, moving_side, start, stop):
            nc.tensor.matmul_mx(
                out=acc,
                lhsT=stationary_side[0].bitcast(FP8X4),
                lhsT_scale=stationary_side[1],
                rhs=moving_side[0].bitcast(FP8X4),
                rhs_scale=moving_side[1],
                start=start,
                stop=stop,
            )

        def columns(quantised, first, count):
            return quantised[0][:, first : first + count], quantised[1][:, first : first + count]

        def scatter(c, first=0, count=S):
            weights = wgs_sb[:] if c < 4 else wgs_dealt[:, c - 4, :]
            cols = slice(first, first + count)
            nc.vector.tensor_tensor(pages[PAGE_OF[c]][:].indirect(idx2[:, entries(first, count)]), h_piece(c, first, count), weights[:, cols], ALU.mult)

        z0_rows = [placed("z0_rows%d" % half, [P, 2, 2, P, 2], BF16, AT_Z0_ROWS + 2 * half) for half in range(2)]

        def sum_and_turn(c, sites, facings):
            z_acc = bank("z_acc", Z_BANK + c % 2)
            terms = ([minus_ideal[:, c, :]], sites, facings)
            for number, pieces in enumerate(terms):
                blocks = [piece[:, P * i : P * (i + 1)] for piece in pieces for i in range(piece.shape[1] // P)]
                for j in range(4):
                    nc.tensor.matmul(
                        z_acc[:, P * j : P * (j + 1)],
                        blocks[j],
                        ident[:],
                        start=(number == 0 and j == 0),
                        stop=(number == 2 and j == 3),
                        is_transpose=True,
                    )
            for half in range(2):
                nc.scalar.copy(
                    z0_rows[half][:, :, :, 32 * c : 32 * (c + 1), :],
                    z_acc[:, HALF * half : HALF * (half + 1)].rearrange("m (j p u e) -> m j u p e", j=2, u=2, e=2),
                )

        def spent(c, piece, width=PIECE):
            return h_tiles[c][:, PIECE * piece : PIECE * piece + width]

        def read_plain(c, offsets, m0, dst):
            nc.vector.tensor_copy(dst, pages[PAGE_OF[c]][:].indirect(offsets[:, entries(m0, dst.shape[1])]))
            return dst

        def scatter_piece(turn):
            scatter(turn[0], PIECE * turn[1], PIECE)

        turns = [(c, piece) for piece in range(4) for c in (2, 3)]
        turns = turns + [(4, 0), (5, 0), (4, 1), (5, 1), (4, 2), (5, 2), (4, 3)]
        turns = turns + [(6, 0), (5, 3), (6, 1), (7, 0), (6, 2), (7, 1), (6, 3), (7, 2)]
        for pair, kib in ((0, AT_READS0), (1, AT_READS2)):
            c = 2 * pair
            site = placed("site%d" % c, [P, M], F32, kib)
            facing = placed("facing%d" % c, [P, M], F32, kib + 2)
            sum_and_turn(c, [read_plain(c, idx3, 0, site[:])], [read_plain(c, idx4, 0, facing[:])])
            reads = []
            for i in range(8):
                if i > 0:
                    scatter_piece(turns[8 * pair + i - 1])
                if i < 2:
                    dst = placed("early%d%d" % (pair, i), [P, QUARTER], F32, kib + 4 + 0.5 * i)[:]
                else:
                    dst = spent(turns[8 * pair + i - 2][0], turns[8 * pair + i - 2][1], QUARTER)
                reads.append(read_plain(c + 1, (idx3, idx4)[i % 2], QUARTER * (i // 2), dst))
            sum_and_turn(c + 1, reads[0::2], reads[1::2])
            if pair == 0:
                scatter_piece(turns[7])
                nc.gpsimd.memset(pages[3][:], 0.0)
        z0_grouped = [placed("z0_grouped%d" % half, [P, HALF, 4], BF16, AT_Z0_GROUPED + 2 * half) for half in range(2)]
        for j in range(M // P):
            if j == 2:
                copy_back(7, 1, h7_back, PIECE, PIECE)
            pairs = z0_rows[j // 2][:].rearrange("m j u p e -> m j u (p e)").bitcast(F32)
            turned = bank("turned", TURN_BANK + (j == 1))
            for u in range(2):
                nc.tensor.transpose(turned[:, P * u : P * (u + 1)], pairs[:, j % 2, u, :], ident[:])
            nc.scalar.copy(
                z0_grouped[j // 2][:, P * (j % 2) : P * (j % 2 + 1), :].bitcast(F32),
                turned[:, 0 : 2 * P].rearrange("p (u m) -> p m u", u=2),
            )

        for b in (1, 0):
            round_w(w_right[:, b], b, 1)

        minus_target = dict()
        for side in range(2):
            for q in range(2):
                turned = bank("target_turned", q + 2 * side)
                for i in range(4):
                    nc.tensor.transpose(turned[:, P * i : P * (i + 1)], target_sb[:, 4 * side + i, P * q : P * (q + 1)], ident[:])
                minus_target[q, side] = placed("minus_target%d%d" % (q, side), [P, BANK], F32, AT_TARGET_TURNED + 2 * (q + 2 * side))
                nc.scalar.activation(minus_target[q, side][:], turned[:], ACT.Copy, scale=-1.0)
        out_banks = [bank("out_acc", 4 + j) for j in range(4)]

        def add_turned(j, q, tiles, opening):
            for i in range(2):
                n0 = P * (2 * (j % 2) + i)
                nc.tensor.matmul(
                    out_banks[j][:, HALF * i + P * q : HALF * i + P * (q + 1)],
                    tiles[q, j // 2][:, n0 : n0 + P],
                    ident[:],
                    start=(opening and i == 0 and q == 0),
                    stop=(not opening and i == 1 and q == 1),
                    is_transpose=True,
                )

        for j in range(4):
            for q in range(2):
                add_turned(j, q, minus_target, True)

        def read_site(c, m0, width, kib, name):
            return read_site_into(c, m0, width, placed(name, [P, width], F32, kib)[:])

        def read_site_into(c, m0, width, dst):
            nc.vector.tensor_tensor(
                dst, pages[PAGE_OF[c]][:].indirect(idx3[:, entries(m0, width)]), ideal_up[:, c - 4, m0 : m0 + width], ALU.subtract
            )
            return dst

        def read_facing(c, m0, width, site_part, dst):
            nc.vector.tensor_tensor(dst, pages[PAGE_OF[c]][:].indirect(idx4[:, entries(m0, width)]), site_part, ALU.add)

        def weave(grouped, z_tiles):
            nc.scalar.copy(grouped, z_tiles.rearrange("p e m -> p m e"))

        low_grouped = placed("low_grouped", [P, HALF, 4], BF16, AT_LOW_GROUPED)
        z45_low = placed("z45_low", [P, 2, HALF], F32, AT_Z45_LOW)
        z67_low = [placed("z67_low%d" % q, [P, 2, QUARTER], F32, AT_Z67_LOW + q) for q in range(2)]
        site4 = []
        for q in range(2):
            scatter_piece(turns[15 + q])
            site4.append(read_site_into(4, QUARTER * q, QUARTER, spent(turns[14 + q][0], turns[14 + q][1], QUARTER)))
        for q in range(2):
            scatter_piece(turns[17 + q])
            read_facing(4, QUARTER * q, QUARTER, site4[q], z45_low[:, 0, QUARTER * q : QUARTER * (q + 1)])
        scatter_piece(turns[19])
        site5 = read_site(5, 0, HALF, AT_H7_FIRST, "site5")
        for q in range(2):
            scatter_piece(turns[20 + q])
            cols = slice(QUARTER * q, QUARTER * (q + 1))
            read_facing(5, QUARTER * q, QUARTER, site5[:, cols], z45_low[:, 1, cols])
        weave(low_grouped[:, :, 0:2], z45_low[:])
        scatter(7, 2 * PIECE, PIECE)
        site6 = read_site_into(6, 0, HALF, spent(6, 3))
        w0 = [quantise("w0_left", w_rounded[0, 0][:], AT_H7_FIRST)]
        for q in range(2):
            read_facing(6, QUARTER * q, QUARTER, site6[:, QUARTER * q : QUARTER * (q + 1)], z67_low[q][:, 0, :])
        z0_low = quantise("z0_low", z0_grouped[0][:], AT_H7_FIRST + 0.5)
        yt_banks = dict()
        for q in range(2):
            yt_banks[q, 0] = bank("yt_acc", q)
            multiply(yt_banks[q, 0][:], columns(z0_low, P * q, P), columns(w0[0], 0, BANK), True, False)
        scatter(7, S - FIRST, FIRST)
        w1_left = quantise("w1_left", w_rounded[1, 0][:], None, AT_Z0_ROWS + 2)
        for q in range(2):
            yt_banks[q, 1] = bank("yt_acc", q + 2)
        site7 = [read_site(7, QUARTER * q, QUARTER, AT_SITE7_LOW + 0.5 * q, "site7_%d" % q) for q in range(2)]
        for q in range(2):
            read_facing(7, QUARTER * q, QUARTER, site7[q], z67_low[q][:, 1, :])
        for q in range(2):
            weave(low_grouped[:, QUARTER * q : QUARTER * (q + 1), 2:4], z67_low[q][:])
        w1_right = [quantise("w1_right0", w_rounded[1, 1][:, 0:HALF, :], AT_SITE7_LOW)]
        z1 = [quantise("z1_0", low_grouped[:, 0:QUARTER, :])]
        multiply(yt_banks[0, 0][:], columns(z1[0], 0, P), columns(w1_left, 0, BANK), False, True)
        w1_right.append(quantise("w1_right1", w_rounded[1, 1][:, HALF:BANK, :], AT_Z67_LOW))
        z1.append(quantise("z1_1", low_grouped[:, QUARTER:HALF, :]))
        multiply(yt_banks[1, 0][:], columns(z1[1], 0, P), columns(w1_left, 0, BANK), False, True)
        w0.append(quantise("w0_right", w_rounded[0, 1][:], AT_Z67_LOW + 1))
        for q in range(2):
            for part in range(2):
                acc = yt_banks[q, 1][:, HALF * part : HALF * (part + 1)]
                multiply(acc, columns(z1[q], 0, P), columns(w1_right[part], 0, HALF), part == 0, False)
            multiply(yt_banks[q, 1][:], columns(z0_low, P * q, P), columns(w0[1], 0, BANK), False, True)
        z0_third = quantise("z0_third", z0_grouped[1][:, 0:QUARTER, :], AT_Z67_LOW + 1.5)

        bounded_low = dict()
        for side in range(2):
            for q in range(2):
                bounded_low[q, side] = placed("bounded_low%d%d" % (q, side), [P, BANK], F32, AT_BOUNDED_LOW + 2 * (q + 2 * side))
                nc.scalar.activation(bounded_low[q, side][:], yt_banks[q, side][:], ACT.Tanh)
                for j in (2 * side, 2 * side + 1):
                    add_turned(j, q, bounded_low, False)
        out_rows = out.rearrange("(c p) m -> p c m", p=P)

        def finish_low(j):
            result = placed("result_low%d" % j, [P, 2, HALF], F32, AT_RESULT_LOW + 2 * j)
            nc.scalar.copy(result[:], out_banks[j][:].rearrange("p (i m) -> p i m", i=2))
            nc.sync.dma_start(out_rows[:, 2 * j : 2 * j + 2, 0:HALF], result[:])

        def w_block(b, block):
            if b == 0:
                return columns(w0[block // 4], P * (block % 4), P)
            if block < 4:
                return columns(w1_left, P * block, P)
            return columns(w1_right[(block - 4) // 2], P * (block % 2), P)

        blocks_in = {2: 4, 3: 2}
        y_banks = dict()

        def high_product(b, q, moving_side):
            count = blocks_in[q]
            for j in range(ROW_TILES // count):
                if b == 0:
                    y_banks[q, j] = bank("y_acc", 4 * (q - 2) + j)
                for i in range(count):
                    acc = y_banks[q, j][:, P * i : P * (i + 1)]
                    multiply(acc, w_block(b, count * j + i), moving_side, b == 0 and i == 0, b == 1 and i == count - 1)

        def high_sites(q):
            return [read_site(c, QUARTER * q, QUARTER, AT_LOW_GROUPED + 0.5 * (c - 4), "site_high%d" % c) for c in range(4, 8)]

        def bound_high(q, j, pieces):
            count = blocks_in[q]
            bounded = placed("bounded_high%d%d" % (q, j), [P, count, P], F32, AT_BOUNDED_HIGH + 4 * (q - 2) + 0.5 * count * j)
            for first, many in pieces:
                nc.scalar.activation(
                    bounded[:, first : first + many, :].rearrange("p i m -> p (i m)"),
                    y_banks[q, j][:, P * first : P * (first + many)],
                    ACT.Tanh,
                )
            return bounded

        def finish_high(q, j, bounded, pieces):
            count = blocks_in[q]
            result = placed("result_high%d%d" % (q, j), [P, count, P], F32, AT_RESULT_HIGH + 4 * (q - 2) + 0.5 * count * j)
            for first, many in pieces:
                place = (slice(None), slice(count * j + first, count * j + first + many), slice(QUARTER * q, QUARTER * (q + 1)))
                piece = result[:, first : first + many, :]
                nc.vector.tensor_tensor(piece, bounded[:, first : first + many, :], target_sb[place], ALU.subtract)
                nc.sync.dma_start(out_rows[place], piece)

        whole, halves = ((0, 4),), ((0, 2), (2, 2))
        sites = high_sites(2)
        z_third = placed("z_third", [P, 4, QUARTER], F32, AT_Z_HIGH)
        for c in range(4, 8):
            read_facing(c, QUARTER * 2, QUARTER, sites[c - 4], z_third[:, c - 4, :])
        finish_low(0)
        finish_low(1)
        third_grouped = placed("third_grouped", [P, QUARTER, 4], BF16, AT_BOUNDED_LOW + 4)
        weave(third_grouped[:], z_third[:])
        finish_low(2)
        finish_low(3)
        high_product(0, 2, columns(z0_third, 0, QUARTER))
        sites = high_sites(3)
        z1.append(quantise("z1_2", third_grouped[:], AT_LAST_GROUPED))
        high_product(1, 2, columns(z1[2], 0, QUARTER))
        z_last = [placed("z_last%d" % u, [P, 2, QUARTER], F32, AT_Z_HIGH + u) for u in range(2)]
        for c in range(4, 8):
            if c == 6:
                z0_last = quantise("z0_last", z0_grouped[1][:, QUARTER:HALF, :], AT_BOUNDED_LOW + 4)
                high_product(0, 3, columns(z0_last, 0, QUARTER))
            read_facing(c, QUARTER * 3, QUARTER, sites[c - 4], z_last[(c - 4) // 2][:, c % 2, :])
        last_grouped = placed("last_grouped", [P, QUARTER, 4], BF16, AT_LAST_GROUPED)
        bounded_left = bound_high(2, 0, whole)
        for u in range(2):
            weave(last_grouped[:, :, 2 * u : 2 * u + 2], z_last[u][:])
        bounded_right = bound_high(2, 1, halves)
        finish_high(2, 0, bounded_left, whole)
        z1.append(quantise("z1_3", last_grouped[:]))
        high_product(1, 3, columns(z1[3], 0, QUARTER))
        finish_high(2, 1, bounded_right, halves)
        for j in range(4):
            pieces = ((0, 2),) if j < 3 else ((0, 1), (1, 1))
            finish_high(3, j, bound_high(3, j, pieces), pieces)
